import numpy as np, ml_dtypes
CORES = [35,38,43,46]
N = 4
BF = ml_dtypes.bfloat16
V, M, W, TR, RO, CAP = 512, 256, 4096, 4, 3, 60
def spot(a, b, p, q):
    return ((a * (2 * b + 1) >> 4) + a + p * (2 * b + 613) + q * (2 * a + 37)) & (W - 1)
def look(X, a, b, p, q):
    return np.take_along_axis(X, spot(a, b, p, q).reshape(N, 8, 1, 16 * M), 3).reshape(N, 8, 16, 16, M)
def excess(R, z):
    return np.add.reduce(np.maximum(R - z[:, :, :, None, :], 0), axis=2)
def scan(X, G, B, d, z, t):
    ra = np.arange(N)[:, None, None, None]; ga = np.arange(8)[None, :, None, None]; z = z.astype(np.int32)
    n = np.add.reduce((G >= 0).astype(np.int64), axis=2)
    s = np.where((G >= 0) & ((G & 1) == (t & 1)), n[ra, ga, np.maximum(G, 0)], -1)
    e = np.take_along_axis(G, np.argmax(s, axis=2)[:, :, None, :], 2)[:, :, 0]
    e = np.where(np.max(s, axis=2) >= 0, e, -1)
    v = 2 * np.arange(M) + (t & 1); L = G[..., v]; on = L >= 0; a = np.maximum(L, 0)
    old = d[ra, ga, a]; mine = on & (e[ra, ga, a] == v); dv = d[:, :, v][:, :, None, :]
    new = old; pick = look(X, a, v, old, dv); low = excess(pick, z)
    for j in range(1, TR):
        p = (old + j) & 15; R = look(X, a, v, p, dv); x = excess(R, z); w = mine & (x < low)
        low = np.where(w, x, low); new = np.where(w, p, new); pick = np.where(w[:, :, None], R, pick)
    up = np.max(np.where(on[:, :, None], pick, 0), axis=3)
    o = np.take_along_axis(B, a, 3); both = np.concatenate([d, np.roll(d, -1, axis=0)], axis=2); do = both[ra, ga, o]
    dmg = np.where(on, excess(look(X, o, a, do, new), z) - excess(look(X, o, a, do, old), z), -99999)
    k = np.argmax(dmg, axis=2)[:, :, None, :]
    return n[:, :, v], v, L, a, mine, new, up, np.take_along_axis(dmg, k, 2)[:, :, 0], np.take_along_axis(o, k, 2)[:, :, 0]
def graph(rng, S, share):
    m = np.argsort(rng.random((S, V)), axis=1); i = np.arange(S)[:, None]; mate = np.zeros((S, V), np.int64)
    mate[i, m[:, :M]] = m[:, M:]; mate[i, m[:, M:]] = m[:, :M]
    act = 0.3 + 0.7 * rng.random(V); act[rng.random(V) < 0.04] = 0.0
    r = rng.random((S, V))[i, np.minimum(mate, np.arange(V))]
    return np.where(r < share * act * act[mate], mate, -1)
def tidy(tab):
    tab = np.array(tab, np.int64)
    for k in range(1, len(tab)): tab[k] = np.where(np.any(tab[:k] == tab[k], axis=0), -1, tab[k])
    tab = np.take_along_axis(tab, np.argsort(tab < 0, axis=0, kind="stable"), 0)[:16]
    return np.concatenate([tab, np.full((16 - len(tab), V), -1, np.int64)])
def plain(rng, share):
    return tidy(np.concatenate([np.where(rng.random((1, V)) < 0.15, np.arange(V), -1), graph(rng, 16, share)]))
def blocks(rng, own):
    p = rng.permutation(V).reshape(-1, 16); tab = np.zeros((16, V), np.int64)
    o = np.argsort(rng.random((len(p), 16, 16)), axis=2)
    tab[:, p.reshape(-1)] = p[np.arange(len(p))[:, None, None], o].reshape(-1, 16).T
    return tab if own else tidy(np.where(tab == np.arange(V), -1, tab))
def edges():
    return np.concatenate([np.arange(8), np.arange(V - 8, V)])
def corner(rng):
    c = edges(); tab = c[np.argsort(rng.random((16, V)), axis=0)]
    size = rng.choice(np.array([16, 16, 15, 14, 2, 0]), V); size[c] = rng.choice(np.array([16, 16, 15, 14]), 16)
    tab[:2, size == 2] = np.array([[0], [V - 1]])
    for u in (0, V - 1): tab[:, u] = np.concatenate([[V - 2], rng.permutation(c[c != V - 2])])
    tab[:, V - 2] = np.concatenate([[0], rng.permutation(c[1:15]), [V - 1]]); size[[0, V - 2, V - 1]] = 16
    return np.where(np.arange(16)[:, None] < size, tab, -1)
def lift(rng, rec, z, a, v, dv, o, do):
    def ex(x): return np.add.reduce(np.maximum(rec[:, x] - z.reshape((16,) + (1,) * (x.ndim - 1) + (-1,)), 0), axis=0)
    p = np.arange(16)[:, None]; E = ex(spot(a, v, p, dv))
    new = (p + np.argmin(np.stack([np.roll(E, -j, axis=0) for j in range(TR)]), axis=0)) & 15
    F = ex(spot(o[:, None], a, do[:, None], p))
    D = np.take_along_axis(F, np.broadcast_to(new, F.shape), 1) - F
    s = np.where(D > 0, 1 + rng.random(D.shape) + 2 * (np.arange(len(o))[:, None, None] == 0), 0)
    b = np.argmax(s.reshape(-1, s.shape[-1]), axis=0)
    return b & 15, b >> 4
def parts(rng):
    gl = np.stack([np.stack([plain(rng, float(rng.choice(np.array([0.7, 1.0, 1.5, 2.5])))) for g in range(8)]) for r in range(N)])
    rec = (256 * rng.random((N, 8, 16, W)) * (0.4 + 0.6 * rng.random((N, 8, 1, W)))).astype(np.int64)
    val = rng.integers(0, 16, (N, 8, V)); zl = (256 * rng.random((N, 8, 16, M)) ** 1.5).astype(np.int64)
    th = (rng.choice(np.array([4, 40, 200, 1000]), (N, 8, M)) * rng.random((N, 8, M))).astype(np.int64)
    gs = rng.choice(np.array([0.3, 0.5, 0.8]), (N, 8, 1, 1)); full = rng.integers(0, 8, N); gs[np.arange(N), full] = 1.0; th[np.arange(N), full] = rng.integers(0, 8, (N, M))
    nb = rng.integers(0, V, (N, 8, 16, V)) + V * (rng.random((N, 8, 16, V)) < gs)
    return rec, gl, nb, val, zl, th
def pack(rec, gl, nb, val, zl, th):
    return {"rec": rec.reshape(N, 128, W).astype(np.float32).astype(BF), "gl": np.ascontiguousarray(gl.reshape(N, 128, V)).astype(np.int32), "nb": np.ascontiguousarray(nb.reshape(N, 128, V)).astype(np.int32),
            "val": val.astype(np.int32), "zl": zl.reshape(N, 128, M).astype(np.float32).astype(BF), "th": th.astype(np.int32)}
def largest(rec, gl, nb, val, zl):
    return scan(rec.astype(np.int32), gl, nb, val, zl, 0)[7]
def tune(rng, top, want):
    pos = np.argsort(np.argsort(np.where(top > 0, rng.random(top.shape), 2.0), axis=2), axis=2); sel = (pos < want) & (top > 0); coin = rng.random(top.shape)
    low = np.where(coin < 0.5, top - 1, (rng.random(top.shape) * top).astype(np.int64))
    return np.where(sel, low, np.where(coin < 0.1, 4080, np.maximum(top, 0)))
def setup_inputs(rng):
    return pack(*parts(rng))
def setup_inputs_spread(rng):
    rec, gl, nb, val, zl, th = parts(rng)
    rec = (np.exp2(8 * rng.random((N, 8, 1, W))) * rng.random((N, 8, 16, W))).astype(np.int64)
    zl = (np.exp2(8 * rng.random((N, 8, 1, M))) * rng.random((N, 8, 16, M))).astype(np.int64)
    th = np.minimum((np.exp2(12 * rng.random((N, 8, M)) ** 1.5) - 1).astype(np.int64), 4080)
    nb = (2 * V * rng.random((N, 8, 16, V)) ** 1.5).astype(np.int64); val = (16 * rng.random((N, 8, V)) ** 2).astype(np.int64)
    return pack(rec, gl, nb, val, zl, th)
def setup_inputs_ends(rng):
    rec, gl, nb, val, zl, th = parts(rng)
    rec = 255 * np.where(rng.random((N, 8, 1, W)) < 0.8, rng.integers(0, 2, (N, 8, 1, W)), rng.integers(0, 2, (N, 8, 16, W)))
    val = 15 * rng.integers(0, 2, (N, 8, V)); th = 4080 * (rng.random((N, 8, M)) < 0.4).astype(np.int64)
    zl = 255 * np.where(rng.random((N, 8, 1, M)) < 0.6, rng.random((N, 8, 1, M)) < 0.35, rng.random((N, 8, 16, M)) < 0.35).astype(np.int64)
    e = rng.random((N, 8, 16, V)); nb = np.where(e < 0.4, 0, np.where(e < 0.85, 2 * V - 1, nb))
    for r in range(N):
        few = [6, 7] + [int(g) for g in rng.permutation(6)[:2]]
        for g in range(8):
            gl[r, g] = corner(rng) if g in few else tidy(np.concatenate([graph(rng, 14, 1.5), np.zeros((1, V), np.int64), np.full((1, V), V - 1, np.int64)]))
    for g in (6, 7):
        val[:, g, 0] = 15; val[:, g, V - 2] = 0; val[:, g, V - 1] = 0; zl[:, g, :, M - 1] = 0
        th[:, g, M - 1] = np.where(np.arange(N) % 2 == 1, 0, 4080)
        nb[:, g, 15, V - 1] = 2 * V - 1; nb[:, g, 0, 0] = 0 if g == 7 else 2 * V - 1
        hi = [spot(0, V - 2, 15, 0), spot(V - 1, V - 2, 0, 0), spot(2 * V - 1, V - 1, 0, 1), spot(0, 0, 15, 0) if g == 7 else spot(2 * V - 1, 0, 0, 15)]
        lo = [spot(0, V - 2, 0, 0), spot(V - 1, V - 2, 1, 0), spot(2 * V - 1, V - 1, 0, 0), spot(0, 0, 15, 15) if g == 7 else spot(2 * V - 1, 0, 0, 0)]
        for x in lo: rec[:, g, :, x] = 0
        for x in hi: rec[:, g, :, x] = 255
    return pack(rec, gl, nb, val, zl, th)
def setup_inputs_corners(rng):
    rec, gl, nb, val, zl, th = parts(rng); c = edges(); late = []
    for r in range(N):
        for g, k in enumerate(rng.permutation(8)):
            if k == 0:
                ev = np.concatenate([[V - 2], 2 * rng.permutation(M - 1)]); od = 2 * rng.permutation(M) + 1; h = M // 2
                tab = np.full((16, V), -1, np.int64)
                tab[0, ev[:h]] = od[:h]; tab[0, od[:h]] = ev[:h]; tab[0, od[h:]] = ev[:h]; tab[1, od[h:]] = ev[h:]; tab[0, ev[h:]] = od[h:]
                late.append((r, g, ev[:h], od[:h], od[h:]))
            elif k == 1: tab = blocks(rng, True)
            elif k == 2: tab = blocks(rng, False)
            elif k == 3:
                tab = graph(rng, 16, 2.0); tab = tidy(np.where((tab & 1 == 1) & (np.arange(V) & 1 == 1), tab, -1))
            elif k == 4:
                tab = graph(rng, 16, 2.0); off = rng.random(V) < 0.5; tab = tidy(np.where(off | off[tab], -1, tab))
            elif k == 5:
                tab = np.argsort(rng.random((V, V)), axis=1)[:, :16].T; tab = np.where(np.arange(16)[:, None] < rng.integers(0, 17, V), tab, -1)
            elif k == 6:
                tab = c[np.argsort(rng.random((16, V)), axis=0)]; tab[:, c] = np.argsort(rng.random((16, V)), axis=1)[:, :16].T
            else: tab = plain(rng, 1.5)
            gl[r, g] = tab
    m = np.arange(V); e = rng.integers(0, 10, (N, 8, 16, V))
    for k, x in enumerate((0, V - 1, V, 2 * V - 1, m, m + V)): nb = np.where(e == k, x, nb)
    e = rng.integers(0, 4, (N, 8, V)); val = np.where(e == 0, 0, np.where(e == 1, 15, val))
    e = rng.integers(0, 6, (N, 8, 1, M)); zl = np.where(e == 0, 0, np.where(e == 1, 255, zl >> 1))
    want = rng.choice(np.array([0, 1, CAP - 1, CAP, CAP + 1, M]), (N, 8, 1))
    for r, g, v, a, o in late:
        zl[r, g, :, M - 1] = 0; dv = val[r, g, v]; do = val[r, g, o]; q = (np.arange(16) + 1) & 15
        x = spot(a[0], v[0], np.arange(16), dv[0]); y = spot(o[0], a[0], do[0], np.arange(16))
        s = int(np.argmax((x != y) & (x[q] != y[q]))); u = int(q[s])
        rec[r, g, :, int(x[s])] = 255; rec[r, g, :, int(y[u])] = 255; rec[r, g, :, int(x[u])] = 0; rec[r, g, :, int(y[s])] = 0
        p = lift(rng, rec[r, g], zl[r, g][:, v >> 1], a, v, dv, o[None], do[None])[0]
        val[r, g, a] = p; val[r, g, a[0]] = s; nb[r, g][:, a] = o; want[r, g, 0] = M
    th = tune(rng, largest(rec, gl, nb, val, zl), want)
    for r, g, v, a, o in late: th[r, g, M - 1] = 4079
    return pack(rec, gl, nb, val, zl, th)
def setup_inputs_crowd(rng):
    rec, gl, nb, val, zl, th = parts(rng); zl = zl >> 1; ev = 2 * np.arange(M)
    spots = np.array([V, 2 * V - 1, V + M]); cnt = np.array([CAP, CAP + 1, CAP - 1, M, CAP + 1]); want = np.zeros((N, 8, 1), np.int64)
    for r in range(N):
        most = ((2, 3), (4, 5), (3, 2), (5, 4))[r % 4]
        left = [g for g in range(1, 8) if g not in most]
        want[r, left, 0] = cnt if r == 0 else rng.permutation(cnt)
        want[r, most[0], 0] = M; want[r, most[1], 0] = M - 1
        for g in range(8):
            gl[r, g] = plain(rng, 1.5); s = int(rng.choice(spots))
            if g in most:
                od = 2 * rng.permutation(M) + 1; tab = np.full((16, V), -1, np.int64); tab[0, ev] = od; tab[0, od] = ev; gl[r, g] = tab
                o = np.tile(rng.permutation(spots)[:, None], (1, M))
                p, k = lift(rng, rec[r, g], zl[r, g], od, ev, val[r, g, ev], o, val[(r + 1) % N, g][o - V])
                val[r, g, od] = p; nb[r, g] = o[0, 0]; nb[r, g][:, od] = o[k, np.arange(M)]
            elif g == 0: nb[r, g] = (0, V - 1)[r % 2]
            elif g < 5: nb[r, g] = s
            elif g == 5: nb[r, g] = rng.choice(spots, (16, V))
            else: nb[r, g] = np.where(rng.random((16, V)) * CAP < 1, 2 * V - 1 if s == V else V, s)
    top = largest(rec, gl, nb, val, zl); got = np.minimum(np.add.reduce((top > 0).astype(np.int64), axis=2), want[:, :, 0])
    for r in range(N): want[r, 0, 0] = ((31, 0)[r % 2] - int(np.add.reduce(got[r, 1:]))) & 31
    return pack(rec, gl, nb, val, zl, tune(rng, top, want))
def check_inputs(d):
    bad = []
    for k, lo, hi in (("rec", 0, 255), ("gl", -1, V - 1), ("nb", 0, 2 * V - 1), ("val", 0, 15), ("zl", 0, 255), ("th", 0, 4080)):
        x = np.asarray(d[k]).astype(np.float64)
        if not (np.min(x) >= lo and np.max(x) <= hi): bad.append("range of " + k)
        if np.any(x != np.floor(x)): bad.append("whole numbers in " + k)
    g = np.asarray(d["gl"]).reshape(N, 8, 16, V); on = g >= 0; s = np.sort(g, axis=2)
    if np.any(on[:, :, 1:] & ~on[:, :, :-1]): bad.append("gl: a name after an empty slot")
    if np.any((s[:, :, 1:] == s[:, :, :-1]) & (s[:, :, 1:] >= 0)): bad.append("gl: a name twice in one list")
    return bad
def reference(rec, gl, nb, val, zl, th):
    X = rec.astype(np.float32).astype(np.int32).reshape(N, 8, 16, W); G = gl.astype(np.int64).reshape(N, 8, 16, V); B = nb.astype(np.int64).reshape(N, 8, 16, V)
    d = val.astype(np.int64); z = zl.astype(np.float32).astype(np.int32).reshape(N, 8, 16, M); h = th.astype(np.int64); c = np.zeros((N, 1, 1), np.int64)
    for t in range(RO):
        n, v, L, a, mine, new, up, top, who = scan(X, G, B, d, z, t)
        hurt = top > h + (c & 31)
        c = np.add.reduce(hurt.astype(np.int64).reshape(N, 8 * M), axis=1).reshape(N, 1, 1)
        z = np.roll((z + up) >> 1, 1 + t, axis=0)
        w = np.nonzero(mine); d = d + 0; d[w[0], w[1], a[w]] = new[w]
        gh = (hurt & (who >= V)).astype(np.int64); told = (gh == 1) & (np.add.accumulate(gh, axis=2) - gh < CAP)
        w = np.nonzero(told); np.add.at(d, ((w[0] + 1) % N, w[1], who[w] - V), 1); d = d & 15
        w = np.nonzero(hurt & (who < V) & (n < 16) & ~np.any(L == who[:, :, None, :], axis=2))
        G[w[0], w[1], n[w], v[w[2]]] = who[w]
    return {"yl": G.reshape(N, 128, V).astype(np.float32), "yd": d.astype(np.float32), "yz": z.reshape(N, 128, M).astype(np.float32).astype(BF)}

@@ -1,0 +1,711 @@
+from concourse.mybir import AluOpType, ActivationFunctionType, AxisListType
+
+F, B, H, I, U = "float32", "bfloat16", "float16", "int32", "uint16"
+SB = {
+    "X": (512, F), "gx": (128, F), "mA": (32, F), "ci": (16, I), "cf": (16, F), "cc": (32, F),
+    "BD": (128, B), "BDh": (128, H), "BDdp": (128, B), "BDdn": (128, B), "BDo": (128, H), "BDo2": (128, B), "BDt": (128, B),
+    "ID": (128, B), "TRI": (128, B), "ones": (2048, B), "Tlo": (128, B), "x32": (512, B), "rI": (32, I), "offR": (32, U), "FH": (2048, B),
+    "E64": (144, B), "Er0": (144, B), "En0": (144, B), "En1": (144, B), "En2": (144, B), "Es": (144, B), "Ek": (144, B), "Eo": (144, B),
+    "E1": (144, B), "Eth": (144, B), "Eh": (144, H),
+    "TA": (1024, H), "HX": (512, H), "mask": (1024, B), "tie": (256, B), "Mrow": (512, F), "x21": (512, F), "x613": (512, F),
+    "m21": (32, F), "m37": (32, F), "m613": (32, F), "mneg": (32, F), "cB": (16, F),
+    "glI": (512, I), "LSp": (528, F), "offN": (512, U), "onb": (512, B), "C": (512, F), "C0": (512, F), "C1": (512, F), "GN": (8192, B), "T01": (528, B),
+    "nrow": (512, B), "ky": (512, F), "kyT": (512, F), "ks": (512, F), "kp": (512, F), "kI": (32, I), "khI": (32, I), "khH": (32, H), "klI": (32, I), "klH": (32, H),
+    "km0": (32, F), "km1": (32, F), "km2": (32, F), "c15m": (32, F),
+    "W": (4112, B), "nbI": (512, I), "vr0": (512, I), "vrh": (512, H), "thr": (256, I), "thI": (512, I), "thb": (512, B), "thB": (16, F), "thK": (16, F), "thT": (16, F),
+    "z0": (272, B), "z1": (272, B), "z2": (272, B), "z3": (256, B), "drow": (1024, B),
+    "dA": (32, F), "p4": (128, F), "pI": (256, I), "low": (128, B),
+    "gs0": (32, B), "gs1": (32, B), "gs2": (32, B), "gl0": (32, B), "gl1": (32, B), "gl2": (32, B),
+    "hs0": (32, B), "hs1": (32, B), "hs2": (32, B), "hl0": (32, B), "hl1": (32, B), "hl2": (32, B),
+    "sI": (512, I), "sF": (1024, F), "sU": (512, U), "eq": (512, B), "Zq": (512, B), "gr": (512, B), "gr2": (512, B), "prod": (512, H),
+    "G4": (2048, B), "D2": (1024, B), "tA": (64, F), "rowh": (64, B), "dlt": (512, B), "WK": (4608, B),
+    "GA": (4608, B), "GL": (4096, B), "sc": (4096, B), "offL": (256, U), "offM": (256, U), "zs": (256, B), "zf": (256, F), "lv": (1280, F), "lvI": (512, I),
+    "on16": (256, F), "hiT": (512, B), "yv": (512, B), "tk": (512, F), "kwI": (32, I), "wr": (256, B), "eqo": (256, B), "sg": (256, B),
+    "sB": (256, F), "sBb": (64, B), "full": (16, B), "mk": (512, B), "jv": (16, H), "jw": (48, B), "oX": (32, F), "lt": (2048, B), "rt": (512, B),
+}
+ALIAS = {}
+
+
+def share(to, names):
+    at = 0
+    for n in names:
+        ALIAS[n] = (to, at)
+        at += SB[n][0]
+    return at
+
+
+SCRATCH = {}
+for _to, _ns in (("aI", ("vr0", "nbI", "thr", "thI")), ("aB", ("onb", "thb")), ("aF", ("ks", "kp")),
+                 ("sm", ("m21", "m37", "m613", "mneg", "c15m", "km0", "km1", "km2", "oX", "dA", "tA", "cB", "thB", "thK", "thT")),
+                 ("smI", ("kI", "khI", "klI", "rI", "kwI")),
+                 ("EE", ("E64", "Er0", "En0", "En1", "En2", "Es", "Ek", "Eo", "E1", "Eth"))):
+    SCRATCH[_to] = ("sbuf", [128, share(_to, _ns)], SB[_ns[0]][1])
+for _n in SB:
+    if _n not in ALIAS:
+        SCRATCH[_n] = ("sbuf", [128, SB[_n][0]], SB[_n][1])
+for _b in range(8):
+    SCRATCH["b%d" % _b] = ("psum", [128, 512], F)
+SEMAPHORES = ["sV", "sS", "sP", "sG"] + ["d%d" % i for i in range(12)] + [a + str(t) for a in ("az", "ah", "ag", "lz", "lh", "lg") for t in range(3)]
+
+
+def rank_program(g, core, T, topo):
+    rank = T.rank_of(core)
+    if rank is None:
+        return
+    N = len(T.cores)
+    OP, AF = AluOpType, ActivationFunctionType
+    ADD, SUB, MUL, MAX, MIN = OP.add, OP.subtract, OP.mult, OP.max, OP.min
+    GT, GE, LT, LE, EQ = OP.is_gt, OP.is_ge, OP.is_lt, OP.is_le, OP.is_equal
+    SHR, AND = OP.arith_shift_right, OP.bitwise_and
+    eng = {"V": g.vector, "S": g.scalar, "P": g.tensor, "G": g, "D": g.sync}
+    hist, known, total, nd = {}, {q: {} for q in "VSPGD"}, {}, [0]
+    banks = ["b%d" % k for k in range(8)]
+
+    def order(q, acc):
+        toks = []
+        for (n, lo, hi), w in acc:
+            for r in hist.get(n, []):
+                if n in banks and r[3] != q:
+                    toks.append(r[4])
+                    continue
+                if not (lo < r[1] and r[0] < hi) or not (w or r[2]):
+                    continue
+                if r[3] == q == "P":
+                    continue
+                toks.append(r[4])
+        toks.sort(key=lambda k: -len(k[2]))
+        for i, (s, v, kn) in enumerate(toks):
+            if known[q].get(s, 0) >= v:
+                continue
+            if any(j != i and (k[2].get(s, 0) >= v and (k[0] != s or k[1] > v)) for j, k in enumerate(toks)):
+                continue
+            eng[q].wait_ge(T.sem[s], v)
+            for a, b in kn.items():
+                known[q][a] = max(known[q].get(a, 0), b)
+            known[q][s] = max(known[q].get(s, 0), v)
+
+    def note(q, acc, tok, dma=False):
+        for (n, lo, hi), w in acc:
+            keep = []
+            for r in hist.get(n, []):
+                inside = lo <= r[0] and r[1] <= hi
+                ps = n in banks
+                if inside and (w if not ps else (w or not r[2])) and not (ps and r[3] != q and not w):
+                    continue
+                if inside and not w and not r[2] and r[3] == q and not dma:
+                    continue
+                keep.append(r)
+            keep.append((lo, hi, w, "dma" if dma else q, tok))
+            hist[n] = keep
+
+    def emit(q, outs, ins, call):
+        acc = [(a, False) for v in ins if v is not None and not isinstance(v, (int, float)) for a in v[1]] + [(a, True) for a in outs[1]]
+        order(q, acc)
+        s = "s" + q
+        total[s] = total.get(s, 0) + 1
+        call(eng[q]).then_inc(T.sem[s], 1)
+        kn = dict(known[q])
+        kn[s] = total[s]
+        note(q, acc, (s, total[s], kn))
+
+    def a(n, lo=0, hi=None, st=1):
+        hi = SB[n][0] if hi is None and n in SB else 512 if hi is None else hi
+        if n in ALIAS:
+            o = ALIAS[n][1]
+            n, lo, hi = ALIAS[n][0], lo + o, hi + o
+        return (T[n][:, lo:hi:st] if st > 1 else T[n][:, lo:hi], [(n, lo, hi)])
+
+    def ind(w, o):
+        return (w[0].indirect(o[0]), w[1] + o[1])
+
+    def x(v):
+        return v if v is None or isinstance(v, (int, float)) else v[0]
+
+    def ts(o, i, s1, op0, s2=None, op1=None):
+        if op1 is None:
+            emit("V", o, [i, s1], lambda e: e.tensor_scalar(o[0], i[0], x(s1), None, op0))
+        else:
+            emit("V", o, [i, s1, s2], lambda e: e.tensor_scalar(o[0], i[0], x(s1), x(s2), op0, op1))
+
+    def tt(o, i, j, op):
+        emit("V", o, [i, j], lambda e: e.tensor_tensor(o[0], i[0], j[0], op))
+
+    def cp(o, i):
+        emit("V", o, [i], lambda e: e.tensor_copy(o[0], i[0]))
+
+    def fill(o, c):
+        emit("V", o, [], lambda e: e.memset(o[0], c))
+
+    def scan(o, d0, d1, init, op1):
+        emit("V", o, [d0, d1], lambda e: e.tensor_tensor_scan(o[0], d0[0], d1[0], init, MUL, op1))
+
+    def act(o, i, scale=1.0, bias=0.0, f=None):
+        f = (AF.Copy if bias == 0.0 else AF.Identity) if f is None else f
+        emit("S", o, [i, scale], lambda e: e.activation(o[0], i[0], f, bias=bias, scale=x(scale)))
+
+    def mm(o, l, r, start, stop):
+        emit("P", o, [l, r], lambda e: e.matmul(o[0], l[0], r[0], start, stop))
+
+    def iota(o, pat, base, cm):
+        emit("G", o, [], lambda e: e.iota(o[0], pat, base, cm, allow_small_or_imprecise_dtypes=True))
+
+    def keep(o, i, pat, op, base, cm, c=0.0):
+        emit("G", o, [i], lambda e: e.affine_select(o[0], i[0], pat, op, c, base, cm))
+
+    def dma(q, out, in_, acc):
+        order(q, acc)
+        s = "d%d" % nd[0]
+        nd[0] += 1
+        eng[q].dma_start(out, in_).then_inc(T.sem[s], 16)
+        total[s] = 16
+        kn = dict(known[q])
+        kn[s] = 16
+        note(q, acc, (s, 16, kn), True)
+
+    def es(E, q):
+        return a(E, 15 - q, 143 - q)
+
+    def conv(o, E, src, first=True, last=True):
+        for q in range(16):
+            mm(o, es(E, q), src(q), first and q == 0, last and q == 15)
+
+    def every(n, lo, hi):
+        return lambda q: a(n, lo + q, hi, 16)
+
+    def rows(bank, src, n, lo=0, rest=None):
+        for q in range(16):
+            o, w = a(bank, lo + q, lo + 16 * n, 16), a("FH", 128 * q, 128 * q + 128)
+            mm(o, w, src, True, rest is None)
+            if rest is not None:
+                mm(o, w, rest, False, True)
+
+    def send(dst, buf, rbuf, n, arr, loc):
+        to = T.cores[dst]
+        use = topo.engines(core, to)[:8]
+        rid, pid = topo.addr(to)[0], topo.addr(to)[1]
+        acc = [((buf, 0, n), False)]
+        order("G", acc)
+        g.remote_dma(T[rbuf][:, 0:n], T[buf][:, 0:n], T.sem[arr], T.sem[loc], pid, rid, sum(1 << e for e in use))
+        total[loc] = len(use)
+        note("G", acc, (loc, len(use), {loc: len(use)}), True)
+
+    def lands(src, buf, n, arr):
+        k = len(topo.engines(T.cores[src], core)[:8])
+        total[arr] = k
+        note("R", [((buf, 0, n), True)], (arr, k, {arr: k}), True)
+
+    up, dn = (rank + 1) % N, (rank - 1) % N
+    for t in range(3):
+        lands((rank - 1 - t) % N, "z%d" % (t + 1), 256, "az%d" % t)
+        lands(dn, "hl%d" % t, 32, "ah%d" % t)
+        lands(up, "gl%d" % t, 32, "ag%d" % t)
+
+    def load(q, v, src, part=None):
+        dma(q, v[0] if part is None else part, src, [(r, True) for r in v[1]])
+
+    load("D", a("glI"), T.gl[:, :])
+    iota(a("ci", 0, 1), [[0, 1]], 0, 1)
+    iota(a("gx"), [[1, 8], [0, 16]], 0, 0)
+    iota(a("X"), [[1, 512]], 0, 0)
+    load("S", a("W", 16), T.rec[:, :])
+    fill(a("vr0"), 0)
+    fill(a("thr"), 0)
+    load("D", a("vr0"), T.val[:, :], T["aI"][0:128:16, 0:512])
+    load("D", a("nbI"), T.nb[:, :])
+    load("D", a("z0", 0, 256), T.zl[:, :])
+    load("D", a("thr"), T.th[:, :], T["aI"][0:128:16, 1024:1280])
+    iota(a("ones"), [[0, 2048]], 1, 0)
+    keep(a("mask"), a("ones", 0, 1024), [[0, 64], [1, 16]], GT, 0, 0)
+    iota(a("mA"), [[16, 32]], 0, 1)
+    iota(a("tie"), [[-256, 16], [0, 16]], 3840, 0)
+    iota(a("x32"), [[0, 16], [1, 32]], 0, 0)
+    iota(a("rI"), [[1, 16], [0, 2]], 0, 0)
+    keep(a("ID"), a("ones", 0, 128), [[-1, 128]], EQ, 0, 1)
+    keep(a("FH"), a("ones"), [[-1, 16], [-16, 8], [0, 16]], EQ, 0, 1)
+    iota(a("Tlo"), [[0, 8], [1, 16]], 0, 0)
+    keep(a("Tlo"), a("Tlo"), [[-16, 8], [0, 16]], GE, 0, 1, -1.0)
+    keep(a("Tlo"), a("Tlo"), [[16, 8], [0, 16]], GE, 15, -1, -1.0)
+
+    for n, (op, c) in enumerate(((AND, 15), (AND, 112), (AND, 96), (SHR, 4), (AND, 14), (AND, 1), (AND, 7), (AND, 8))):
+        ts(a("ci", n + 1, n + 2), a("ci", 0, 1), c, op)
+    ts(a("ci", 9, 10), a("ci", 0, 1), 4, SHR, 1, AND)
+    cp(a("cf", 0, 10), a("ci", 0, 10))
+
+    def cf(n):
+        return a("cf", n, n + 1)
+
+    def cc(n):
+        return a("cc", n, n + 1)
+
+    def mk_e(n, w):
+        ts(a(n), a("X", 0, 144), cc(0), EQ, w, MUL)
+
+    ts(a("BD"), a("gx"), cf(4), EQ)
+    keep(a("BDdp"), a("BD"), [[0, 8], [-1, 16]], GE, 1, 0)
+    keep(a("BDt"), a("BD"), [[0, 8], [1, 16]], GE, -2, 0)
+    keep(a("BDt"), a("BDt"), [[0, 8], [-1, 16]], GE, 3, 0)
+    keep(a("TRI"), a("BD"), [[-1, 128]], GT, 0, 1)
+    ts(cc(8), cf(1), 1.0, OP.not_equal)
+    ts(cc(7), cf(1), 0.0, OP.not_equal)
+    ts(cc(9), cc(8), 33.0, MUL, -32.0, ADD)
+    ts(cc(10), cc(7), 33.0, MUL, -32.0, ADD)
+    ts(cc(0), cf(2), 15.0, ADD)
+    ts(cc(2), cf(1), 2.0, EQ, 16384.0, MUL)
+    ts(cc(11), cf(1), -1024.0, MUL, 15359.0, ADD)
+    fill(a("T01", 0, 1), -32.0)
+    mk_e("En2", cc(2))
+    ts(a("LSp", 0, 512), a("glI"), 1.0, ADD)
+    act(a("onb"), a("LSp", 0, 512), f=AF.Sign)
+    ts(a("offN"), a("glI"), 1.0, ADD)
+    mm(a("b5"), a("BD"), a("onb"), True, True)
+    ts(a("T01", 1, 513, 2), a("b5", 0, 512, 2), cc(8), MUL, cc(9), ADD)
+    ts(a("T01", 2, 514, 2), a("b5", 1, 512, 2), cc(7), MUL, cc(10), ADD)
+
+    def gather_n(q, ch):
+        o, i = a("GN", 1024 * ch, 1024 * ch + 1024), ind(a("T01", 0, 513), a("offN", 64 * ch, 64 * ch + 64))
+        if q == "V":
+            cp(o, i)
+        else:
+            act(o, i)
+
+    def kmax_pe(bank, ch):
+        conv(a(bank, 128 * ch, 128 * ch + 128), "En2", every("GN", 2048 * ch, 2048 * ch + 2048))
+
+    def kmax_key(src, add, ch):
+        lo, hi = 128 * ch, 128 * ch + 128
+        if add is not None:
+            tt(a("ky", lo, hi), a(src, lo, hi), a(add, lo, hi), ADD)
+            src = "ky"
+        emit("V", a("kyT", lo, hi), [a(src, lo, hi)], lambda e: e.transpose(a("kyT", lo, hi)[0], a(src, lo, hi)[0]))
+        scan(a("ks", lo, hi), a("mask", 0, 128), a("kyT", lo, hi), 0.0, MAX)
+
+    def kmax_fin(small, so, dest):
+        cp(a("kI"), a("ks", 15, 512, 16))
+        ts(a("khI"), a("kI"), 10, SHR)
+        ts(a("klI"), a("kI"), 1023, AND)
+        cp(a("khH"), a("khI"))
+        cp(a("klH"), a("klI"))
+        for c1 in range(2):
+            n = 0
+            for g1 in range(2):
+                for part, src in ((1, "khH"), (0, "klH")):
+                    k = 128 * (4 * part + 2 * c1 + g1)
+                    mm(a(small, so + c1, so + 32, 2), a("TA", k, k + 128), a(src, g1, 32, 2), n == 0, n == 3)
+                    n += 1
+        return lambda: ts(a(dest), a(small, so, so + 32), 512.0, MAX)
+
+    for ch in range(1, 6):
+        gather_n("S", ch)
+    for ch in (0, 6, 7):
+        gather_n("V", ch)
+    ts(a("mA"), a("mA"), cf(2), SUB)
+    mk_e("E1", 1.0)
+    kmax_pe("b6", 0)
+    kmax_pe("b6", 1)
+    kmax_pe("b4", 3)
+    kmax_pe("b4", 2)
+    ts(a("C"), a("LSp", 0, 512), cc(11), ADD)
+    ts(a("lvI", 0, 512), a("glI"), 1, AND)
+    ts(a("kp"), a("lvI", 0, 512), -524288.0, MUL)
+    tt(a("C0"), a("C"), a("kp"), ADD)
+    kmax_key("b6", "C0", 0)
+    kmax_key("b6", "C0", 1)
+    mk_e("Eh", 1.0)
+    cp(a("BDh"), a("BD"))
+    cp(a("vrh"), a("vr0"))
+    mm(a("b7"), a("BDh"), a("vrh"), True, True)
+    conv(a("b3", 0, 32), "Eh", every("vrh", 0, 512))
+    for n, s, b, src in (("m21", 2.0, 1.0, "mA"), ("m37", 2.0, 37.0, "mA"), ("m613", 2.0, 613.0, "mA"), ("mneg", 1.0, -512.0, "mA"),
+                         ("Mrow", 1.0, 1.0, "X"), ("x613", 2.0, 613.0, "X"), ("x21", 2.0, 1.0, "X")):
+        act(a(n), a(src), s, b)
+    act(a("nrow"), a("b5"))
+    act(a("drow", 0, 512), a("b7"))
+    act(a("C1"), a("kp"), -2.0, -524288.0)
+    for g1 in range(2):
+        ts(cc(16 + g1), cf(3), cf(1), ADD, 16.0 * g1, ADD)
+    ts(cc(18), cf(9), 0.0, EQ)
+    for c1, c in enumerate((cc(18), cf(9))):
+        ts(cc(20 + c1), c, 1024.0, MUL)
+        for g1 in range(2):
+            for part in range(2):
+                k = 128 * (4 * part + 2 * c1 + g1)
+                ts(a("TA", k, k + 128), a("X", 0, 128), cc(16 + g1), EQ, cc(20 + c1) if part else c, MUL)
+    kmax_key("b4", "C0", 3)
+    kmax_key("b4", "C0", 2)
+    km0 = kmax_fin("b1", 0, "km0")
+    ts(cc(1), cf(1), 0.0, EQ)
+    ts(cc(4), cf(1), 256.0, MUL, 1024.0, ADD)
+    ts(cc(5), cf(5), 0.0, EQ, 4096.0, MUL)
+    ts(cc(6), cf(5), 2.0, EQ)
+    ts(cc(22), cc(1), 64.0, MUL)
+    ts(cc(3), cf(1), 1.0, EQ, 16384.0, MUL)
+    ts(cc(23), cc(1), 16384.0, MUL)
+    act(a("Er0"), a("E1"), cc(1))
+    km0()
+    cp(a("dA"), a("b3", 0, 32))
+    cp(a("gs0"), a("dA"))
+    send(dn, "gs0", "gl0", 32, "ag0", "lg0")
+    iota(a("WK", 512), [[0, 4096]], 0, 0)
+    later = [None] * 4
+    fill(a("LSp", 512, 528), 0.0)
+    fill(a("drow", 512, 528), 0.0)
+    fill(a("W", 0, 16), 0.0)
+    fill(a("z0", 256, 272), 0.0)
+
+    def trial_tables():
+        for j in range(4):
+            ts(a("pI", 32 * j, 32 * j + 32), a("dA"), float(j), ADD)
+        ts(a("pI", 128, 256), a("pI", 0, 128), 15, AND)
+        cp(a("p4"), a("pI", 128, 256))
+
+    def consts_t():
+        ts(a("thI", 0, 256), a("thr"), 6, SHR)
+        ts(a("thI", 256, 512), a("thr"), 63, AND)
+        cp(a("thb"), a("thI"))
+        conv(a("b5", 64, 80), "Eth", every("thb", 0, 256), True, False)
+        conv(a("b5", 64, 80), "Er0", every("thb", 256, 512), False, True)
+        conv(a("b5", 96, 128), "Er0", every("nrow", 0, 512))
+
+    def consts_d():
+        cp(a("thB"), a("b5", 64, 80))
+        ts(a("thK"), a("thB"), 4096.0, MUL, 4095.0, ADD)
+        ts(a("c15m"), a("b5", 96, 128), -1024.0, MUL, 15359.0, ADD)
+
+    def consts_e():
+        ts(cc(12), cf(7), 2.0, MUL, cf(2), ADD)
+        ts(cc(13), cc(12), 1.0, ADD)
+        ts(cc(14), cf(8), 0.0, EQ)
+        ts(cc(15), cf(8), 0.0, GT)
+        for t in range(2):
+            for h in range(2):
+                k = 128 * (2 * t + h)
+                ts(a("HX", k, k + 128), a("X", 0, 128), cc(12 + t), EQ, cc(14 + h), MUL)
+        for t in (1, 2):
+            fill(a("z%d" % t, 256, 272), 0.0)
+
+    def ghost_rows(src):
+        rows("b7", src, 32)
+        act(a("drow", 512, 1024), a("b7"))
+
+    def f(n):
+        return a("sF", 32 * n, 32 * n + 32)
+
+    def i(n):
+        return a("sI", 32 * n, 32 * n + 32)
+
+    def u(n, m=1):
+        return a("sU", 32 * n, 32 * (n + m))
+
+    for t in range(3):
+        par, zt = t & 1, "z%d" % t
+
+        def med(n, o=0, par=par):
+            return a(n, o + par, o + 512, 2)
+
+        if t == 0:
+            cp(i(0), a("km0"))
+        else:
+            tt(i(0), a("km%d" % t), f(31), MAX)
+        ts(i(1), i(0), 1023, AND)
+        cp(u(0), i(1))
+        ts(i(2), i(0), 1, SHR, 511, AND)
+        cp(u(2), i(2))
+        act(a("gr"), ind(a("drow", 0, 528), u(0)))
+        ts(f(0), i(1), 2.0, MUL, 1.0, ADD)
+        ts(a("offL"), med("LSp"), -1.0, ADD)
+        tt(a("eq"), ind(a("LSp"), u(0)), a("Mrow"), EQ)
+        if t == 0:
+            act(a("Zq"), ind(a(zt), u(2)))
+
+        def ga(ch):
+            act(a("GA", 512 + 1024 * ch, 1536 + 1024 * ch), ind(a("drow", 0, 512), a("offL", 64 * ch, 64 * ch + 64)))
+
+        if t == 0:
+            for n, c in (("Es", cc(4)), ("E64", 64.0), ("Eth", cc(22))):
+                act(a(n), a("E1"), c)
+            trial_tables()
+        for j in range(4):
+            act(f(4 + j), f(0), 1.0, 612.0)
+        act(f(2), f(0), 0.25, -1024.25 - 0.5 * par)
+        act(f(27), f(0), 4.0, -4.0 - 8.0 * par)
+        for j in range(4):
+            act(a("low", 32 * j, 32 * j + 32), a("p4", 32 * j, 32 * j + 32), 1.0, 16.0 * j)
+        if t:
+            act(a("Zq"), ind(a(zt), u(2)))
+        if t != 1:
+            ga(0)
+        else:
+            gather_n("S", 1)
+        if t:
+            later[0]()
+        conv(a("b1", 0, 32), "Er0", every("gr", 0, 512))
+        conv(a("b3", 0, 32), "Es", every("eq", 0, 512))
+        tt(i(3), f(0), a("mA"), MUL)
+        ts(i(4), i(3), 4, SHR, 4095, AND)
+        tt(f(1), i(4), a("mA"), ADD)
+        tt(a("sF", 256, 384), a("p4"), a("sF", 128, 256), MUL)
+        if t == 0:
+            tt(a("kp"), a("ky"), a("C1"), ADD)
+            ts(a("b0"), a("nbI"), 1.0, ADD)
+        tt(a("prod"), a("b0"), a("eq"), MUL)
+        conv(a("b2", 0, 32), "Eh", every("prod", 0, 512))
+        if t:
+            ghost_rows(a("rowh", 32, 64))
+        conv(a("b4", 0, 16), "Er0", lambda q: a("nrow", 2 * q + par, 512, 32))
+        tt(f(3), a("b1", 0, 32), a("m37"), MUL)
+        tt(f(3), f(3), f(1), ADD)
+        for j in range(4):
+            tt(i(8 + j), f(8 + j), f(3), ADD)
+        ts(a("sI", 256, 384), a("sI", 256, 384), 4095, AND)
+        ts(u(4, 4), a("sI", 256, 384), 16.0, ADD)
+
+        def trial(j):
+            tt(a("G4", 512 * j, 512 * j + 512), ind(a("W"), u(4 + j)), a("Zq"), MAX)
+
+        act(a("lv", 0, 256), med("LSp"), 1.0, -1.0)
+        act(a("lv", 512, 768), med("LSp"), 2.0, 35.0)
+        act(a("on16"), med("LSp"), f=AF.Sign)
+        act(a("on16"), a("on16"), 8208.0, -8192.0)
+        trial(0)
+        trial(1)
+        if t == 0:
+            cp(a("rowh", 32, 64), a("gl0"))
+            ghost_rows(a("rowh", 32, 64))
+        ts(f(16), a("b2", 0, 32), -1.0, ADD, 0.0, MAX)
+        cp(u(8), f(16))
+        act(a("gr2"), ind(a("drow"), u(8)))
+        if t == 1:
+            ga(0)
+        mm(a("b1", 64, 128), a("ID"), a("low", 0, 64), True, False)
+        conv(a("b1", 64, 128), "E64", every("G4", 0, 1024), False, True)
+        act(a("tA"), a("b1", 64, 128))
+        ga(1)
+        tt(f(17), a("b3", 0, 32), f(2), ADD)
+        ts(f(18), a("b3", 0, 32), 0.0, GT)
+        ts(f(26), a("b3", 0, 32), 1.0 / 256, MUL, 508.0, ADD)
+        conv(a("b3", 32, 64), "Er0", every("gr2", 0, 512))
+        trial(2)
+        tt(f(17), f(17), a("mneg"), MAX)
+        tt(i(5), f(16), a("m21"), MUL)
+        ts(f(20), f(16), 2.0, MUL, 37.0, ADD)
+        ts(u(10), f(17), 512.0, ADD)
+        ts(i(5), i(5), 4, SHR, 4095, AND)
+        tt(f(22), a("dA"), f(20), MUL)
+        tt(f(26), f(26), f(27), ADD)
+        ts(a("full"), a("b4", 0, 16), 15.5, GT)
+        tt(f(26), f(26), f(18), MUL)
+        trial(3)
+        mm(a("b2", 64, 128), a("ID"), a("low", 64, 128), True, False)
+        conv(a("b2", 64, 128), "E64", every("G4", 1024, 2048), False, True)
+        if t == 0:
+            act(a("BDdn"), a("BDdp"), -1.0)
+            cp(a("BDo"), a("BDt"))
+            cp(a("offR"), a("rI"))
+        mm(a("b4"), a("BDo"), a("prod"), True, False)
+        ga(2)
+        ga(3)
+        tt(f(26), f(26), a("mA"), MAX)
+        tt(f(19), i(5), f(16), ADD)
+        cp(u(11), f(26))
+        tt(f(21), a("b3", 32, 64), a("m613"), MUL)
+        tt(f(19), f(19), f(21), ADD)
+        tt(i(6), f(22), f(19), ADD)
+        ts(i(6), i(6), 4095, AND)
+        ts(u(12), i(6), 16.0, ADD)
+        tt(a("D2", 0, 512), ind(a("W"), u(12)), a("Zq"), MAX)
+        mm(a("b4"), a("BDdn"), a("D2", 0, 512), False, False)
+        tt(a("tk", 0, 64), a("tA"), a("b2", 64, 128), MIN)
+        tt(i(7), a("tk", 0, 32), a("tk", 32, 64), MIN)
+        ts(i(7), i(7), 15, AND)
+        tt(f(23), i(7), f(20), MUL)
+        cp(a("rowh", 0, 32), i(7))
+        tt(i(12), f(23), f(19), ADD)
+        tt(f(24), i(7), a("dA"), SUB)
+        ts(i(12), i(12), 4095, AND)
+        ts(u(14), i(12), 16.0, ADD)
+        tt(a("D2", 512, 1024), ind(a("W"), u(14)), a("Zq"), MAX)
+        rows("b7", a("rowh", 0, 32), 32)
+        act(a("dlt"), a("b7"))
+        mm(a("b4"), a("BDdp"), a("D2", 512, 1024), False, True)
+        act(a("hiT"), a("b4"), cf(6))
+        if t:
+            later[2]()
+        if t == 1:
+            gather_n("S", 2)
+            gather_n("S", 3)
+            kmax_pe("b5", 0)
+        if t == 0:
+            for n, s, src in (("Ek", cc(5), "E1"), ("Eo", cc(6), "E1"), ("BDo2", cc(6), "BD"), ("En1", cc(3), "E1"), ("En0", cc(23), "E1")):
+                act(a(n), a(src), s)
+            act(a("cB"), a("mA", 0, 16), 1.0, 3840.0)
+            consts_t()
+        tt(f(24), f(24), f(18), MUL)
+        tt(f(25), a("dA"), f(24), ADD)
+        if t < 2:
+            cp(a("gs%d" % (t + 1)), f(25))
+            send(dn, "gs%d" % (t + 1), "gl%d" % (t + 1), 32, "ag%d" % (t + 1), "lg%d" % (t + 1))
+        ts(a("mk", 256 * par, 256 * par + 256), med("nrow"), cf(1), EQ)
+        tt(a("lvI", 0, 256), a("lv", 0, 256), med("x21"), MUL)
+        ts(a("lvI", 0, 256), a("lvI", 0, 256), 4, SHR, 4095, AND)
+        cp(ind(a("GA"), u(11)), a("dlt"))
+        conv(a("b6", 0, 256), "Er0", every("GA", 512, 4608))
+        tt(a("yv"), a("b4"), a("hiT"), SUB)
+        cp(ind(a("WK"), u(10)), a("yv"))
+        mm(a("b7", 0, 256), a("ID"), a("tie"), True, False)
+        conv(a("b7", 0, 256), "Ek", every("WK", 512, 4608), False, True)
+        tt(a("lv", 256, 512), a("lvI", 0, 256), a("lv", 0, 256), ADD)
+        tt(a("lv", 768, 1024), a("lv", 512, 768), med("drow"), MUL)
+        tt(a("lv", 256, 512), a("lv", 256, 512), a("lv", 768, 1024), ADD)
+        tt(a("b6", 256, 512), a("b6", 0, 256), med("x613"), MUL)
+        tt(a("lvI", 256, 512), a("b6", 256, 512), a("lv", 256, 512), ADD)
+        ts(a("lvI", 256, 512), a("lvI", 256, 512), 4095, AND)
+        tt(a("lv", 768, 1024), a("lvI", 256, 512), a("on16"), ADD)
+        cp(a("offM"), a("lv", 768, 1024))
+        for ch in range(4):
+            act(a("GL", 1024 * ch, 1024 * ch + 1024), ind(a("W"), a("offM", 64 * ch, 64 * ch + 64)))
+
+        def level_scan(ch):
+            lo = 1024 * ch
+            scan(a("sc", lo, lo + 1024), a("mask"), a("GL", lo, lo + 1024), 0.0, MAX)
+
+        if t == 0:
+            consts_d()
+            for ch in range(4):
+                kmax_key("kp", None, ch)
+            later[1] = kmax_fin("b1", 224, "km1")
+        if t == 1:
+            gather_n("V", 4)
+            for ch in (5, 6, 7):
+                gather_n("S", ch)
+            kmax_key("b5", "C0", 0)
+            kmax_pe("b5", 1)
+        if t:
+            later[3]()
+        cp(a("tk", 64, 192), a("b7", 128, 256))
+        tt(a("tk", 192, 320), a("b7", 0, 128), a("tk", 64, 192), MAX)
+        tt(a("tk", 320, 384), a("tk", 192, 256), a("tk", 256, 320), MAX)
+        tt(a("tk", 384, 416), a("tk", 320, 352), a("tk", 352, 384), MAX)
+        tt(a("kwI", 0, 16), a("tk", 384, 400), a("tk", 400, 416), MAX)
+        ts(a("kwI", 16, 32), a("kwI", 0, 16), 3840, AND)
+        tt(a("sB", 0, 16), a("cB"), a("kwI", 16, 32), SUB)
+        cp(a("sU", 480, 496), a("sB", 0, 16))
+        cp(a("wr"), ind(a("WK", 512, 4608), a("sU", 480, 496)))
+        tt(a("sB", 16, 32), a("kwI", 0, 16), a("thK"), GT)
+        cp(a("sBb", 0, 16), a("sB", 16, 32))
+        conv(a("b1", 128, 144), "Eo", every("wr", 0, 256))
+        mm(a("b4", 0, 256), a("BDo2"), a("wr"), True, True)
+        if t < 2:
+            mm(a("b3", 128, 144), a("ones", 0, 128), a("sBb", 0, 16), True, True)
+        level_scan(0)
+        tt(a("sB", 32, 48), a("b1", 128, 144), a("sB", 16, 32), MUL)
+        ts(a("sBb", 16, 32), a("sB", 32, 48), 512.5, GT)
+        mm(a("b2", 128, 144), a("BD"), a("sBb", 16, 32), True, True)
+        mm(a("b2", 144, 160), a("TRI"), a("sBb", 16, 32), True, True)
+        tt(a("eqo"), med("LSp"), a("b4", 0, 256), EQ)
+        mm(a("b1", 192, 208), a("ID"), a("full"), True, False)
+        conv(a("b1", 192, 208), "E1", every("eqo", 0, 256), False, True)
+        ts(a("sB", 48, 64), a("sB", 32, 48), -512.0, ADD, 0.0, MAX)
+        scan(a("sB", 64, 80), a("ones", 0, 16), a("b2", 128, 144), -60.0, ADD)
+        tt(a("sB", 80, 96), a("sB", 64, 80), a("b2", 144, 160), LE)
+        tt(a("sB", 96, 112), a("sB", 80, 96), a("sB", 48, 64), MUL)
+        ts(a("kwI", 0, 16), a("sB", 96, 112), -1.0, ADD)
+        ts(a("kwI", 16, 32), a("kwI", 0, 16), 15, AND)
+        ts(a("kwI", 0, 16), a("kwI", 0, 16), 4, SHR)
+        cp(a("sB", 112, 144), a("kwI", 0, 32))
+        tt(a("rt"), ind(a("sB", 112, 128), a("offR")), a("x32"), EQ)
+        for h in range(16):
+            ts(a("lt", 128 * h, 128 * h + 128), a("Tlo"), a("sB", 128 + h, 129 + h), EQ)
+            mm(a("b2", 192, 224), a("lt", 128 * h, 128 * h + 128), a("rt", 32 * h, 32 * h + 32), h == 0, h == 15)
+        ts(a("sB", 144, 160), a("sB", 32, 48), 512.5, LT)
+        cp(a("hs%d" % t), a("b2", 192, 224))
+        send(up, "hs%d" % t, "hl%d" % t, 32, "ah%d" % t, "lh%d" % t)
+        tt(a("sB", 144, 160), a("sB", 144, 160), a("b1", 192, 208), GT)
+        tt(a("jv"), a("sB", 144, 160), a("sB", 32, 48), MUL)
+        cp(a("jw", 0, 16), a("jv"))
+        tt(a("jw", 16, 32), a("jv"), a("jw", 0, 16), SUB)
+        if t == 0:
+            consts_e()
+        if t < 2:
+            for h in range(2):
+                k = 128 * (2 * par + h)
+                mm(a("b3", 160 + h, 192, 2), a("HX", k, k + 128), a("jv"), True, True)
+
+        def jv_rows():
+            rows("b2", a("jw", 0, 16), 16, 256, a("jw", 16, 32))
+
+        if t == 2:
+            jv_rows()
+        if t == 1:
+            kmax_key("b5", "C0", 1)
+            kmax_pe("b5", 2)
+        level_scan(1)
+        if t == 0:
+            ts(a("jw", 32, 48), a("jv"), 1.0, MIN)
+            rows("b2", a("jw", 32, 48), 16, 256)
+            act(a("sg"), a("b2", 256, 512))
+        if t < 2:
+            if t == 0:
+                cp(a("oX"), a("b3", 160, 192))
+            else:
+                tt(a("oX"), a("oX"), a("b3", 160, 192), ADD)
+            cp(u(14), a("oX"))
+            act(a("gr"), ind(a("T01", 0, 513), u(14)))
+            tt(f(30), a("oX"), a("c15m"), ADD)
+            tt(i(13), a("gl%d" % (t + 1)), a("hs%d" % t), ADD)
+            ts(i(14), i(13), 15, AND)
+            cp(a("rowh", 32, 64), i(14))
+        level_scan(2)
+        level_scan(3)
+        mm(a("b6", 256, 512), a("ID"), a(zt, 0, 256), True, False)
+        mm(a("b6", 256, 512), a("ID"), a("sc", 15, 4096, 16), False, True)
+        if t == 1:
+            kmax_key("b5", "C0", 2)
+            kmax_pe("b5", 3)
+        act(a("zf"), a("b6", 256, 512), 0.5, -0.25)
+        act(a("zf"), a("zf"), 1.0, 12582912.0)
+        act(a("zs"), a("zf"), 1.0, -12582912.0)
+        send((rank + 1 + t) % N, "zs", "z%d" % (t + 1), 256, "az%d" % t, "lz%d" % t)
+
+        def lists(t=t, med=med):
+            tt(a("lv", 1024, 1280), a("b2", 256, 512), a("mk", 256 * (t & 1), 256 * (t & 1) + 256), MUL)
+            tt(med("LSp"), med("LSp"), a("lv", 1024, 1280), ADD)
+            if t == 0:
+                tt(a("nrow", 0, 512, 2), a("nrow", 0, 512, 2), a("sg"), ADD)
+
+        def limits():
+            emit("V", a("sB", 160, 161), [a("b3", 128, 144)], lambda e: e.tensor_reduce(a("sB", 160, 161)[0], a("b3", 128, 144)[0], axis=AxisListType.X, op=ADD))
+            cp(a("kwI", 0, 1), a("sB", 160, 161))
+            ts(a("kwI", 1, 2), a("kwI", 0, 1), 31, AND)
+            cp(a("sB", 161, 162), a("kwI", 1, 2))
+            ts(a("thT"), a("thB"), a("sB", 161, 162), ADD, 4080.0, MIN)
+            ts(a("thK"), a("thT"), 4096.0, MUL, 4095.0, ADD)
+
+        if t < 2:
+            conv(a("b3", 192, 224), "En1" if t == 0 else "En0", every("gr", 0, 512))
+            iota(a("WK", 512), [[0, 4096]], 0, 0)
+        tt(i(13), f(25), a("hl%d" % t), ADD)
+        ts(i(14), i(13), 15, AND)
+        cp(a("rowh", 0, 32), i(14))
+        rows("b4", a("rowh", 0, 32), 32)
+        if t == 0:
+            tt(a("T01", 1, 513, 2), a("T01", 1, 513, 2), a("sg"), ADD)
+            gather_n("S", 0)
+        elif t == 1:
+            kmax_key("b5", "C0", 3)
+            later[1] = kmax_fin("b1", 224, "km2")
+        if t < 2:
+            tt(f(31), f(30), a("b3", 192, 224), ADD)
+            later[1]()
+            act(a("drow", 0, 512), a("b4"))
+            cp(a("dA"), i(14))
+            trial_tables()
+            later[0], later[2], later[3] = limits, jv_rows, lists
+        else:
+            lists()
+            ts(a("ky"), a("LSp", 0, 512), -1.0, ADD)
+            dma("D", T.yl[:, :], a("ky")[0], [(("ky", 0, 512), False)])
+            act(a("kyT"), a("b4"))
+            dma("D", T.yd[:, :], T.kyT[0:128:16, :], [(("kyT", 0, 512), False)])
+            dma("D", T.yz[:, :], T.z3[:, :], [(("z3", 0, 256), False)])
+    for s, v in total.items():
+        g.wait_ge(T.sem[s], v)

@@ -1,51 +1,20 @@
 from concourse.mybir import AluOpType, ActivationFunctionType, AxisListType
 
 F, B, H, I, U = "float32", "bfloat16", "float16", "int32", "uint16"
-SB = {
-    "X": (512, F), "gx": (128, F), "mA": (32, F), "ci": (16, I), "cf": (16, F), "cc": (32, F),
-    "BD": (128, B), "BDh": (128, H), "BDdp": (128, B), "BDdn": (128, B), "BDo": (128, H), "BDo2": (128, B), "BDt": (128, B),
-    "ID": (128, B), "TRI": (128, B), "ones": (2048, B), "Tlo": (128, B), "x32": (512, B), "rI": (32, I), "offR": (32, U), "FH": (2048, B),
-    "E64": (144, B), "Er0": (144, B), "En0": (144, B), "En1": (144, B), "En2": (144, B), "Es": (144, B), "Ek": (144, B), "Eo": (144, B),
-    "E1": (144, B), "Eth": (144, B), "Eh": (144, H),
-    "TA": (1024, H), "HX": (512, H), "mask": (1024, B), "tie": (256, B), "Mrow": (512, F), "x21": (512, F), "x613": (512, F),
-    "m21": (32, F), "m37": (32, F), "m613": (32, F), "mneg": (32, F), "cB": (16, F),
-    "glI": (512, I), "LSp": (528, F), "offN": (512, U), "onb": (512, B), "C": (512, F), "C0": (512, F), "C1": (512, F), "GN": (8192, B), "T01": (528, B),
-    "nrow": (512, B), "ky": (512, F), "kyT": (512, F), "ks": (512, F), "kp": (512, F), "kI": (32, I), "khI": (32, I), "khH": (32, H), "klI": (32, I), "klH": (32, H),
-    "km0": (32, F), "km1": (32, F), "km2": (32, F), "c15m": (32, F),
-    "W": (4112, B), "nbI": (512, I), "vr0": (512, I), "vrh": (512, H), "thr": (256, I), "thI": (512, I), "thb": (512, B), "thB": (16, F), "thK": (16, F), "thT": (16, F),
-    "z0": (272, B), "z1": (272, B), "z2": (272, B), "z3": (256, B), "drow": (1024, B),
-    "dA": (32, F), "p4": (128, F), "pI": (256, I), "low": (128, B),
-    "gs0": (32, B), "gs1": (32, B), "gs2": (32, B), "gl0": (32, B), "gl1": (32, B), "gl2": (32, B),
-    "hs0": (32, B), "hs1": (32, B), "hs2": (32, B), "hl0": (32, B), "hl1": (32, B), "hl2": (32, B),
-    "sI": (512, I), "sF": (1024, F), "sU": (512, U), "eq": (512, B), "Zq": (512, B), "gr": (512, B), "gr2": (512, B), "prod": (512, H),
-    "G4": (2048, B), "D2": (1024, B), "tA": (64, F), "rowh": (64, B), "dlt": (512, B), "WK": (4608, B),
-    "GA": (4608, B), "GL": (4096, B), "sc": (4096, B), "offL": (256, U), "offM": (256, U), "zs": (256, B), "zf": (256, F), "lv": (1280, F), "lvI": (512, I),
-    "on16": (256, F), "hiT": (512, B), "yv": (512, B), "tk": (512, F), "kwI": (32, I), "wr": (256, B), "eqo": (256, B), "sg": (256, B),
-    "sB": (256, F), "sBb": (64, B), "full": (16, B), "mk": (512, B), "jv": (16, H), "jw": (48, B), "oX": (32, F), "lt": (2048, B), "rt": (512, B),
-}
-ALIAS = {}
-
-
-def share(to, names):
-    at = 0
-    for n in names:
-        ALIAS[n] = (to, at)
-        at += SB[n][0]
-    return at
-
-
-SCRATCH = {}
-for _to, _ns in (("aI", ("vr0", "nbI", "thr", "thI")), ("aB", ("onb", "thb")), ("aF", ("ks", "kp")),
-                 ("sm", ("m21", "m37", "m613", "mneg", "c15m", "km0", "km1", "km2", "oX", "dA", "tA", "cB", "thB", "thK", "thT")),
-                 ("smI", ("kI", "khI", "klI", "rI", "kwI")),
-                 ("EE", ("E64", "Er0", "En0", "En1", "En2", "Es", "Ek", "Eo", "E1", "Eth"))):
-    SCRATCH[_to] = ("sbuf", [128, share(_to, _ns)], SB[_ns[0]][1])
-for _n in SB:
-    if _n not in ALIAS:
-        SCRATCH[_n] = ("sbuf", [128, SB[_n][0]], SB[_n][1])
-for _b in range(8):
-    SCRATCH["b%d" % _b] = ("psum", [128, 512], F)
+POOL = {F: 12288, B: 65536, H: 5120, I: 8192, U: 3072}
+OWN = {"valI": (32, I), "gI0": (32, I), "z0": (272, B), "z1": (272, B), "z2": (272, B), "z3": (272, B)}
+for _t in range(3):
+    for _n in ("gs", "gl", "hs", "hl"):
+        OWN[_n + str(_t)] = (32, B)
+    OWN["zs%d" % _t] = (256, B)
+SCRATCH = {"p" + _d: ("sbuf", [128, _c], _d) for _d, _c in POOL.items()}
+SCRATCH.update({_n: ("sbuf", [128, _c], _d) for _n, (_c, _d) in OWN.items()})
+BANKS = ["b%d" % _b for _b in range(8)]
+SCRATCH.update({_b: ("psum", [128, 512], F) for _b in BANKS})
 SEMAPHORES = ["sV", "sS", "sP", "sG"] + ["d%d" % i for i in range(12)] + [a + str(t) for a in ("az", "ah", "ag", "lz", "lh", "lg") for t in range(3)]
+
+GATHER, SCATTER, LEAST, WAIT, REMOTE, FIRST, DMA0, DMABYTES = 1.56, 3.8, 64, 100, 2400, 2400, 2000, 160.0
+PLAN = {}
 
 
 def rank_program(g, core, T, topo):
@@ -55,24 +24,558 @@ def rank_program(g, core, T, topo):
     N = len(T.cores)
     OP, AF = AluOpType, ActivationFunctionType
     ADD, SUB, MUL, MAX, MIN = OP.add, OP.subtract, OP.mult, OP.max, OP.min
-    GT, GE, LT, LE, EQ = OP.is_gt, OP.is_ge, OP.is_lt, OP.is_le, OP.is_equal
+    GT, GE, LT, EQ = OP.is_gt, OP.is_ge, OP.is_lt, OP.is_equal
     SHR, AND = OP.arith_shift_right, OP.bitwise_and
     eng = {"V": g.vector, "S": g.scalar, "P": g.tensor, "G": g, "D": g.sync}
+    up, dn = (rank + 1) % N, (rank - 1) % N
+
+    tiles, top = {}, {d: 0 for d in POOL}
+    for n, (c, d) in OWN.items():
+        tiles[n] = (n, 0, c, d)
+    for n in BANKS:
+        tiles[n] = (n, 0, 512, F)
+
+    def new(n, c, d):
+        tiles[n] = ("p" + d, top[d], c, d)
+        top[d] += -(-c // 16) * 16
+        assert top[d] <= POOL[d], (d, top)
+        return a(n)
+
+    def a(n, lo=0, hi=None, st=1):
+        b, o, c, d = tiles[n]
+        hi = c if hi is None else min(hi, c)
+        ap = T[b][:, o + lo:o + hi:st] if st > 1 else T[b][:, o + lo:o + hi]
+        return (ap, [(b, o + lo, o + hi)], len(range(lo, hi, st)), d, "P" if b in BANKS else "S")
+
+    def ind(w, o):
+        return (w[0].indirect(o[0]), w[1] + o[1], 16 * o[2], w[3], "I")
+
+    def x(v):
+        return v if v is None or isinstance(v, (int, float)) else v[0]
+
+    steps = []
+
+    def spans(o, ins):
+        r = [(s, False) for v in ins if v is not None and not isinstance(v, (int, float)) for s in v[1]]
+        if o[4] == "I":
+            return r + [(o[1][0], True), (o[1][1], False)]
+        return r + [(o[1][0], True)]
+
+    def step(alts, acc, late=0, kind=None):
+        steps.append({"alts": alts, "acc": acc, "late": late, "kind": kind})
+
+    def vcost(o, ins, two=False):
+        full = [v for v in ins if v is not None and not isinstance(v, (int, float)) and v[2] > 1]
+        if o[4] == "I":
+            return 60 + SCATTER * o[2]
+        if any(v[4] == "I" for v in full):
+            return 60 + GATHER * o[2]
+        if two:
+            return max(LEAST, o[2] * (2 if all(v[4] == "S" for v in full) else 1))
+        return max(LEAST, o[2] * (0.5 if all(v[3] in (B, H, U) for v in full + [o]) else 1))
+
+    def vec(o, ins, call, two=False):
+        acc = spans(o, ins)
+        step({"V": (vcost(o, ins, two), [(acc, call)])}, acc)
+
+    def ts(o, i, s1, op0, s2=None, op1=None):
+        if op1 is None:
+            vec(o, [i, s1], lambda e: e.tensor_scalar(o[0], i[0], x(s1), None, op0))
+        else:
+            vec(o, [i, s1, s2], lambda e: e.tensor_scalar(o[0], i[0], x(s1), x(s2), op0, op1))
+        return o
+
+    def tt(o, i, j, op):
+        vec(o, [i, j], lambda e: e.tensor_tensor(o[0], i[0], j[0], op), True)
+        return o
+
+    def cp(o, i):
+        vec(o, [i], lambda e: e.tensor_copy(o[0], i[0]))
+        return o
+
+    def fill(o, c):
+        vec(o, [], lambda e: e.memset(o[0], c))
+        return o
+
+    def scan(o, d0, d1, op0, op1):
+        vec(o, [d0, d1], lambda e: e.tensor_tensor_scan(o[0], d0[0], d1[0], 0.0, op0, op1))
+        return o
+
+    def aff(o, i, scale=1.0, bias=0.0, on="VS", f=None):
+        acc, alts = spans(o, [i, scale, bias]), {}
+        plain = scale == 1.0 and bias == 0.0
+        if "V" in on and f is None:
+            if plain:
+                alts["V"] = (vcost(o, [i]), [(acc, lambda e: e.tensor_copy(o[0], i[0]))])
+            else:
+                alts["V"] = (vcost(o, [i]), [(acc, lambda e: e.tensor_scalar(o[0], i[0], x(scale), x(bias), MUL, ADD))])
+        if "S" in on:
+            fn = f if f is not None else AF.Copy if bias == 0.0 else AF.Identity
+            c = 80 + GATHER * o[2] if i[4] == "I" else max(LEAST, o[2])
+            alts["S"] = (c, [(acc, lambda e: e.activation(o[0], i[0], fn, bias=x(bias), scale=x(scale)))])
+        step(alts, acc)
+        return o
+
+    def mms(calls):
+        sub = [(spans(o, [l, r]), lambda e, o=o, l=l, r=r, s0=s0, s1=s1: e.matmul(o[0], l[0], r[0], s0, s1)) for o, l, r, s0, s1 in calls]
+        step({"P": (sum(max(64, c[2][2]) for c in calls), sub)}, [s for u in sub for s in u[0]], late=60)
+
+    def mm(o, l, r, start=True, stop=True):
+        mms([(o, l, r, start, stop)])
+
+    def iota(o, pat, base=0, cm=0):
+        acc = spans(o, [])
+        step({"G": (160 + 2 * o[2], [(acc, lambda e: e.iota(o[0], pat, base, cm, allow_small_or_imprecise_dtypes=True))])}, acc)
+        return o
+
+    def dma(q, out, in_, acc, size):
+        step({q: (60, [(acc, lambda e: e.dma_start(out, in_))])}, acc, late=size / DMABYTES, kind="dma")
+
+    def send(dst, buf, rbuf, arr, loc, src):
+        step({"G": (400, [(buf, rbuf, arr, loc, dst, src)])}, [(buf[1][0], False), (rbuf[1][0], True)], late=REMOTE + buf[2], kind="send")
+
+    def es(E, q):
+        return a(E, 15 - q, 143 - q)
+
+    def conv(o, E, src, first=True, last=True, pre=()):
+        mms(list(pre) + [(o, es(E, q), src(q), first and q == 0, last and q == 15) for q in range(16)])
+
+    def every(n, lo, hi):
+        return lambda q: a(n, lo + q, hi, 16)
+
+    def rows(bank, src, alone):
+        mms([(a(bank, 32 * q, 32 * q + 32), a("FH", 128 * q, 128 * q + 128), src, alone, alone or q == 15) for q in range(16)])
+
+    def col(n, k=0):
+        return a(n, k, k + 1)
+
+    def load(q, v, src):
+        dma(q, v[0], src, [(v[1][0], True)], 128 * v[2] * (4 if v[3] == I else 2))
+
+    load("S", a("valI"), T.val[:, :])
+    load("D", new("glI", 512, I), T.gl[:, :])
+    load("D", new("nbI", 512, I), T.nb[:, :])
+    load("D", a("z0", 16), T.zl[:, :])
+    load("D", new("thI", 16, I), T.th[:, :])
+    new("W", 4112, B)
+    load("D", a("W", 16), T.rec[:, :])
+    send(dn, a("valI"), a("gI0"), "ag0", "lg0", up)
+
+    new("ci", 16, I)
+    iota(col("ci"), [[0, 1]], 0, 1)
+    iota(new("X", 256, F), [[1, 256]])
+    for n, (op, c) in enumerate(((AND, 15), (AND, 112), (SHR, 4), (AND, 7), (AND, 8))):
+        ts(col("ci", n + 1), col("ci"), c, op)
+    new("cf", 16, F)
+    cp(a("cf", 0, 6), a("ci", 0, 6))
+    pf, r, g16, gg, r7, r8 = [col("cf", k) for k in range(6)]
+    new("cc", 32, F)
+    used = [0]
+
+    def cc(i, scale, bias=0.0):
+        used[0] += 1
+        return aff(col("cc", used[0]), i, scale, bias)
+
+    ts(new("I16", 16, F), a("X", 0, 16), r, EQ)
+
+    def isr(q):
+        return col("I16", q)
+
+    ts(new("E1", 144, B), a("X", 0, 144), cc(g16, 1.0, 15.0), EQ)
+    for q in range(16):
+        if q == 0:
+            new("FH", 2048, B)
+        aff(a("FH", 128 * q, 128 * q + 128), es("E1", 2), isr(q))
+    ts(new("ID", 128, B), a("X", 0, 128), pf, EQ)
+    s01 = cc(isr(0), 1.0, isr(1))
+    new("Kc", 512, B)
+    aff(a("Kc", 0, 512, 2), a("X"), isr(1), s01)
+    aff(a("Kc", 1, 512, 2), a("Kc", 0, 512, 2), -1.0)
+    aff(new("Ekey", 144, B), a("E1"), cc(isr(0), 16384.0, isr(1)))
+    aff(new("Ed", 144, B), a("E1"), isr(2))
+    for t in range(3):
+        new("TB%d" % t, 1040, B)
+        aff(col("TB%d" % t), isr(2), -128.0)
+        fill(a("z%d" % t, 0, 16), 0.0)
+
+    new("onS", 512, B)
+    for par in range(2):
+        gp = a("glI", par, 512, 2)
+        ts(a("onS", par, 512, 2), gp, 0.0, GE, 1.0 - 2 * par, MUL)
+        ts(new("off%d" % par, 256, U), gp, 1.0, ADD)
+        new("LS%d" % par, 272, F)
+        fill(a("LS%d" % par, 0, 16), 0.0)
+        ts(a("LS%d" % par, 16), gp, 1.0, ADD)
+    cp(new("d0", 32, B), a("valI"))
+
+    def table(t):
+        mms([(a("b0"), es("E1", 0), a("onS"), True, False), (a("b0"), a("ID"), a("Kc"), False, False)])
+        rows("b0", a("d%d" % t), False)
+        aff(a("TB%d" % t, 1, 513), a("b0"))
+
+    def ghosts(t, src):
+        rows("b0", src, True)
+        aff(a("TB%d" % t, 513, 1025), a("b0"))
+
+    def members(t, par, keys, values):
+        n = "GN%d" % par
+        for ch in range(8):
+            aff(a(n, 512 * ch, 512 * ch + 512), ind(a("TB%d" % t, 0, 513), a("off%d" % par, 32 * ch, 32 * ch + 32)))
+            if keys:
+                mms([(a("b2", 256 * par, 256 * par + 256), es("Ekey", q), a(n, 256 * q, 256 * q + 256), q == 0, q == 15) for q in (2 * ch, 2 * ch + 1)])
+            if values and ch % 2:
+                conv(a("b3", 32 * ch - 32, 32 * ch + 32), "Ed", every(n, 512 * ch - 512, 512 * ch + 512))
+
+    def elect(t, par):
+        s = scan(new("ks%d%d" % (t, par), 256, F), a("subp" if t & 1 else "addp"), a("b2", 256 * par, 256 * par + 256), ADD, MIN if t & 1 else MAX)
+        ts(a("key%d" % t, par, 32, 2), a("ks%d%d" % (t, par), 15, 256, 16), -1.0 if t & 1 else 1.0, MUL, 0.0, MAX)
+        return s
+
+    for n, c in (("GN0", 4096), ("GN1", 4096), ("G4", 2048), ("GL", 4608), ("sc", 4096)):
+        for t in ("", "0", "1", "2") if n[1] != "N" else ("",):
+            tiles[n + t] = tiles[n] if t else new(n, c, B) and tiles[n]
+    table(0)
+    iota(new("kpat", 1024, B), [[0, 64], [1, 16]])
+    ts(new("mask", 1024, B), a("kpat"), 1.0, MIN)
+    aff(new("addp", 256, F), a("mask", 0, 256), 4194304.0 + 1024.0, -4194304.0)
+    aff(new("subp", 256, F), a("addp"), -1.0)
+    for t in range(3):
+        new("key%d" % t, 32, I)
+    members(0, 0, True, False)
+    members(0, 1, True, False)
+    for t in range(2):
+        for par in range(2):
+            elect(t, par)
+    for ch in range(4):
+        conv(a("b3", 64 * ch, 64 * ch + 64), "Ed", every("GN0", 1024 * ch, 1024 * ch + 1024))
+
+    ts(new("mA", 32, F), a("X", 0, 32), cc(r, 32.0), ADD)
+    for n, c in (("m17", 17.0), ("m37", 37.0), ("m613", 613.0)):
+        aff(new(n, 32, F), a("mA"), 2.0, c)
+    for par in range(2):
+        aff(new("x17%d" % par, 256, F), a("X"), 4.0, 17.0 + 2 * par)
+        aff(new("x613%d" % par, 256, F), a("X"), 4.0, 613.0 + 2 * par)
+    iota(new("Mrow", 512, F), [[1, 32], [32, 16]], 1)
+    iota(new("gx", 256, F), [[0, 2], [1, 8], [0, 16]])
+    iota(new("x8", 256, B), [[0, 32], [1, 8]])
+    iota(new("x32", 512, B), [[0, 16], [1, 32]])
+    iota(new("j16", 128, B), [[16, 4], [0, 32]])
+    new("pt", 64, F)
+    iota(a("pt", 0, 32), [[1, 16], [0, 2]])
+    iota(a("pt", 32, 48), [[16, 2], [0, 8]])
+    iota(a("pt", 48, 64), [[16, 2], [1, 8]])
+    for ch in range(4):
+        if ch == 0:
+            new("WK0", 4608, B)
+        iota(a("WK0", 512 + 1024 * ch, 1536 + 1024 * ch), [[0, 1024]])
+    for t in (1, 2):
+        o = new("WK%d" % t, 4608, B)
+        dma("D", a("WK%d" % t, 512)[0], a("WK0", 512)[0], [(a("WK0", 512)[1][0], False), (o[1][0], True)], 128 * 8192)
+    cp(new("o16", 16, U), a("X", 0, 16))
+    cp(new("o32", 32, U), a("pt", 0, 32))
+    ts(new("oML", 16, U), a("pt", 32, 48), r, ADD)
+    ts(new("oMT", 16, U), a("pt", 48, 64), r8, ADD)
+    ts(new("oH", 2, U), a("X", 0, 32, 16), cc(g16, 2.0, r), ADD)
+    aff(new("E64", 144, B), a("E1"), 64.0)
+    aff(new("Es", 144, B), a("E1"), cc(r, 1.0, 1.0))
+    aff(new("E0", 144, B), a("E1"), isr(0))
+    cp(new("Eh", 144, H), a("E1"))
+    new("E2", 144, B)
+    tt(a("E2", 8, 144), a("E1", 8, 144), a("E1", 7, 143), ADD)
+    new("E2n", 144, B)
+    aff(a("E2n", 8), a("E2", 8), -1.0)
+    new("E2h", 144, H)
+    cp(a("E2h", 8), a("E2", 8))
+    aff(new("w1", 128, B), es("E2", 2), 49152.0)
+    aff(new("w2", 128, B), es("E1", 4), cc(r, -1.0, 15.0))
+    tt(new("w3", 128, B), a("w1"), a("w2"), ADD)
+    tt(new("Weq", 128, B), a("w3"), es("E1", 6), ADD)
+    ts(new("Bro2", 128, B), a("gx", 0, 128), gg, EQ, isr(2), MUL)
+    cp(new("IDh", 128, H), a("ID"))
+    ts(new("tri", 128, B), a("X", 0, 128), pf, GT)
+    aff(new("id64", 128, B), a("ID"), -64.0)
+    tt(new("TRI", 128, B), a("tri"), a("id64"), ADD)
+    fill(new("ones", 128, B), 1.0)
+    fill(new("cm", 16, B), -1024.0)
+    fill(new("half", 256, B), -0.5)
+    fill(a("W", 0, 16), 0.0)
+    ts(new("G8", 8, B), a("X", 0, 8), gg, EQ)
+    aff(new("G8n", 8, B), a("G8"), -1.0)
+    w = cc(isr(4), 256.0, cc(s01, 4096.0))
+    new("WAB", 16, B)
+    aff(a("WAB", 0, 16, 2), a("G8"), cc(isr(2), 0.125, cc(isr(5), 1.0, cc(isr(6), -6144.0, w))))
+    aff(a("WAB", 1, 16, 2), a("G8"), cc(isr(3), 1.0, cc(isr(6), 127.0, w)))
+    odd = cc(isr(1), 1.0, isr(3))
+    ts(new("MK1", 256, B), a("gx"), r7, EQ)
+    ts(new("MK2", 256, B), a("x8"), gg, EQ)
+    ts(new("R1", 16, F), a("X", 0, 16), cc(r8, 1.0, gg), EQ)
+    aff(new("R1a", 16, B), a("R1"), 262144.0)
+    aff(new("R1b", 16, B), a("R1"), 4096.0)
+    ts(new("R2a", 16, H), a("I16"), 1024.0, MUL)
+    ts(new("R2b", 16, H), a("I16"), 0.5, MUL)
+    aff(new("xQ", 256, B), a("kpat", 0, 256), 8.0, 128.0)
+    ts(new("nbh", 512, H), a("nbI"), 2.0, MUL, -127.0, ADD)
+    mms([(a("b1", q, 512, 16), a("IDh"), a("nbh", 32 * q, 32 * q + 32), True, True) for q in range(16)])
+    new("th2", 32, I)
+    ts(a("th2", 0, 16), a("thI"), 6, SHR)
+    ts(a("th2", 16, 32), a("thI"), 63, AND)
+    tt(new("thx", 256, B), ind(a("th2"), a("oML")), a("MK1"), MUL)
+    mms([(a("b5", 0, 16), a("thx", 0, 128), a("R1a"), True, False), (a("b5", 0, 16), a("thx", 128, 256), a("R1b"), False, True)])
+    aff(new("thK0", 16, F), a("b5", 0, 16), 1.0, 4095.0)
+    ghosts(0, cp(new("gb0", 32, B), a("gI0")))
+
+    for t in range(3):
+        par, s = t & 1, str(t)
+        LS, TB, zt, d, key = "LS%d" % par, "TB" + s, "z" + s, a("d" + s), a("key" + s)
+
+        def n32(n, dt=F, c=32):
+            if t == 2 and c >= 128:
+                tiles[n + s] = tiles[n + "0"]
+                return a(n + s)
+            return new(n + s, c, dt)
+
+        def h(n, lo=0, hi=None, st=1):
+            return a(n + s, lo, hi, st)
+
+        cp(n32("LSh", H, 256), a(LS, 16))
+        mms([(a("b7", 256 + 128 * k, 384 + 128 * k), h("LSh", 128 * k, 128 * k + 128), a("IDh"), True, True) for k in range(2)])
+        aff(n32("LMT", F, 256), a("b7", 256, 512))
+        mms([(a("b5", 16 + 8 * k, 24 + 8 * k), a("onS", par + 256 * k, 256 * k + 256, 2), a("G8n" if par else "G8"), True, True) for k in range(2)])
+        aff(n32("nMT", F, 16), a("b5", 16, 32))
+        tt(n32("mkT", B, 256), ind(h("nMT"), a("o16")), a("kpat", 0, 256), EQ)
+        ts(n32("room", F, 16), h("nMT"), 15.5, LT)
+        aff(n32("c15", F, 16), h("nMT"), -1.0, 15.0)
+        i1 = ts(n32("i1", I), key, 1023, AND)
+        uE = ts(n32("uE", U), i1, 2.0, MUL, par - 1.0, ADD)
+        uZ = ts(n32("uZ", U), i1, 15.0, ADD)
+        aff(n32("gr", B, 512), ind(a(TB, 0, 513), uE))
+        conv(a("b6", 0, 32), "Ed", every("gr" + s, 0, 512))
+        Zq = aff(n32("Zq", B, 512), ind(a(zt), uZ))
+        eq = tt(n32("eq", B, 512), ind(a(LS), uZ), a("Mrow"), EQ)
+        prod = tt(n32("prod", H, 512), a("b1"), eq, MUL)
+        conv(a("b7", 64, 96), "Eh", every("prod" + s, 0, 512))
+        conv(a("b7", 96, 128), "Es", every("eq" + s, 0, 512))
+        mms([(a("b4"), a("Weq"), eq, True, False), (a("b4"), es("E2h", 2), prod, False, False)])
+        f17 = ts(n32("f17"), i1, 4.0, MUL, 13.0 + 2 * par, ADD)
+        c1 = aff(n32("c1"), f17, 1.0, 596.0)
+        base = ts(n32("base", I), tt(n32("b0_", I), f17, a("mA"), MUL), 4, SHR)
+        n32("pI", I, 256)
+        n32("t4", F, 128)
+        for j in range(4):
+            ts(h("pI", 32 * j, 32 * j + 32), d, float(j), ADD)
+        ts(h("pI", 128, 256), h("pI", 0, 128), 15, AND)
+        cp(n32("p4", B, 128), h("pI", 128, 256))
+        for j in range(4):
+            tt(h("t4", 32 * j, 32 * j + 32), h("pI", 128 + 32 * j, 160 + 32 * j), c1, MUL)
+        X2 = tt(n32("X2"), tt(n32("X1"), a("b6", 0, 32), a("m37"), MUL), base, ADD)
+        n32("P4", I, 256)
+        for j in range(4):
+            tt(h("P4", 32 * j, 32 * j + 32), h("t4", 32 * j, 32 * j + 32), X2, ADD)
+        ts(h("P4", 128, 256), h("P4", 0, 128), 4095, AND)
+        ts(n32("u4", U, 128), h("P4", 128, 256), 16.0, ADD)
+        uO = ts(n32("uO", U), a("b7", 64, 96), 0.5, MUL, 64.5, ADD)
+        fo = aff(n32("fo"), a("b7", 64, 96), 0.5, 63.5)
+        f20 = aff(n32("f20"), fo, 2.0, 37.0)
+        flag = ts(n32("flag"), a("b7", 96, 128), 1.0, MIN)
+        pos = tt(n32("pos0"), a("b7", 96, 128), aff(n32("f16i"), f17, 4.0, 443.0 - 8 * par), ADD)
+        pos = tt(n32("pos2"), tt(n32("pos1"), pos, flag, MUL), a("mA"), MAX)
+        uP = cp(n32("uP", U), pos)
+        gr2 = aff(n32("gr2", B, 512), ind(a(TB, 0, 1025), uO), on="S", f=AF.Abs)
+        conv(a("b6", 32, 64), "Ed", every("gr2" + s, 0, 512))
+        mm(a("b4"), es("E0", 5), gr2, False, False)
+        for k, bank in enumerate(("b6", "b7")):
+            for j in (2 * k, 2 * k + 1):
+                tt(h("G4", 512 * j, 512 * j + 512), ind(a("W"), h("u4", 32 * j, 32 * j + 32)), Zq, MAX)
+            o = a(bank, 128, 192)
+            conv(o, "E64", every("G4" + s, 1024 * k, 1024 * k + 1024), False, True,
+                 [(o, a("ID"), h("p4", 64 * k, 64 * k + 64), True, False), (o, a("ID"), a("j16", 64 * k, 64 * k + 64), False, False)])
+            if k == 0:
+                aff(n32("tA", F, 64), o)
+        i5 = ts(n32("i5", I), tt(n32("i5a", I), fo, a("m17"), MUL), 4, SHR)
+        f19 = tt(n32("f19"), tt(n32("f21"), a("b6", 32, 64), a("m613"), MUL), i5, ADD)
+
+        def place(n, p, c, rest):
+            v = tt(n32(n + "b", I), tt(n32(n + "a"), p, c, MUL), rest, ADD)
+            return ts(n32(n, U), ts(n32(n + "c", I), v, 4095, AND), 16.0, ADD)
+
+        Do = tt(n32("Do", B, 512), ind(a("W"), place("uo", d, f20, f19)), Zq, MAX)
+        mm(a("b4"), es("E2n", 0), Do, False, False)
+        tt(n32("tk", F, 64), h("tA"), a("b7", 128, 192), MIN)
+        pn = ts(n32("pn", I), tt(n32("kI", I), h("tk", 0, 32), h("tk", 32, 64), MIN), 15, AND)
+        Dn = tt(n32("Dn", B, 512), ind(a("W"), place("un", pn, f20, f19)), Zq, MAX)
+        mm(a("b4"), es("E2", 0), Dn, False, True)
+        aff(n32("hiT", B, 512), a("b4"), odd, on="S")
+        yv = tt(n32("yv", B, 512), a("b4"), h("hiT"), SUB)
+        cp(ind(a("WK" + s), uP), yv)
+        for k in range(2):
+            mms([(a("b5", 256 * k + q, 256 * k + 256, 16), a("WK" + s, 512 + 2048 * k + q, 2560 + 2048 * k, 16), a("WAB"), True, True) for q in range(16)])
+        pk = aff(n32("pk", B, 512), ind(a("W"), place("up", pn, c1, X2)))
+        dm = tt(h("gs"), tt(n32("dm1"), tt(n32("dm0"), pn, d, SUB), flag, MUL), d, ADD)
+        if t < 2:
+            send(dn, dm, h("gl"), "ag%d" % (t + 1), "lg%d" % (t + 1), up)
+        if t:
+            members(t, par, t == 1, True)
+        if t == 1:
+            members(1, 0, True, False)
+            for p2 in range(2):
+                elect(2, p2)
+        mm(a("b3", 256, 512), a("Bro2"), a(TB, 1 + par, 513, 2))
+        aff(n32("am", F, 256), a(LS, 16), 1.0, -1.0)
+        aff(n32("a37", F, 256), a(LS, 16), 2.0, 35.0)
+        n32("lI", I, 1024)
+        tt(h("lI", 0, 256), h("am"), a("x17%d" % par), MUL)
+        ts(h("lI", 256, 512), h("lI", 0, 256), 4, SHR)
+        tt(a("b3", 256, 512), a("b3", 256, 512), h("a37"), MUL)
+        tt(n32("s1", F, 256), a("b3", 256, 512), h("lI", 256, 512), ADD)
+        n32("offM", U, 256)
+        for k in range(2):
+            lo, hi = 128 * k, 128 * k + 128
+            tt(a("b3", lo, hi), a("b3", lo, hi), a("x613%d" % par, lo, hi), MUL)
+            tt(h("lI", 512 + lo, 512 + hi), a("b3", lo, hi), h("s1", lo, hi), ADD)
+            ts(h("lI", 768 + lo, 768 + hi), h("lI", 512 + lo, 512 + hi), -2147479553, AND)
+            ts(h("offM", lo, hi), h("lI", 768 + lo, 768 + hi), 16.0, ADD)
+            for ch in range(4 * k, 4 * k + 4):
+                aff(h("GL", 512 + 512 * ch, 1024 + 512 * ch), ind(a("W"), h("offM", 32 * ch, 32 * ch + 32)))
+        cp(ind(h("GL"), uP), pk)
+        for ch in range(4):
+            scan(h("sc", 1024 * ch, 1024 * ch + 1024), a("mask"), h("GL", 512 + 1024 * ch, 1536 + 1024 * ch), MUL, MAX)
+        o = a("b3", 0, 256)
+        mms([(o, a("ID"), a("half"), True, False), (o, a("ID"), a(zt, 16), False, False), (o, a("ID"), h("sc", 15, 4096, 16), False, True)])
+        aff(n32("zf", F, 256), o, 0.5, 12582912.0, on="S")
+        aff(h("zs"), h("zf"), 1.0, -12582912.0)
+        send((rank + 1 + t) % N, h("zs"), a("z%d" % (t + 1), 16), "az" + s, "lz" + s, (rank - 1 - t) % N)
+        n32("kw", F, 512)
+        for k in range(2):
+            scan(h("kw", 256 * k, 256 * k + 256), a("mask", 0, 256), a("b5", 256 * k, 256 * k + 256), MUL, MAX)
+        cp(n32("kAB", I), h("kw", 15, 512, 16))
+        kA, kB = h("kAB", 0, 32, 2), h("kAB", 1, 32, 2)
+        inj = tt(n32("inj", B, 16), h("kw", 15, 512, 32), a("thK" + s), GT)
+        t1 = ts(n32("t1", I, 16), kA, 224, AND)
+        cI = ts(n32("cI", I, 16), kB, 1, SHR, 31, AND)
+        t2 = ts(n32("t2", I, 16), kB, 3, SHR, 24, AND)
+        gh = tt(n32("gh", B, 16), ts(n32("g1", F, 16), t1, 128.0, GE), inj, MUL)
+        mms([(a("b6", 192, 208), a("TRI"), gh, True, False), (a("b6", 200, 208), a("ones"), h("gh", 0, 8), False, True)])
+        rt = tt(n32("rt", B, 512), ind(cI, a("o32")), a("x32"), EQ)
+        q8 = tt(n32("q8", F, 16), t1, t2, ADD)
+        q9 = tt(n32("q9", F, 16), ts(n32("nt", F, 16), a("b6", 192, 208), -4.5, GE, 1024.0, MUL), q8, ADD)
+        tt(n32("lt", B, 256), ind(q9, a("o16")), a("xQ"), EQ)
+        mms([(a("b5", 0, 256), h("lt", 128 * k, 128 * k + 128), h("rt", 256 * k, 256 * k + 256), k == 0, k == 1) for k in range(2)])
+        aff(n32("hx", B, 256), a("b5", 0, 256))
+        aff(h("hs"), ind(h("hx"), a("oH")))
+        send(up, h("hs"), h("hl"), "ah" + s, "lh" + s, dn)
+        lI = ts(n32("l7", I, 16), kB, 1, SHR, 127, AND)
+        o1 = tt(n32("o1", F, 16), ts(n32("o4", F, 16), t1, 4.0, MUL, 1.0, ADD), lI, ADD)
+        tt(n32("test", B, 256), ind(o1, a("o16")), h("LMT"), EQ)
+        scan(n32("inl", B, 256), a("mask", 0, 256), h("test"), MUL, MAX)
+        loc = tt(n32("loc1", F, 16), tt(n32("loc0", F, 16), inj, gh, SUB), h("room"), MUL)
+        jf = tt(n32("jf", F, 16), loc, h("inl", 15, 256, 16), GT)
+        if t < 2:
+            n32("jk", F, 32)
+            pb = ts(n32("pb", I, 16), kB, 1, SHR, 1, AND)
+            nn = ts(n32("nn", I, 16), kA, 31, AND)
+            hi0 = tt(n32("hi1", F, 16), ts(n32("hi0", F, 16), nn, 16.0, MUL, 1.0, ADD), h("c15"), ADD)
+            aff(h("jk", 16, 32), o1, 1.0, float(t))
+            tt(h("jk", 0, 16), tt(n32("jp", F, 16), jf, pb, GT if t else MUL), hi0, MUL)
+            tt(n32("jx", H, 256), ind(h("jk"), a("oMT")), a("MK2"), MUL)
+            o = a("b6", 224, 240)
+            mms([(o, a("ID"), a("cm"), True, False), (o, h("jx", 0, 128), a("R2a"), False, False), (o, h("jx", 128, 256), a("R2b"), False, True)])
+            k2 = a("key%d" % (t + 1), par, 32, 2)
+            tt(k2, o, k2, MAX)
+        tt(n32("dl", H, 256), ind(tt(n32("jv", F, 16), jf, o1, MUL), a("o16")), h("mkT"), MUL)
+        mms([(a("b7", 256 + 128 * k, 384 + 128 * k), h("dl", 128 * k, 128 * k + 128), a("IDh"), True, True) for k in range(2)])
+        if t == 0:
+            tt(a(LS, 16), a("b7", 256, 512), a(LS, 16), ADD)
+            ts(a("onS", 0, 512, 2), a(LS, 16), 1.0, MIN)
+            cp(a("off0"), a(LS, 16))
+            new("ky", 512, F)
+        else:
+            tt(a("ky", par, 512, 2), a("b7", 256, 512), h("am"), ADD)
+        if t < 2:
+            mm(a("b6", 208, 224), a("ones"), inj)
+            o, i_ = n32("c0", F, 16), a("b6", 208, 224)
+            vec(h("c0", 0, 1), [i_], lambda e, o=h("c0", 0, 1), i_=i_: e.tensor_reduce(o[0], i_[0], axis=AxisListType.X, op=ADD))
+            n32("cJ", I, 16)
+            cp(h("cJ", 0, 1), h("c0", 0, 1))
+            ts(h("cJ", 1, 2), h("cJ", 0, 1), 31, AND)
+            ts(h("c0", 1, 2), h("cJ", 1, 2), 4096.0, MUL)
+            aff(new("thK%d" % (t + 1), 16, F), a("thK0"), 1.0, h("c0", 1, 2))
+            v = ts(n32("gv1", I), tt(n32("gv0", I), h("gl"), h("hs"), ADD), 15, AND)
+            ghosts(t + 1, cp(n32("gv2", B), v))
+        v = ts(n32("dv1", I), tt(n32("dv0", I), dm, h("hl"), ADD), 15, AND)
+        if t < 2:
+            cp(new("d%d" % (t + 1), 32, B), v)
+            table(t + 1)
+        else:
+            o = cp(new("dF", 32, F), v)
+            dma("D", T.yl[:, :], a("ky")[0], [(a("ky")[1][0], False)], 128 * 2048)
+            dma("S", T.yd[:, :], o[0], [(o[1][0], False)], 128 * 128)
+            dma("D", T.yz[:, :], a("z3", 16)[0], [(a("z3", 16)[1][0], False)], 128 * 512)
+
+    if "order" not in PLAN:
+        PLAN["order"] = arrange(steps)
+    issue(g, core, T, topo, eng, steps, PLAN["order"])
+
+
+def arrange(steps):
+    hist, last, deps = {}, {}, []
+    for k, s in enumerate(steps):
+        d = set()
+        for (n, lo, hi), w in s["acc"]:
+            d.update(j for l2, h2, w2, j in hist.get(n, []) if lo < h2 and l2 < hi and (w or w2))
+            if n in BANKS and "P" in s["alts"] and n in last:
+                d.add(last[n])
+        for (n, lo, hi), w in s["acc"]:
+            hist[n] = [e for e in hist.get(n, []) if not (w and lo <= e[0] and e[1] <= hi)] + [(lo, hi, w, k)]
+            if n in BANKS and "P" in s["alts"]:
+                last[n] = k
+        d.discard(k)
+        deps.append(d)
+    seen = []
+    for k, s in enumerate(steps):
+        if s["kind"] == "dma":
+            s["late"] += DMA0
+        if s["kind"] == "send" and not seen:
+            seen.append(k)
+            s["late"] += FIRST
+    way = [0.0] * len(steps)
+    for k in reversed(range(len(steps))):
+        way[k] += min(c for c, _ in steps[k]["alts"].values()) + steps[k]["late"] + WAIT
+        for j in deps[k]:
+            way[j] = max(way[j], way[k])
+    busy, bank, at, end, free = {q: [] for q in "VSPGD"}, {b: [] for b in BANKS}, {}, {}, [0.0]
+    for k in sorted(range(len(steps)), key=lambda k: (-way[k], k)):
+        s, best = steps[k], None
+        bs = {n for (n, _, _), _ in s["acc"] if n in BANKS}
+        for q, (c, _) in s["alts"].items():
+            t = max([0.0] + [end[j] + (0 if at[j][1] == q == "P" else WAIT) - (steps[j]["late"] if at[j][1] == q == "P" else 0) for j in deps[k]])
+            taken = busy[q] + [(u - WAIT - s["late"], v + WAIT) for b in bs for u, v, q2 in bank[b] if q2 != q]
+            for u, v in sorted(taken):
+                if u < t + c and t < v:
+                    t = v
+            if best is None or t + c < best[0] + best[2]:
+                best = (t, q, c)
+        t, q, c = best
+        busy[q].append((t, t + c))
+        at[k], end[k] = (t, q), t + c + s["late"]
+        if s["kind"] == "dma":
+            end[k] = max(end[k], free[0] + s["late"] - DMA0)
+            free[0] = end[k]
+        for b in bs:
+            bank[b].append((t, end[k], q))
+    return [(k, at[k][1]) for k in sorted(at, key=lambda k: (at[k][0], k))]
+
+
+def issue(g, core, T, topo, eng, steps, plan):
     hist, known, total, nd = {}, {q: {} for q in "VSPGD"}, {}, [0]
-    banks = ["b%d" % k for k in range(8)]
 
     def order(q, acc):
         toks = []
         for (n, lo, hi), w in acc:
             for r in hist.get(n, []):
-                if n in banks and r[3] != q:
+                if n in BANKS and r[3] != q:
                     toks.append(r[4])
-                    continue
-                if not (lo < r[1] and r[0] < hi) or not (w or r[2]):
-                    continue
-                if r[3] == q == "P":
-                    continue
-                toks.append(r[4])
+                elif lo < r[1] and r[0] < hi and (w or r[2]) and not r[3] == q == "P":
+                    toks.append(r[4])
         toks.sort(key=lambda k: -len(k[2]))
         for i, (s, v, kn) in enumerate(toks):
             if known[q].get(s, 0) >= v:
@@ -80,632 +583,50 @@ def rank_program(g, core, T, topo):
             if any(j != i and (k[2].get(s, 0) >= v and (k[0] != s or k[1] > v)) for j, k in enumerate(toks)):
                 continue
             eng[q].wait_ge(T.sem[s], v)
-            for a, b in kn.items():
-                known[q][a] = max(known[q].get(a, 0), b)
+            for n, c in kn.items():
+                known[q][n] = max(known[q].get(n, 0), c)
             known[q][s] = max(known[q].get(s, 0), v)
 
     def note(q, acc, tok, dma=False):
         for (n, lo, hi), w in acc:
             keep = []
             for r in hist.get(n, []):
-                inside = lo <= r[0] and r[1] <= hi
-                ps = n in banks
+                inside, ps = lo <= r[0] and r[1] <= hi, n in BANKS
                 if inside and (w if not ps else (w or not r[2])) and not (ps and r[3] != q and not w):
                     continue
                 if inside and not w and not r[2] and r[3] == q and not dma:
                     continue
                 keep.append(r)
-            keep.append((lo, hi, w, "dma" if dma else q, tok))
-            hist[n] = keep
+            hist[n] = keep + [(lo, hi, w, "dma" if dma else q, tok)]
 
-    def emit(q, outs, ins, call):
-        acc = [(a, False) for v in ins if v is not None and not isinstance(v, (int, float)) for a in v[1]] + [(a, True) for a in outs[1]]
-        order(q, acc)
-        s = "s" + q
-        total[s] = total.get(s, 0) + 1
-        call(eng[q]).then_inc(T.sem[s], 1)
-        kn = dict(known[q])
-        kn[s] = total[s]
-        note(q, acc, (s, total[s], kn))
-
-    def a(n, lo=0, hi=None, st=1):
-        hi = SB[n][0] if hi is None and n in SB else 512 if hi is None else hi
-        if n in ALIAS:
-            o = ALIAS[n][1]
-            n, lo, hi = ALIAS[n][0], lo + o, hi + o
-        return (T[n][:, lo:hi:st] if st > 1 else T[n][:, lo:hi], [(n, lo, hi)])
-
-    def ind(w, o):
-        return (w[0].indirect(o[0]), w[1] + o[1])
-
-    def x(v):
-        return v if v is None or isinstance(v, (int, float)) else v[0]
-
-    def ts(o, i, s1, op0, s2=None, op1=None):
-        if op1 is None:
-            emit("V", o, [i, s1], lambda e: e.tensor_scalar(o[0], i[0], x(s1), None, op0))
-        else:
-            emit("V", o, [i, s1, s2], lambda e: e.tensor_scalar(o[0], i[0], x(s1), x(s2), op0, op1))
-
-    def tt(o, i, j, op):
-        emit("V", o, [i, j], lambda e: e.tensor_tensor(o[0], i[0], j[0], op))
-
-    def cp(o, i):
-        emit("V", o, [i], lambda e: e.tensor_copy(o[0], i[0]))
-
-    def fill(o, c):
-        emit("V", o, [], lambda e: e.memset(o[0], c))
-
-    def scan(o, d0, d1, init, op1):
-        emit("V", o, [d0, d1], lambda e: e.tensor_tensor_scan(o[0], d0[0], d1[0], init, MUL, op1))
-
-    def act(o, i, scale=1.0, bias=0.0, f=None):
-        f = (AF.Copy if bias == 0.0 else AF.Identity) if f is None else f
-        emit("S", o, [i, scale], lambda e: e.activation(o[0], i[0], f, bias=bias, scale=x(scale)))
-
-    def mm(o, l, r, start, stop):
-        emit("P", o, [l, r], lambda e: e.matmul(o[0], l[0], r[0], start, stop))
-
-    def iota(o, pat, base, cm):
-        emit("G", o, [], lambda e: e.iota(o[0], pat, base, cm, allow_small_or_imprecise_dtypes=True))
-
-    def keep(o, i, pat, op, base, cm, c=0.0):
-        emit("G", o, [i], lambda e: e.affine_select(o[0], i[0], pat, op, c, base, cm))
-
-    def dma(q, out, in_, acc):
-        order(q, acc)
-        s = "d%d" % nd[0]
-        nd[0] += 1
-        eng[q].dma_start(out, in_).then_inc(T.sem[s], 16)
-        total[s] = 16
-        kn = dict(known[q])
-        kn[s] = 16
-        note(q, acc, (s, 16, kn), True)
-
-    def es(E, q):
-        return a(E, 15 - q, 143 - q)
-
-    def conv(o, E, src, first=True, last=True):
-        for q in range(16):
-            mm(o, es(E, q), src(q), first and q == 0, last and q == 15)
-
-    def every(n, lo, hi):
-        return lambda q: a(n, lo + q, hi, 16)
-
-    def rows(bank, src, n, lo=0, rest=None):
-        for q in range(16):
-            o, w = a(bank, lo + q, lo + 16 * n, 16), a("FH", 128 * q, 128 * q + 128)
-            mm(o, w, src, True, rest is None)
-            if rest is not None:
-                mm(o, w, rest, False, True)
-
-    def send(dst, buf, rbuf, n, arr, loc):
-        to = T.cores[dst]
-        use = topo.engines(core, to)[:8]
-        rid, pid = topo.addr(to)[0], topo.addr(to)[1]
-        acc = [((buf, 0, n), False)]
-        order("G", acc)
-        g.remote_dma(T[rbuf][:, 0:n], T[buf][:, 0:n], T.sem[arr], T.sem[loc], pid, rid, sum(1 << e for e in use))
-        total[loc] = len(use)
-        note("G", acc, (loc, len(use), {loc: len(use)}), True)
-
-    def lands(src, buf, n, arr):
-        k = len(topo.engines(T.cores[src], core)[:8])
-        total[arr] = k
-        note("R", [((buf, 0, n), True)], (arr, k, {arr: k}), True)
-
-    up, dn = (rank + 1) % N, (rank - 1) % N
-    for t in range(3):
-        lands((rank - 1 - t) % N, "z%d" % (t + 1), 256, "az%d" % t)
-        lands(dn, "hl%d" % t, 32, "ah%d" % t)
-        lands(up, "gl%d" % t, 32, "ag%d" % t)
-
-    def load(q, v, src, part=None):
-        dma(q, v[0] if part is None else part, src, [(r, True) for r in v[1]])
-
-    load("D", a("glI"), T.gl[:, :])
-    iota(a("ci", 0, 1), [[0, 1]], 0, 1)
-    iota(a("gx"), [[1, 8], [0, 16]], 0, 0)
-    iota(a("X"), [[1, 512]], 0, 0)
-    load("S", a("W", 16), T.rec[:, :])
-    fill(a("vr0"), 0)
-    fill(a("thr"), 0)
-    load("D", a("vr0"), T.val[:, :], T["aI"][0:128:16, 0:512])
-    load("D", a("nbI"), T.nb[:, :])
-    load("D", a("z0", 0, 256), T.zl[:, :])
-    load("D", a("thr"), T.th[:, :], T["aI"][0:128:16, 1024:1280])
-    iota(a("ones"), [[0, 2048]], 1, 0)
-    keep(a("mask"), a("ones", 0, 1024), [[0, 64], [1, 16]], GT, 0, 0)
-    iota(a("mA"), [[16, 32]], 0, 1)
-    iota(a("tie"), [[-256, 16], [0, 16]], 3840, 0)
-    iota(a("x32"), [[0, 16], [1, 32]], 0, 0)
-    iota(a("rI"), [[1, 16], [0, 2]], 0, 0)
-    keep(a("ID"), a("ones", 0, 128), [[-1, 128]], EQ, 0, 1)
-    keep(a("FH"), a("ones"), [[-1, 16], [-16, 8], [0, 16]], EQ, 0, 1)
-    iota(a("Tlo"), [[0, 8], [1, 16]], 0, 0)
-    keep(a("Tlo"), a("Tlo"), [[-16, 8], [0, 16]], GE, 0, 1, -1.0)
-    keep(a("Tlo"), a("Tlo"), [[16, 8], [0, 16]], GE, 15, -1, -1.0)
-
-    for n, (op, c) in enumerate(((AND, 15), (AND, 112), (AND, 96), (SHR, 4), (AND, 14), (AND, 1), (AND, 7), (AND, 8))):
-        ts(a("ci", n + 1, n + 2), a("ci", 0, 1), c, op)
-    ts(a("ci", 9, 10), a("ci", 0, 1), 4, SHR, 1, AND)
-    cp(a("cf", 0, 10), a("ci", 0, 10))
-
-    def cf(n):
-        return a("cf", n, n + 1)
-
-    def cc(n):
-        return a("cc", n, n + 1)
-
-    def mk_e(n, w):
-        ts(a(n), a("X", 0, 144), cc(0), EQ, w, MUL)
-
-    ts(a("BD"), a("gx"), cf(4), EQ)
-    keep(a("BDdp"), a("BD"), [[0, 8], [-1, 16]], GE, 1, 0)
-    keep(a("BDt"), a("BD"), [[0, 8], [1, 16]], GE, -2, 0)
-    keep(a("BDt"), a("BDt"), [[0, 8], [-1, 16]], GE, 3, 0)
-    keep(a("TRI"), a("BD"), [[-1, 128]], GT, 0, 1)
-    ts(cc(8), cf(1), 1.0, OP.not_equal)
-    ts(cc(7), cf(1), 0.0, OP.not_equal)
-    ts(cc(9), cc(8), 33.0, MUL, -32.0, ADD)
-    ts(cc(10), cc(7), 33.0, MUL, -32.0, ADD)
-    ts(cc(0), cf(2), 15.0, ADD)
-    ts(cc(2), cf(1), 2.0, EQ, 16384.0, MUL)
-    ts(cc(11), cf(1), -1024.0, MUL, 15359.0, ADD)
-    fill(a("T01", 0, 1), -32.0)
-    mk_e("En2", cc(2))
-    ts(a("LSp", 0, 512), a("glI"), 1.0, ADD)
-    act(a("onb"), a("LSp", 0, 512), f=AF.Sign)
-    ts(a("offN"), a("glI"), 1.0, ADD)
-    mm(a("b5"), a("BD"), a("onb"), True, True)
-    ts(a("T01", 1, 513, 2), a("b5", 0, 512, 2), cc(8), MUL, cc(9), ADD)
-    ts(a("T01", 2, 514, 2), a("b5", 1, 512, 2), cc(7), MUL, cc(10), ADD)
-
-    def gather_n(q, ch):
-        o, i = a("GN", 1024 * ch, 1024 * ch + 1024), ind(a("T01", 0, 513), a("offN", 64 * ch, 64 * ch + 64))
-        if q == "V":
-            cp(o, i)
-        else:
-            act(o, i)
-
-    def kmax_pe(bank, ch):
-        conv(a(bank, 128 * ch, 128 * ch + 128), "En2", every("GN", 2048 * ch, 2048 * ch + 2048))
-
-    def kmax_key(src, add, ch):
-        lo, hi = 128 * ch, 128 * ch + 128
-        if add is not None:
-            tt(a("ky", lo, hi), a(src, lo, hi), a(add, lo, hi), ADD)
-            src = "ky"
-        emit("V", a("kyT", lo, hi), [a(src, lo, hi)], lambda e: e.transpose(a("kyT", lo, hi)[0], a(src, lo, hi)[0]))
-        scan(a("ks", lo, hi), a("mask", 0, 128), a("kyT", lo, hi), 0.0, MAX)
-
-    def kmax_fin(small, so, dest):
-        cp(a("kI"), a("ks", 15, 512, 16))
-        ts(a("khI"), a("kI"), 10, SHR)
-        ts(a("klI"), a("kI"), 1023, AND)
-        cp(a("khH"), a("khI"))
-        cp(a("klH"), a("klI"))
-        for c1 in range(2):
-            n = 0
-            for g1 in range(2):
-                for part, src in ((1, "khH"), (0, "klH")):
-                    k = 128 * (4 * part + 2 * c1 + g1)
-                    mm(a(small, so + c1, so + 32, 2), a("TA", k, k + 128), a(src, g1, 32, 2), n == 0, n == 3)
-                    n += 1
-        return lambda: ts(a(dest), a(small, so, so + 32), 512.0, MAX)
-
-    for ch in range(1, 6):
-        gather_n("S", ch)
-    for ch in (0, 6, 7):
-        gather_n("V", ch)
-    ts(a("mA"), a("mA"), cf(2), SUB)
-    mk_e("E1", 1.0)
-    kmax_pe("b6", 0)
-    kmax_pe("b6", 1)
-    kmax_pe("b4", 3)
-    kmax_pe("b4", 2)
-    ts(a("C"), a("LSp", 0, 512), cc(11), ADD)
-    ts(a("lvI", 0, 512), a("glI"), 1, AND)
-    ts(a("kp"), a("lvI", 0, 512), -524288.0, MUL)
-    tt(a("C0"), a("C"), a("kp"), ADD)
-    kmax_key("b6", "C0", 0)
-    kmax_key("b6", "C0", 1)
-    mk_e("Eh", 1.0)
-    cp(a("BDh"), a("BD"))
-    cp(a("vrh"), a("vr0"))
-    mm(a("b7"), a("BDh"), a("vrh"), True, True)
-    conv(a("b3", 0, 32), "Eh", every("vrh", 0, 512))
-    for n, s, b, src in (("m21", 2.0, 1.0, "mA"), ("m37", 2.0, 37.0, "mA"), ("m613", 2.0, 613.0, "mA"), ("mneg", 1.0, -512.0, "mA"),
-                         ("Mrow", 1.0, 1.0, "X"), ("x613", 2.0, 613.0, "X"), ("x21", 2.0, 1.0, "X")):
-        act(a(n), a(src), s, b)
-    act(a("nrow"), a("b5"))
-    act(a("drow", 0, 512), a("b7"))
-    act(a("C1"), a("kp"), -2.0, -524288.0)
-    for g1 in range(2):
-        ts(cc(16 + g1), cf(3), cf(1), ADD, 16.0 * g1, ADD)
-    ts(cc(18), cf(9), 0.0, EQ)
-    for c1, c in enumerate((cc(18), cf(9))):
-        ts(cc(20 + c1), c, 1024.0, MUL)
-        for g1 in range(2):
-            for part in range(2):
-                k = 128 * (4 * part + 2 * c1 + g1)
-                ts(a("TA", k, k + 128), a("X", 0, 128), cc(16 + g1), EQ, cc(20 + c1) if part else c, MUL)
-    kmax_key("b4", "C0", 3)
-    kmax_key("b4", "C0", 2)
-    km0 = kmax_fin("b1", 0, "km0")
-    ts(cc(1), cf(1), 0.0, EQ)
-    ts(cc(4), cf(1), 256.0, MUL, 1024.0, ADD)
-    ts(cc(5), cf(5), 0.0, EQ, 4096.0, MUL)
-    ts(cc(6), cf(5), 2.0, EQ)
-    ts(cc(22), cc(1), 64.0, MUL)
-    ts(cc(3), cf(1), 1.0, EQ, 16384.0, MUL)
-    ts(cc(23), cc(1), 16384.0, MUL)
-    act(a("Er0"), a("E1"), cc(1))
-    km0()
-    cp(a("dA"), a("b3", 0, 32))
-    cp(a("gs0"), a("dA"))
-    send(dn, "gs0", "gl0", 32, "ag0", "lg0")
-    iota(a("WK", 512), [[0, 4096]], 0, 0)
-    later = [None] * 4
-    fill(a("LSp", 512, 528), 0.0)
-    fill(a("drow", 512, 528), 0.0)
-    fill(a("W", 0, 16), 0.0)
-    fill(a("z0", 256, 272), 0.0)
-
-    def trial_tables():
-        for j in range(4):
-            ts(a("pI", 32 * j, 32 * j + 32), a("dA"), float(j), ADD)
-        ts(a("pI", 128, 256), a("pI", 0, 128), 15, AND)
-        cp(a("p4"), a("pI", 128, 256))
-
-    def consts_t():
-        ts(a("thI", 0, 256), a("thr"), 6, SHR)
-        ts(a("thI", 256, 512), a("thr"), 63, AND)
-        cp(a("thb"), a("thI"))
-        conv(a("b5", 64, 80), "Eth", every("thb", 0, 256), True, False)
-        conv(a("b5", 64, 80), "Er0", every("thb", 256, 512), False, True)
-        conv(a("b5", 96, 128), "Er0", every("nrow", 0, 512))
-
-    def consts_d():
-        cp(a("thB"), a("b5", 64, 80))
-        ts(a("thK"), a("thB"), 4096.0, MUL, 4095.0, ADD)
-        ts(a("c15m"), a("b5", 96, 128), -1024.0, MUL, 15359.0, ADD)
-
-    def consts_e():
-        ts(cc(12), cf(7), 2.0, MUL, cf(2), ADD)
-        ts(cc(13), cc(12), 1.0, ADD)
-        ts(cc(14), cf(8), 0.0, EQ)
-        ts(cc(15), cf(8), 0.0, GT)
-        for t in range(2):
-            for h in range(2):
-                k = 128 * (2 * t + h)
-                ts(a("HX", k, k + 128), a("X", 0, 128), cc(12 + t), EQ, cc(14 + h), MUL)
-        for t in (1, 2):
-            fill(a("z%d" % t, 256, 272), 0.0)
-
-    def ghost_rows(src):
-        rows("b7", src, 32)
-        act(a("drow", 512, 1024), a("b7"))
-
-    def f(n):
-        return a("sF", 32 * n, 32 * n + 32)
-
-    def i(n):
-        return a("sI", 32 * n, 32 * n + 32)
-
-    def u(n, m=1):
-        return a("sU", 32 * n, 32 * (n + m))
-
-    for t in range(3):
-        par, zt = t & 1, "z%d" % t
-
-        def med(n, o=0, par=par):
-            return a(n, o + par, o + 512, 2)
-
-        if t == 0:
-            cp(i(0), a("km0"))
-        else:
-            tt(i(0), a("km%d" % t), f(31), MAX)
-        ts(i(1), i(0), 1023, AND)
-        cp(u(0), i(1))
-        ts(i(2), i(0), 1, SHR, 511, AND)
-        cp(u(2), i(2))
-        act(a("gr"), ind(a("drow", 0, 528), u(0)))
-        ts(f(0), i(1), 2.0, MUL, 1.0, ADD)
-        ts(a("offL"), med("LSp"), -1.0, ADD)
-        tt(a("eq"), ind(a("LSp"), u(0)), a("Mrow"), EQ)
-        if t == 0:
-            act(a("Zq"), ind(a(zt), u(2)))
-
-        def ga(ch):
-            act(a("GA", 512 + 1024 * ch, 1536 + 1024 * ch), ind(a("drow", 0, 512), a("offL", 64 * ch, 64 * ch + 64)))
-
-        if t == 0:
-            for n, c in (("Es", cc(4)), ("E64", 64.0), ("Eth", cc(22))):
-                act(a(n), a("E1"), c)
-            trial_tables()
-        for j in range(4):
-            act(f(4 + j), f(0), 1.0, 612.0)
-        act(f(2), f(0), 0.25, -1024.25 - 0.5 * par)
-        act(f(27), f(0), 4.0, -4.0 - 8.0 * par)
-        for j in range(4):
-            act(a("low", 32 * j, 32 * j + 32), a("p4", 32 * j, 32 * j + 32), 1.0, 16.0 * j)
-        if t:
-            act(a("Zq"), ind(a(zt), u(2)))
-        if t != 1:
-            ga(0)
-        else:
-            gather_n("S", 1)
-        if t:
-            later[0]()
-        conv(a("b1", 0, 32), "Er0", every("gr", 0, 512))
-        conv(a("b3", 0, 32), "Es", every("eq", 0, 512))
-        tt(i(3), f(0), a("mA"), MUL)
-        ts(i(4), i(3), 4, SHR, 4095, AND)
-        tt(f(1), i(4), a("mA"), ADD)
-        tt(a("sF", 256, 384), a("p4"), a("sF", 128, 256), MUL)
-        if t == 0:
-            tt(a("kp"), a("ky"), a("C1"), ADD)
-            ts(a("b0"), a("nbI"), 1.0, ADD)
-        tt(a("prod"), a("b0"), a("eq"), MUL)
-        conv(a("b2", 0, 32), "Eh", every("prod", 0, 512))
-        if t:
-            ghost_rows(a("rowh", 32, 64))
-        conv(a("b4", 0, 16), "Er0", lambda q: a("nrow", 2 * q + par, 512, 32))
-        tt(f(3), a("b1", 0, 32), a("m37"), MUL)
-        tt(f(3), f(3), f(1), ADD)
-        for j in range(4):
-            tt(i(8 + j), f(8 + j), f(3), ADD)
-        ts(a("sI", 256, 384), a("sI", 256, 384), 4095, AND)
-        ts(u(4, 4), a("sI", 256, 384), 16.0, ADD)
-
-        def trial(j):
-            tt(a("G4", 512 * j, 512 * j + 512), ind(a("W"), u(4 + j)), a("Zq"), MAX)
-
-        act(a("lv", 0, 256), med("LSp"), 1.0, -1.0)
-        act(a("lv", 512, 768), med("LSp"), 2.0, 35.0)
-        act(a("on16"), med("LSp"), f=AF.Sign)
-        act(a("on16"), a("on16"), 8208.0, -8192.0)
-        trial(0)
-        trial(1)
-        if t == 0:
-            cp(a("rowh", 32, 64), a("gl0"))
-            ghost_rows(a("rowh", 32, 64))
-        ts(f(16), a("b2", 0, 32), -1.0, ADD, 0.0, MAX)
-        cp(u(8), f(16))
-        act(a("gr2"), ind(a("drow"), u(8)))
-        if t == 1:
-            ga(0)
-        mm(a("b1", 64, 128), a("ID"), a("low", 0, 64), True, False)
-        conv(a("b1", 64, 128), "E64", every("G4", 0, 1024), False, True)
-        act(a("tA"), a("b1", 64, 128))
-        ga(1)
-        tt(f(17), a("b3", 0, 32), f(2), ADD)
-        ts(f(18), a("b3", 0, 32), 0.0, GT)
-        ts(f(26), a("b3", 0, 32), 1.0 / 256, MUL, 508.0, ADD)
-        conv(a("b3", 32, 64), "Er0", every("gr2", 0, 512))
-        trial(2)
-        tt(f(17), f(17), a("mneg"), MAX)
-        tt(i(5), f(16), a("m21"), MUL)
-        ts(f(20), f(16), 2.0, MUL, 37.0, ADD)
-        ts(u(10), f(17), 512.0, ADD)
-        ts(i(5), i(5), 4, SHR, 4095, AND)
-        tt(f(22), a("dA"), f(20), MUL)
-        tt(f(26), f(26), f(27), ADD)
-        ts(a("full"), a("b4", 0, 16), 15.5, GT)
-        tt(f(26), f(26), f(18), MUL)
-        trial(3)
-        mm(a("b2", 64, 128), a("ID"), a("low", 64, 128), True, False)
-        conv(a("b2", 64, 128), "E64", every("G4", 1024, 2048), False, True)
-        if t == 0:
-            act(a("BDdn"), a("BDdp"), -1.0)
-            cp(a("BDo"), a("BDt"))
-            cp(a("offR"), a("rI"))
-        mm(a("b4"), a("BDo"), a("prod"), True, False)
-        ga(2)
-        ga(3)
-        tt(f(26), f(26), a("mA"), MAX)
-        tt(f(19), i(5), f(16), ADD)
-        cp(u(11), f(26))
-        tt(f(21), a("b3", 32, 64), a("m613"), MUL)
-        tt(f(19), f(19), f(21), ADD)
-        tt(i(6), f(22), f(19), ADD)
-        ts(i(6), i(6), 4095, AND)
-        ts(u(12), i(6), 16.0, ADD)
-        tt(a("D2", 0, 512), ind(a("W"), u(12)), a("Zq"), MAX)
-        mm(a("b4"), a("BDdn"), a("D2", 0, 512), False, False)
-        tt(a("tk", 0, 64), a("tA"), a("b2", 64, 128), MIN)
-        tt(i(7), a("tk", 0, 32), a("tk", 32, 64), MIN)
-        ts(i(7), i(7), 15, AND)
-        tt(f(23), i(7), f(20), MUL)
-        cp(a("rowh", 0, 32), i(7))
-        tt(i(12), f(23), f(19), ADD)
-        tt(f(24), i(7), a("dA"), SUB)
-        ts(i(12), i(12), 4095, AND)
-        ts(u(14), i(12), 16.0, ADD)
-        tt(a("D2", 512, 1024), ind(a("W"), u(14)), a("Zq"), MAX)
-        rows("b7", a("rowh", 0, 32), 32)
-        act(a("dlt"), a("b7"))
-        mm(a("b4"), a("BDdp"), a("D2", 512, 1024), False, True)
-        act(a("hiT"), a("b4"), cf(6))
-        if t:
-            later[2]()
-        if t == 1:
-            gather_n("S", 2)
-            gather_n("S", 3)
-            kmax_pe("b5", 0)
-        if t == 0:
-            for n, s, src in (("Ek", cc(5), "E1"), ("Eo", cc(6), "E1"), ("BDo2", cc(6), "BD"), ("En1", cc(3), "E1"), ("En0", cc(23), "E1")):
-                act(a(n), a(src), s)
-            act(a("cB"), a("mA", 0, 16), 1.0, 3840.0)
-            consts_t()
-        tt(f(24), f(24), f(18), MUL)
-        tt(f(25), a("dA"), f(24), ADD)
-        if t < 2:
-            cp(a("gs%d" % (t + 1)), f(25))
-            send(dn, "gs%d" % (t + 1), "gl%d" % (t + 1), 32, "ag%d" % (t + 1), "lg%d" % (t + 1))
-        ts(a("mk", 256 * par, 256 * par + 256), med("nrow"), cf(1), EQ)
-        tt(a("lvI", 0, 256), a("lv", 0, 256), med("x21"), MUL)
-        ts(a("lvI", 0, 256), a("lvI", 0, 256), 4, SHR, 4095, AND)
-        cp(ind(a("GA"), u(11)), a("dlt"))
-        conv(a("b6", 0, 256), "Er0", every("GA", 512, 4608))
-        tt(a("yv"), a("b4"), a("hiT"), SUB)
-        cp(ind(a("WK"), u(10)), a("yv"))
-        mm(a("b7", 0, 256), a("ID"), a("tie"), True, False)
-        conv(a("b7", 0, 256), "Ek", every("WK", 512, 4608), False, True)
-        tt(a("lv", 256, 512), a("lvI", 0, 256), a("lv", 0, 256), ADD)
-        tt(a("lv", 768, 1024), a("lv", 512, 768), med("drow"), MUL)
-        tt(a("lv", 256, 512), a("lv", 256, 512), a("lv", 768, 1024), ADD)
-        tt(a("b6", 256, 512), a("b6", 0, 256), med("x613"), MUL)
-        tt(a("lvI", 256, 512), a("b6", 256, 512), a("lv", 256, 512), ADD)
-        ts(a("lvI", 256, 512), a("lvI", 256, 512), 4095, AND)
-        tt(a("lv", 768, 1024), a("lvI", 256, 512), a("on16"), ADD)
-        cp(a("offM"), a("lv", 768, 1024))
-        for ch in range(4):
-            act(a("GL", 1024 * ch, 1024 * ch + 1024), ind(a("W"), a("offM", 64 * ch, 64 * ch + 64)))
-
-        def level_scan(ch):
-            lo = 1024 * ch
-            scan(a("sc", lo, lo + 1024), a("mask"), a("GL", lo, lo + 1024), 0.0, MAX)
-
-        if t == 0:
-            consts_d()
-            for ch in range(4):
-                kmax_key("kp", None, ch)
-            later[1] = kmax_fin("b1", 224, "km1")
-        if t == 1:
-            gather_n("V", 4)
-            for ch in (5, 6, 7):
-                gather_n("S", ch)
-            kmax_key("b5", "C0", 0)
-            kmax_pe("b5", 1)
-        if t:
-            later[3]()
-        cp(a("tk", 64, 192), a("b7", 128, 256))
-        tt(a("tk", 192, 320), a("b7", 0, 128), a("tk", 64, 192), MAX)
-        tt(a("tk", 320, 384), a("tk", 192, 256), a("tk", 256, 320), MAX)
-        tt(a("tk", 384, 416), a("tk", 320, 352), a("tk", 352, 384), MAX)
-        tt(a("kwI", 0, 16), a("tk", 384, 400), a("tk", 400, 416), MAX)
-        ts(a("kwI", 16, 32), a("kwI", 0, 16), 3840, AND)
-        tt(a("sB", 0, 16), a("cB"), a("kwI", 16, 32), SUB)
-        cp(a("sU", 480, 496), a("sB", 0, 16))
-        cp(a("wr"), ind(a("WK", 512, 4608), a("sU", 480, 496)))
-        tt(a("sB", 16, 32), a("kwI", 0, 16), a("thK"), GT)
-        cp(a("sBb", 0, 16), a("sB", 16, 32))
-        conv(a("b1", 128, 144), "Eo", every("wr", 0, 256))
-        mm(a("b4", 0, 256), a("BDo2"), a("wr"), True, True)
-        if t < 2:
-            mm(a("b3", 128, 144), a("ones", 0, 128), a("sBb", 0, 16), True, True)
-        level_scan(0)
-        tt(a("sB", 32, 48), a("b1", 128, 144), a("sB", 16, 32), MUL)
-        ts(a("sBb", 16, 32), a("sB", 32, 48), 512.5, GT)
-        mm(a("b2", 128, 144), a("BD"), a("sBb", 16, 32), True, True)
-        mm(a("b2", 144, 160), a("TRI"), a("sBb", 16, 32), True, True)
-        tt(a("eqo"), med("LSp"), a("b4", 0, 256), EQ)
-        mm(a("b1", 192, 208), a("ID"), a("full"), True, False)
-        conv(a("b1", 192, 208), "E1", every("eqo", 0, 256), False, True)
-        ts(a("sB", 48, 64), a("sB", 32, 48), -512.0, ADD, 0.0, MAX)
-        scan(a("sB", 64, 80), a("ones", 0, 16), a("b2", 128, 144), -60.0, ADD)
-        tt(a("sB", 80, 96), a("sB", 64, 80), a("b2", 144, 160), LE)
-        tt(a("sB", 96, 112), a("sB", 80, 96), a("sB", 48, 64), MUL)
-        ts(a("kwI", 0, 16), a("sB", 96, 112), -1.0, ADD)
-        ts(a("kwI", 16, 32), a("kwI", 0, 16), 15, AND)
-        ts(a("kwI", 0, 16), a("kwI", 0, 16), 4, SHR)
-        cp(a("sB", 112, 144), a("kwI", 0, 32))
-        tt(a("rt"), ind(a("sB", 112, 128), a("offR")), a("x32"), EQ)
-        for h in range(16):
-            ts(a("lt", 128 * h, 128 * h + 128), a("Tlo"), a("sB", 128 + h, 129 + h), EQ)
-            mm(a("b2", 192, 224), a("lt", 128 * h, 128 * h + 128), a("rt", 32 * h, 32 * h + 32), h == 0, h == 15)
-        ts(a("sB", 144, 160), a("sB", 32, 48), 512.5, LT)
-        cp(a("hs%d" % t), a("b2", 192, 224))
-        send(up, "hs%d" % t, "hl%d" % t, 32, "ah%d" % t, "lh%d" % t)
-        tt(a("sB", 144, 160), a("sB", 144, 160), a("b1", 192, 208), GT)
-        tt(a("jv"), a("sB", 144, 160), a("sB", 32, 48), MUL)
-        cp(a("jw", 0, 16), a("jv"))
-        tt(a("jw", 16, 32), a("jv"), a("jw", 0, 16), SUB)
-        if t == 0:
-            consts_e()
-        if t < 2:
-            for h in range(2):
-                k = 128 * (2 * par + h)
-                mm(a("b3", 160 + h, 192, 2), a("HX", k, k + 128), a("jv"), True, True)
-
-        def jv_rows():
-            rows("b2", a("jw", 0, 16), 16, 256, a("jw", 16, 32))
-
-        if t == 2:
-            jv_rows()
-        if t == 1:
-            kmax_key("b5", "C0", 1)
-            kmax_pe("b5", 2)
-        level_scan(1)
-        if t == 0:
-            ts(a("jw", 32, 48), a("jv"), 1.0, MIN)
-            rows("b2", a("jw", 32, 48), 16, 256)
-            act(a("sg"), a("b2", 256, 512))
-        if t < 2:
-            if t == 0:
-                cp(a("oX"), a("b3", 160, 192))
+    for s in steps:
+        if s["kind"] == "send":
+            buf, rbuf, arr, loc, dst, src = s["alts"]["G"][1][0]
+            total[arr] = len(topo.engines(T.cores[src], core)[:8])
+            note("R", [(rbuf[1][0], True)], (arr, total[arr], {arr: total[arr]}), True)
+    for k, q in plan:
+        s = steps[k]
+        if s["kind"] == "send":
+            buf, rbuf, arr, loc, dst, src = s["alts"][q][1][0]
+            to = T.cores[dst]
+            use = topo.engines(core, to)[:8]
+            acc = [(buf[1][0], False)]
+            order(q, acc)
+            g.remote_dma(rbuf[0], buf[0], T.sem[arr], T.sem[loc], topo.addr(to)[1], topo.addr(to)[0], sum(1 << e for e in use))
+            total[loc] = len(use)
+            note(q, acc, (loc, len(use), {loc: len(use)}), True)
+            continue
+        for acc, call in s["alts"][q][1]:
+            order(q, acc)
+            if s["kind"] == "dma":
+                sem, n = "d%d" % nd[0], 16
+                nd[0] += 1
             else:
-                tt(a("oX"), a("oX"), a("b3", 160, 192), ADD)
-            cp(u(14), a("oX"))
-            act(a("gr"), ind(a("T01", 0, 513), u(14)))
-            tt(f(30), a("oX"), a("c15m"), ADD)
-            tt(i(13), a("gl%d" % (t + 1)), a("hs%d" % t), ADD)
-            ts(i(14), i(13), 15, AND)
-            cp(a("rowh", 32, 64), i(14))
-        level_scan(2)
-        level_scan(3)
-        mm(a("b6", 256, 512), a("ID"), a(zt, 0, 256), True, False)
-        mm(a("b6", 256, 512), a("ID"), a("sc", 15, 4096, 16), False, True)
-        if t == 1:
-            kmax_key("b5", "C0", 2)
-            kmax_pe("b5", 3)
-        act(a("zf"), a("b6", 256, 512), 0.5, -0.25)
-        act(a("zf"), a("zf"), 1.0, 12582912.0)
-        act(a("zs"), a("zf"), 1.0, -12582912.0)
-        send((rank + 1 + t) % N, "zs", "z%d" % (t + 1), 256, "az%d" % t, "lz%d" % t)
-
-        def lists(t=t, med=med):
-            tt(a("lv", 1024, 1280), a("b2", 256, 512), a("mk", 256 * (t & 1), 256 * (t & 1) + 256), MUL)
-            tt(med("LSp"), med("LSp"), a("lv", 1024, 1280), ADD)
-            if t == 0:
-                tt(a("nrow", 0, 512, 2), a("nrow", 0, 512, 2), a("sg"), ADD)
-
-        def limits():
-            emit("V", a("sB", 160, 161), [a("b3", 128, 144)], lambda e: e.tensor_reduce(a("sB", 160, 161)[0], a("b3", 128, 144)[0], axis=AxisListType.X, op=ADD))
-            cp(a("kwI", 0, 1), a("sB", 160, 161))
-            ts(a("kwI", 1, 2), a("kwI", 0, 1), 31, AND)
-            cp(a("sB", 161, 162), a("kwI", 1, 2))
-            ts(a("thT"), a("thB"), a("sB", 161, 162), ADD, 4080.0, MIN)
-            ts(a("thK"), a("thT"), 4096.0, MUL, 4095.0, ADD)
-
-        if t < 2:
-            conv(a("b3", 192, 224), "En1" if t == 0 else "En0", every("gr", 0, 512))
-            iota(a("WK", 512), [[0, 4096]], 0, 0)
-        tt(i(13), f(25), a("hl%d" % t), ADD)
-        ts(i(14), i(13), 15, AND)
-        cp(a("rowh", 0, 32), i(14))
-        rows("b4", a("rowh", 0, 32), 32)
-        if t == 0:
-            tt(a("T01", 1, 513, 2), a("T01", 1, 513, 2), a("sg"), ADD)
-            gather_n("S", 0)
-        elif t == 1:
-            kmax_key("b5", "C0", 3)
-            later[1] = kmax_fin("b1", 224, "km2")
-        if t < 2:
-            tt(f(31), f(30), a("b3", 192, 224), ADD)
-            later[1]()
-            act(a("drow", 0, 512), a("b4"))
-            cp(a("dA"), i(14))
-            trial_tables()
-            later[0], later[2], later[3] = limits, jv_rows, lists
-        else:
-            lists()
-            ts(a("ky"), a("LSp", 0, 512), -1.0, ADD)
-            dma("D", T.yl[:, :], a("ky")[0], [(("ky", 0, 512), False)])
-            act(a("kyT"), a("b4"))
-            dma("D", T.yd[:, :], T.kyT[0:128:16, :], [(("kyT", 0, 512), False)])
-            dma("D", T.yz[:, :], T.z3[:, :], [(("z3", 0, 256), False)])
+                sem, n = "s" + q, 1
+            total[sem] = total.get(sem, 0) + n
+            call(eng[q]).then_inc(T.sem[sem], n)
+            kn = dict(known[q])
+            kn[sem] = total[sem]
+            note(q, acc, (sem, total[sem], kn), s["kind"] == "dma")
     for s, v in total.items():
         g.wait_ge(T.sem[s], v)

@@ -13,7 +13,13 @@ BANKS = ["b%d" % _b for _b in range(8)]
 SCRATCH.update({_b: ("psum", [128, 512], F) for _b in BANKS})
 SEMAPHORES = ["sV", "sS", "sP", "sG"] + ["d%d" % i for i in range(12)] + [a + str(t) for a in ("az", "ah", "ag", "lz", "lh", "lg") for t in range(3)]
 
-GATHER, SCATTER, LEAST, WAIT, REMOTE, FIRST, DMA0, DMABYTES = 1.56, 3.8, 64, 100, 2400, 2400, 2000, 160.0
+GATHER, SCATTER, LEAST, WAIT, REMOTE, FIRST, DMA0, DMABYTES = 1.56, 3.8, 64, 125, 2400, 2400, 2000, 160.0
+SPARE, FILL, HOLD = 1000, 0.5, 150
+ONGN, ONGL = ("VS", "VS", "VS"), ("S", "S", "S")
+OPEN = ("b0", "b4")
+MORE = {'Do2/2': 2000, 'inl1/1': -150, 't21/1': 4000, 'pk2/2': -150, 'out1/1': 4000, 'b5@15/2': 1000, 'loc02/2': 1500, 'uO2/2': -150,
+        'p40/0': 4000, 'b6@32/1': -150, 'w2/': 1000, 'eq0/0': 4000, 'b3@0/': 200}
+YV = 0
 PLAN = {}
 
 
@@ -29,7 +35,7 @@ def rank_program(g, core, T, topo):
     eng = {"V": g.vector, "S": g.scalar, "P": g.tensor, "G": g, "D": g.sync}
     up, dn = (rank + 1) % N, (rank - 1) % N
 
-    tiles, top = {}, {d: 0 for d in POOL}
+    tiles, top, named, now = {}, {d: 0 for d in POOL}, {}, ["/"]
     for n, (c, d) in OWN.items():
         tiles[n] = (n, 0, c, d)
     for n in BANKS:
@@ -45,6 +51,7 @@ def rank_program(g, core, T, topo):
         b, o, c, d = tiles[n]
         hi = c if hi is None else min(hi, c)
         ap = T[b][:, o + lo:o + hi:st] if st > 1 else T[b][:, o + lo:o + hi]
+        named[(b, o + lo, o + hi)] = n + ("@%d" % lo if b in BANKS else "")
         return (ap, [(b, o + lo, o + hi)], len(range(lo, hi, st)), d, "P" if b in BANKS else "S")
 
     def ind(w, o):
@@ -62,7 +69,10 @@ def rank_program(g, core, T, topo):
         return r + [(o[1][0], True)]
 
     def step(alts, acc, late=0, kind=None):
-        steps.append({"alts": alts, "acc": acc, "late": late, "kind": kind})
+        steps.append({"alts": alts, "acc": acc, "late": late, "kind": kind, "run": None, "name": named.get(acc[-1][0], named.get(acc[0][0])) + now[0]})
+
+    def run(name):
+        steps[-1]["run"] = name
 
     def vcost(o, ins, two=False):
         full = [v for v in ins if v is not None and not isinstance(v, (int, float)) and v[2] > 1]
@@ -130,6 +140,7 @@ def rank_program(g, core, T, topo):
 
     def dma(q, out, in_, acc, size):
         step({q: (60, [(acc, lambda e: e.dma_start(out, in_))])}, acc, late=size / DMABYTES, kind="dma")
+        run(q)
 
     def send(dst, buf, rbuf, arr, loc, src):
         step({"G": (400, [(buf, rbuf, arr, loc, dst, src)])}, [(buf[1][0], False), (rbuf[1][0], True)], late=REMOTE + buf[2], kind="send")
@@ -143,8 +154,8 @@ def rank_program(g, core, T, topo):
     def every(n, lo, hi):
         return lambda q: a(n, lo + q, hi, 16)
 
-    def rows(bank, src, alone):
-        mms([(a(bank, 32 * q, 32 * q + 32), a("FH", 128 * q, 128 * q + 128), src, alone, alone or q == 15) for q in range(16)])
+    def rows(bank, src, alone, last=True):
+        mms([(a(bank, 32 * q, 32 * q + 32), a("FH", 128 * q, 128 * q + 128), src, alone, alone or (last and q == 15)) for q in range(16)])
 
     def col(n, k=0):
         return a(n, k, k + 1)
@@ -154,9 +165,9 @@ def rank_program(g, core, T, topo):
 
     load("S", a("valI"), T.val[:, :])
     load("D", new("glI", 512, I), T.gl[:, :])
+    load("D", new("thI", 16, I), T.th[:, :])
     load("D", new("nbI", 512, I), T.nb[:, :])
     load("D", a("z0", 16), T.zl[:, :])
-    load("D", new("thI", 16, I), T.th[:, :])
     new("W", 4112, B)
     load("D", a("W", 16), T.rec[:, :])
     send(dn, a("valI"), a("gI0"), "ag0", "lg0", up)
@@ -185,13 +196,12 @@ def rank_program(g, core, T, topo):
     for q in range(16):
         if q == 0:
             new("FH", 2048, B)
-        aff(a("FH", 128 * q, 128 * q + 128), es("E1", 2), isr(q))
+        aff(a("FH", 128 * q, 128 * q + 128), es("E1", 2), isr(q), on="S" if q % 3 == 2 else "V")
     ts(new("ID", 128, B), a("X", 0, 128), pf, EQ)
     s01 = cc(isr(0), 1.0, isr(1))
     new("Kc", 512, B)
     aff(a("Kc", 0, 512, 2), a("X"), isr(1), s01)
     aff(a("Kc", 1, 512, 2), a("Kc", 0, 512, 2), -1.0)
-    aff(new("Ekey", 144, B), a("E1"), cc(isr(0), 16384.0, isr(1)))
     aff(new("Ed", 144, B), a("E1"), isr(2))
     for t in range(3):
         new("TB%d" % t, 1040, B)
@@ -208,28 +218,43 @@ def rank_program(g, core, T, topo):
         ts(a("LS%d" % par, 16), gp, 1.0, ADD)
     cp(new("d0", 32, B), a("valI"))
 
+    def sizes():
+        return [(a("b0"), a("ID"), a("Kc"), True, False)], [(a("b0"), es("E1", 0), a("onS"), False, True)]
+
     def table(t):
-        mms([(a("b0"), es("E1", 0), a("onS"), True, False), (a("b0"), a("ID"), a("Kc"), False, False)])
-        rows("b0", a("d%d" % t), False)
+        if t == 0:
+            mms(sizes()[0])
+        if t == 1:
+            mm(a("b0"), a("ID"), a("TK", 1, 513), True, False)
+        rows("b0", a("d%d" % t), t == 2, t > 0)
+        if t == 0:
+            mms(sizes()[1])
         aff(a("TB%d" % t, 1, 513), a("b0"))
 
     def ghosts(t, src):
         rows("b0", src, True)
         aff(a("TB%d" % t, 513, 1025), a("b0"))
 
-    def members(t, par, keys, values):
+    def members(tab, par, keys, values, on):
         n = "GN%d" % par
+        bank, lo, w = ("b2", 0 if keys else 128, 256) if values else ("b5", 256, 128)
         for ch in range(8):
-            aff(a(n, 512 * ch, 512 * ch + 512), ind(a("TB%d" % t, 0, 513), a("off%d" % par, 32 * ch, 32 * ch + 32)))
-            if keys:
-                mms([(a("b2", 256 * par, 256 * par + 256), es("Ekey", q), a(n, 256 * q, 256 * q + 256), q == 0, q == 15) for q in (2 * ch, 2 * ch + 1)])
-            if values and ch % 2:
-                conv(a("b3", 32 * ch - 32, 32 * ch + 32), "Ed", every(n, 512 * ch - 512, 512 * ch + 512))
+            aff(a(n, 512 * ch, 512 * ch + 512), ind(a(tab, 0, 513), a("off%d" % par, 32 * ch, 32 * ch + 32)), on=on)
+            run(tab)
+            k = ch // 4
+            if ch % 4 == 3:
+                mms([(a(bank, lo + w * k + q, lo // w * w + w * k + w, 16), a(n, 2048 * k + q, 2048 * k + 2048, 16),
+                      a("WKD", 0 if keys else 8, 16 if values else 8), True, True) for q in range(16)])
+                if values:
+                    aff(a("dM", 128 * k, 128 * k + 128), a(bank, 256 * k + 128, 256 * k + 256))
+                    mm(a("b3", 128 * k, 128 * k + 128), a("dM", 128 * k, 128 * k + 128), a("ID"))
+        return [a(bank, lo + w * k, lo + w * k + 128) for k in range(2)]
 
-    def elect(t, par):
-        s = scan(new("ks%d%d" % (t, par), 256, F), a("subp" if t & 1 else "addp"), a("b2", 256 * par, 256 * par + 256), ADD, MIN if t & 1 else MAX)
-        ts(a("key%d" % t, par, 32, 2), a("ks%d%d" % (t, par), 15, 256, 16), -1.0 if t & 1 else 1.0, MUL, 0.0, MAX)
-        return s
+    def elect(t, par, src):
+        for k in range(2):
+            lo = 256 * par + 128 * k
+            scan(a("ks%d" % t, lo, lo + 128), a("subp" if t & 1 else "addp"), src[k], ADD, MIN if t & 1 else MAX)
+        ts(a("key%d" % t, 16 * par, 16 * par + 16), a("ks%d" % t, 256 * par + 15, 256 * par + 256, 16), -1.0 if t & 1 else 1.0, MUL, 0.0, MAX)
 
     for n, c in (("GN0", 4096), ("GN1", 4096), ("G4", 2048), ("GL", 4608), ("sc", 4096)):
         for t in ("", "0", "1", "2") if n[1] != "N" else ("",):
@@ -237,23 +262,27 @@ def rank_program(g, core, T, topo):
     table(0)
     iota(new("kpat", 1024, B), [[0, 64], [1, 16]])
     ts(new("mask", 1024, B), a("kpat"), 1.0, MIN)
-    aff(new("addp", 256, F), a("mask", 0, 256), 4194304.0 + 1024.0, -4194304.0)
-    aff(new("subp", 256, F), a("addp"), -1.0)
+    aff(new("addp", 128, F), a("mask", 0, 128), 4194304.0 + 1024.0, -4194304.0)
+    aff(new("subp", 128, F), a("addp"), -1.0)
     for t in range(3):
         new("key%d" % t, 32, I)
-    members(0, 0, True, False)
-    members(0, 1, True, False)
+        new("ks%d" % t, 512, F)
+    ts(new("G8", 8, B), a("X", 0, 8), gg, EQ)
+    new("WKD", 16, B)
+    aff(a("WKD", 0, 8), a("G8"), cc(isr(0), 16384.0, isr(1)))
+    aff(a("WKD", 8, 16), a("G8"), isr(2))
+    new("dM", 256, B)
+    aff(new("TK", 528, B) and col("TK"), isr(2), 0.0)
+    keys = [members("TB0", 0, True, True, ONGN[0]), members("TB0", 1, True, False, ONGN[0])]
     for t in range(2):
         for par in range(2):
-            elect(t, par)
-    for ch in range(4):
-        conv(a("b3", 64 * ch, 64 * ch + 64), "Ed", every("GN0", 1024 * ch, 1024 * ch + 1024))
+            elect(t, par, keys[par])
 
     ts(new("mA", 32, F), a("X", 0, 32), cc(r, 32.0), ADD)
     for n, c in (("m17", 17.0), ("m37", 37.0), ("m613", 613.0)):
         aff(new(n, 32, F), a("mA"), 2.0, c)
     for par in range(2):
-        aff(new("x17%d" % par, 256, F), a("X"), 4.0, 17.0 + 2 * par)
+        aff(new("x17%d" % par, 256, H), a("X"), 4.0, 17.0 + 2 * par, on="V")
         aff(new("x613%d" % par, 256, F), a("X"), 4.0, 613.0 + 2 * par)
     iota(new("Mrow", 512, F), [[1, 32], [32, 16]], 1)
     iota(new("gx", 256, F), [[0, 2], [1, 8], [0, 16]])
@@ -264,13 +293,12 @@ def rank_program(g, core, T, topo):
     iota(a("pt", 0, 32), [[1, 16], [0, 2]])
     iota(a("pt", 32, 48), [[16, 2], [0, 8]])
     iota(a("pt", 48, 64), [[16, 2], [1, 8]])
-    for ch in range(4):
-        if ch == 0:
-            new("WK0", 4608, B)
-        iota(a("WK0", 512 + 1024 * ch, 1536 + 1024 * ch), [[0, 1024]])
-    for t in (1, 2):
+    for t in range(3):
         o = new("WK%d" % t, 4608, B)
-        dma("D", a("WK%d" % t, 512)[0], a("WK0", 512)[0], [(a("WK0", 512)[1][0], False), (o[1][0], True)], 128 * 8192)
+        for ch in range(4 if t < 2 else 0):
+            iota(a("WK%d" % t, 512 + 1024 * ch, 1536 + 1024 * ch), [[0, 1024]])
+            run("WK")
+    dma("D", a("WK2", 512)[0], a("WK1", 512)[0], [(a("WK1", 512)[1][0], False), (o[1][0], True)], 128 * 8192)
     cp(new("o16", 16, U), a("X", 0, 16))
     cp(new("o32", 32, U), a("pt", 0, 32))
     ts(new("oML", 16, U), a("pt", 32, 48), r, ADD)
@@ -290,16 +318,21 @@ def rank_program(g, core, T, topo):
     aff(new("w2", 128, B), es("E1", 4), cc(r, -1.0, 15.0))
     tt(new("w3", 128, B), a("w1"), a("w2"), ADD)
     tt(new("Weq", 128, B), a("w3"), es("E1", 6), ADD)
-    ts(new("Bro2", 128, B), a("gx", 0, 128), gg, EQ, isr(2), MUL)
+    ts(new("B32", 128, B), a("gx", 0, 128), gg, EQ, cc(isr(2), 32.0), MUL)
+    aff(new("B37", 128, B), a("B32"), 37.0 / 32)
+    aff(new("ID64", 128, B), a("ID"), 64.0)
+    aff(new("IDn", 128, B), a("ID"), -1.0)
+    aff(new("j4", 128, B), a("j16"), 1.0 / 16)
+    aff(new("k0", 128, B), a("mask", 0, 128), -1.0, 1.0)
+    acc = spans(new("Sh", 128, B), [a("mask", 0, 128)])
+    step({"G": (460, [(acc, lambda e: e.affine_select(a("Sh")[0], a("mask", 0, 128)[0], [[-1, 128]], EQ, 0.0, 1, 1))])}, acc)
+    aff(new("Shn", 128, B), a("Sh"), -1.0)
     cp(new("IDh", 128, H), a("ID"))
-    ts(new("tri", 128, B), a("X", 0, 128), pf, GT)
-    aff(new("id64", 128, B), a("ID"), -64.0)
+    ts(new("tri", 128, B), a("X", 0, 128), pf, GT, 1.0 / 128, MUL)
+    aff(new("id64", 128, B), a("ID"), -0.5)
     tt(new("TRI", 128, B), a("tri"), a("id64"), ADD)
-    fill(new("ones", 128, B), 1.0)
-    fill(new("cm", 16, B), -1024.0)
-    fill(new("half", 256, B), -0.5)
+    fill(new("ones", 128, B), 1.0 / 128)
     fill(a("W", 0, 16), 0.0)
-    ts(new("G8", 8, B), a("X", 0, 8), gg, EQ)
     aff(new("G8n", 8, B), a("G8"), -1.0)
     w = cc(isr(4), 256.0, cc(s01, 4096.0))
     new("WAB", 16, B)
@@ -311,8 +344,7 @@ def rank_program(g, core, T, topo):
     ts(new("R1", 16, F), a("X", 0, 16), cc(r8, 1.0, gg), EQ)
     aff(new("R1a", 16, B), a("R1"), 262144.0)
     aff(new("R1b", 16, B), a("R1"), 4096.0)
-    ts(new("R2a", 16, H), a("I16"), 1024.0, MUL)
-    ts(new("R2b", 16, H), a("I16"), 0.5, MUL)
+    aff(new("R2", 16, B), a("I16"))
     aff(new("xQ", 256, B), a("kpat", 0, 256), 8.0, 128.0)
     ts(new("nbh", 512, H), a("nbI"), 2.0, MUL, -127.0, ADD)
     mms([(a("b1", q, 512, 16), a("IDh"), a("nbh", 32 * q, 32 * q + 32), True, True) for q in range(16)])
@@ -320,12 +352,13 @@ def rank_program(g, core, T, topo):
     ts(a("th2", 0, 16), a("thI"), 6, SHR)
     ts(a("th2", 16, 32), a("thI"), 63, AND)
     tt(new("thx", 256, B), ind(a("th2"), a("oML")), a("MK1"), MUL)
-    mms([(a("b5", 0, 16), a("thx", 0, 128), a("R1a"), True, False), (a("b5", 0, 16), a("thx", 128, 256), a("R1b"), False, True)])
-    aff(new("thK0", 16, F), a("b5", 0, 16), 1.0, 4095.0)
+    mms([(a("b7", 208, 224), a("thx", 0, 128), a("R1a"), True, False), (a("b7", 208, 224), a("thx", 128, 256), a("R1b"), False, True)])
+    aff(new("thK0", 16, F), a("b7", 208, 224), 1.0, 4095.0)
     ghosts(0, cp(new("gb0", 32, B), a("gI0")))
 
     for t in range(3):
         par, s = t & 1, str(t)
+        now[0] = "/" + s
         LS, TB, zt, d, key = "LS%d" % par, "TB" + s, "z" + s, a("d" + s), a("key" + s)
 
         def n32(n, dt=F, c=32):
@@ -337,17 +370,19 @@ def rank_program(g, core, T, topo):
         def h(n, lo=0, hi=None, st=1):
             return a(n + s, lo, hi, st)
 
-        cp(n32("LSh", H, 256), a(LS, 16))
-        mms([(a("b7", 256 + 128 * k, 384 + 128 * k), h("LSh", 128 * k, 128 * k + 128), a("IDh"), True, True) for k in range(2)])
-        aff(n32("LMT", F, 256), a("b7", 256, 512))
-        mms([(a("b5", 16 + 8 * k, 24 + 8 * k), a("onS", par + 256 * k, 256 * k + 256, 2), a("G8n" if par else "G8"), True, True) for k in range(2)])
-        aff(n32("nMT", F, 16), a("b5", 16, 32))
-        tt(n32("mkT", B, 256), ind(h("nMT"), a("o16")), a("kpat", 0, 256), EQ)
-        ts(n32("room", F, 16), h("nMT"), 15.5, LT)
-        aff(n32("c15", F, 16), h("nMT"), -1.0, 15.0)
-        i1 = ts(n32("i1", I), key, 1023, AND)
+        n32("i1", I)
+        n32("ex", B, 256)
+        for p2 in (par, 1 - par):
+            ts(h("i1", 16 * p2, 16 * p2 + 16), a("key" + s, 16 * p2, 16 * p2 + 16), 1023, AND)
+            tt(h("ex", 128 * p2, 128 * p2 + 128), ind(h("i1", 16 * p2, 16 * p2 + 16), a("oMT", 0, 8)), a("MK2", 0, 128), MUL)
+            mm(a("b6", 224 + p2, 256, 2), h("ex", 128 * p2, 128 * p2 + 128), a("R2"))
+        i1 = a("b6", 224, 256)
         uE = ts(n32("uE", U), i1, 2.0, MUL, par - 1.0, ADD)
         uZ = ts(n32("uZ", U), i1, 15.0, ADD)
+        mms([(a("b6", 256, 384), a("ID"), a("j4"), True, False)] + [(a("b6", 256 + 32 * j, 288 + 32 * j), a("ID"), d, False, j == 3) for j in range(4)])
+        n32("pI", I, 256)
+        cp(h("pI", 0, 128), a("b6", 256, 384))
+        cp(n32("p4", B, 128), ts(h("pI", 128, 256), h("pI", 0, 128), 15, AND))
         aff(n32("gr", B, 512), ind(a(TB, 0, 513), uE))
         conv(a("b6", 0, 32), "Ed", every("gr" + s, 0, 512))
         Zq = aff(n32("Zq", B, 512), ind(a(zt), uZ))
@@ -356,18 +391,14 @@ def rank_program(g, core, T, topo):
         conv(a("b7", 64, 96), "Eh", every("prod" + s, 0, 512))
         conv(a("b7", 96, 128), "Es", every("eq" + s, 0, 512))
         mms([(a("b4"), a("Weq"), eq, True, False), (a("b4"), es("E2h", 2), prod, False, False)])
-        f17 = ts(n32("f17"), i1, 4.0, MUL, 13.0 + 2 * par, ADD)
-        c1 = aff(n32("c1"), f17, 1.0, 596.0)
+        f17 = aff(n32("f17"), i1, 4.0, 13.0 + 2 * par)
+        n32("c5", F, 160)
+        for j in range(4):
+            aff(h("c5", 32 * j + 32, 32 * j + 64), f17, 1.0, 596.0, on="S")
         base = ts(n32("base", I), tt(n32("b0_", I), f17, a("mA"), MUL), 4, SHR)
-        n32("pI", I, 256)
-        n32("t4", F, 128)
-        for j in range(4):
-            ts(h("pI", 32 * j, 32 * j + 32), d, float(j), ADD)
-        ts(h("pI", 128, 256), h("pI", 0, 128), 15, AND)
-        cp(n32("p4", B, 128), h("pI", 128, 256))
-        for j in range(4):
-            tt(h("t4", 32 * j, 32 * j + 32), h("pI", 128 + 32 * j, 160 + 32 * j), c1, MUL)
-        X2 = tt(n32("X2"), tt(n32("X1"), a("b6", 0, 32), a("m37"), MUL), base, ADD)
+        tt(n32("t4", F, 128), h("p4"), h("c5", 32), MUL)
+        n32("r2", F, 64)
+        X2 = tt(h("r2", 32), tt(n32("X1"), a("b6", 0, 32), a("m37"), MUL), base, ADD)
         n32("P4", I, 256)
         for j in range(4):
             tt(h("P4", 32 * j, 32 * j + 32), h("t4", 32 * j, 32 * j + 32), X2, ADD)
@@ -375,58 +406,78 @@ def rank_program(g, core, T, topo):
         ts(n32("u4", U, 128), h("P4", 128, 256), 16.0, ADD)
         uO = ts(n32("uO", U), a("b7", 64, 96), 0.5, MUL, 64.5, ADD)
         fo = aff(n32("fo"), a("b7", 64, 96), 0.5, 63.5)
-        f20 = aff(n32("f20"), fo, 2.0, 37.0)
-        flag = ts(n32("flag"), a("b7", 96, 128), 1.0, MIN)
-        pos = tt(n32("pos0"), a("b7", 96, 128), aff(n32("f16i"), f17, 4.0, 443.0 - 8 * par), ADD)
-        pos = tt(n32("pos2"), tt(n32("pos1"), pos, flag, MUL), a("mA"), MAX)
+        f20 = aff(h("c5", 0, 32), fo, 2.0, 37.0, on="S")
+        out = aff(n32("out", B), a("b7", 96, 128), -8192.0, 8192.0, on="S", f=AF.Relu)
+        pos = tt(n32("pos0"), a("b7", 96, 128), aff(n32("f16i"), f17, 4.0, 443.0 - 8 * par, on="S"), ADD)
+        pos = tt(n32("pos2"), tt(n32("pos1"), pos, out, SUB), a("mA"), MAX)
         uP = cp(n32("uP", U), pos)
         gr2 = aff(n32("gr2", B, 512), ind(a(TB, 0, 1025), uO), on="S", f=AF.Abs)
         conv(a("b6", 32, 64), "Ed", every("gr2" + s, 0, 512))
-        mm(a("b4"), es("E0", 5), gr2, False, False)
+        if t < 2:
+            mm(a("b4"), es("E0", 5), gr2, False, False)
         for k, bank in enumerate(("b6", "b7")):
             for j in (2 * k, 2 * k + 1):
                 tt(h("G4", 512 * j, 512 * j + 512), ind(a("W"), h("u4", 32 * j, 32 * j + 32)), Zq, MAX)
+                run("W")
             o = a(bank, 128, 192)
             conv(o, "E64", every("G4" + s, 1024 * k, 1024 * k + 1024), False, True,
-                 [(o, a("ID"), h("p4", 64 * k, 64 * k + 64), True, False), (o, a("ID"), a("j16", 64 * k, 64 * k + 64), False, False)])
+                 [(o, a("ID"), h("p4", 64 * k, 64 * k + 64), True, False), (o, a("ID"), a("j16", 64 * k, 64 * k + 64), False, False)]
+                 + [(a(bank, 128 + 32 * j, 160 + 32 * j), a("ID64"), out, False, False) for j in range(1 - k, 2)])
             if k == 0:
                 aff(n32("tA", F, 64), o)
         i5 = ts(n32("i5", I), tt(n32("i5a", I), fo, a("m17"), MUL), 4, SHR)
-        f19 = tt(n32("f19"), tt(n32("f21"), a("b6", 32, 64), a("m613"), MUL), i5, ADD)
+        f19 = tt(h("r2", 0, 32), tt(n32("f21"), a("b6", 32, 64), a("m613"), MUL), i5, ADD)
 
         def place(n, p, c, rest):
-            v = tt(n32(n + "b", I), tt(n32(n + "a"), p, c, MUL), rest, ADD)
-            return ts(n32(n, U), ts(n32(n + "c", I), v, 4095, AND), 16.0, ADD)
+            v = tt(n32(n + "b", I, p[2]), tt(n32(n + "a", F, p[2]), p, c, MUL), rest, ADD)
+            return ts(n32(n, U, p[2]), ts(n32(n + "c", I, p[2]), v, 4095, AND), 16.0, ADD)
 
         Do = tt(n32("Do", B, 512), ind(a("W"), place("uo", d, f20, f19)), Zq, MAX)
+        run("W")
         mm(a("b4"), es("E2n", 0), Do, False, False)
         tt(n32("tk", F, 64), h("tA"), a("b7", 128, 192), MIN)
-        pn = ts(n32("pn", I), tt(n32("kI", I), h("tk", 0, 32), h("tk", 32, 64), MIN), 15, AND)
-        Dn = tt(n32("Dn", B, 512), ind(a("W"), place("un", pn, f20, f19)), Zq, MAX)
-        mm(a("b4"), es("E2", 0), Dn, False, True)
+        n32("kI", I, 64)
+        for k in range(2):
+            tt(h("kI", 32 * k, 32 * k + 32), h("tk", 0, 32), h("tk", 32, 64), MIN)
+        place("un", ts(n32("pn", I, 64), h("kI"), 15, AND), h("c5", 0, 64), h("r2"))
+        Dn = tt(n32("Dn", B, 512), ind(a("W"), h("un", 0, 32)), Zq, MAX)
+        mm(a("b4"), es("E2", 0), Dn, False, not YV)
         aff(n32("hiT", B, 512), a("b4"), odd, on="S")
-        yv = tt(n32("yv", B, 512), a("b4"), h("hiT"), SUB)
+        if YV:
+            mm(a("b4"), a("IDn"), h("hiT"), False, True)
+            yv = aff(n32("yv", B, 512), a("b4"), on="S")
+        else:
+            yv = tt(n32("yv", B, 512), a("b4"), h("hiT"), SUB)
+        cp(n32("LSh", H, 256), a(LS, 16))
+        mms([(a("b7", 256 + 128 * k, 384 + 128 * k), h("LSh", 128 * k, 128 * k + 128), a("IDh"), True, True) for k in range(2)])
+        aff(n32("LMT", F, 256), a("b7", 256, 512), on="S")
+        mms([(a("b7", 192 + 8 * k, 200 + 8 * k), a("onS", par + 256 * k, 256 * k + 256, 2), a("G8n" if par else "G8"), True, True) for k in range(2)])
+        aff(n32("room", F, 16), a("b7", 192, 208), -1.0, 15.5, on="S", f=AF.Sign)
+        if t < 2:
+            aff(n32("c15", F, 16), a("b7", 192, 208), -1024.0, 15360.0 + 0.5 * t, on="S")
+        for k in range(2):
+            o, on = a("b7", 256 + 128 * k, 384 + 128 * k), a("onS", par + 256 * k, 256 * k + 256, 2)
+            mms([(o, a("ones"), a("k0"), True, False), (o, on, a("Shn" if par else "Sh"), False, False), (o, on, a("ID" if par else "IDn"), False, True)])
+        aff(n32("mkT", B, 256), a("b7", 256, 512), on="S")
         cp(ind(a("WK" + s), uP), yv)
         for k in range(2):
             mms([(a("b5", 256 * k + q, 256 * k + 256, 16), a("WK" + s, 512 + 2048 * k + q, 2560 + 2048 * k, 16), a("WAB"), True, True) for q in range(16)])
-        pk = aff(n32("pk", B, 512), ind(a("W"), place("up", pn, c1, X2)))
-        dm = tt(h("gs"), tt(n32("dm1"), tt(n32("dm0"), pn, d, SUB), flag, MUL), d, ADD)
+        pk = aff(n32("pk", B, 512), ind(a("W"), h("un", 32, 64)))
+        dm = cp(h("gs"), h("pn", 0, 32))
         if t < 2:
             send(dn, dm, h("gl"), "ag%d" % (t + 1), "lg%d" % (t + 1), up)
         if t:
-            members(t, par, t == 1, True)
+            keys = members(TB, par, t == 1, True, ONGN[t])
         if t == 1:
-            members(1, 0, True, False)
-            for p2 in range(2):
-                elect(2, p2)
-        mm(a("b3", 256, 512), a("Bro2"), a(TB, 1 + par, 513, 2))
-        aff(n32("am", F, 256), a(LS, 16), 1.0, -1.0)
-        aff(n32("a37", F, 256), a(LS, 16), 2.0, 35.0)
+            elect(2, 1, keys)
+        o, dv = a("b3", 256, 512), a(TB, 1 + par, 513, 2)
+        mms([(o, a("IDh"), a("x17%d" % par), True, False), (o, a("B32"), dv, False, True)])
+        aff(n32("am", F, 256), a(LS, 16), 1.0, -1.0, on="S")
         n32("lI", I, 1024)
-        tt(h("lI", 0, 256), h("am"), a("x17%d" % par), MUL)
+        tt(h("lI", 0, 256), o, h("am"), MUL)
         ts(h("lI", 256, 512), h("lI", 0, 256), 4, SHR)
-        tt(a("b3", 256, 512), a("b3", 256, 512), h("a37"), MUL)
-        tt(n32("s1", F, 256), a("b3", 256, 512), h("lI", 256, 512), ADD)
+        mm(o, a("B37"), dv)
+        tt(n32("s1", F, 256), o, h("lI", 256, 512), ADD)
         n32("offM", U, 256)
         for k in range(2):
             lo, hi = 128 * k, 128 * k + 128
@@ -435,13 +486,15 @@ def rank_program(g, core, T, topo):
             ts(h("lI", 768 + lo, 768 + hi), h("lI", 512 + lo, 512 + hi), -2147479553, AND)
             ts(h("offM", lo, hi), h("lI", 768 + lo, 768 + hi), 16.0, ADD)
             for ch in range(4 * k, 4 * k + 4):
-                aff(h("GL", 512 + 512 * ch, 1024 + 512 * ch), ind(a("W"), h("offM", 32 * ch, 32 * ch + 32)))
+                aff(h("GL", 512 + 512 * ch, 1024 + 512 * ch), ind(a("W"), h("offM", 32 * ch, 32 * ch + 32)), on=ONGL[t])
+                run("GL")
         cp(ind(h("GL"), uP), pk)
         for ch in range(4):
             scan(h("sc", 1024 * ch, 1024 * ch + 1024), a("mask"), h("GL", 512 + 1024 * ch, 1536 + 1024 * ch), MUL, MAX)
+            run("sc")
         o = a("b3", 0, 256)
-        mms([(o, a("ID"), a("half"), True, False), (o, a("ID"), a(zt, 16), False, False), (o, a("ID"), h("sc", 15, 4096, 16), False, True)])
-        aff(n32("zf", F, 256), o, 0.5, 12582912.0, on="S")
+        mms([(o, a("ID"), a(zt, 16), True, False), (o, a("ID"), h("sc", 15, 4096, 16), False, True)])
+        aff(n32("zf", F, 256), o, 0.4995, 12582912.0, on="S")
         aff(h("zs"), h("zf"), 1.0, -12582912.0)
         send((rank + 1 + t) % N, h("zs"), a("z%d" % (t + 1), 16), "az" + s, "lz" + s, (rank - 1 - t) % N)
         n32("kw", F, 512)
@@ -453,7 +506,7 @@ def rank_program(g, core, T, topo):
         t1 = ts(n32("t1", I, 16), kA, 224, AND)
         cI = ts(n32("cI", I, 16), kB, 1, SHR, 31, AND)
         t2 = ts(n32("t2", I, 16), kB, 3, SHR, 24, AND)
-        gh = tt(n32("gh", B, 16), ts(n32("g1", F, 16), t1, 128.0, GE), inj, MUL)
+        gh = tt(n32("gh", B, 16), ts(n32("g1", I, 16), kA, 128, AND), inj, MUL)
         mms([(a("b6", 192, 208), a("TRI"), gh, True, False), (a("b6", 200, 208), a("ones"), h("gh", 0, 8), False, True)])
         rt = tt(n32("rt", B, 512), ind(cI, a("o32")), a("x32"), EQ)
         q8 = tt(n32("q8", F, 16), t1, t2, ADD)
@@ -467,40 +520,40 @@ def rank_program(g, core, T, topo):
         o1 = tt(n32("o1", F, 16), ts(n32("o4", F, 16), t1, 4.0, MUL, 1.0, ADD), lI, ADD)
         tt(n32("test", B, 256), ind(o1, a("o16")), h("LMT"), EQ)
         scan(n32("inl", B, 256), a("mask", 0, 256), h("test"), MUL, MAX)
-        loc = tt(n32("loc1", F, 16), tt(n32("loc0", F, 16), inj, gh, SUB), h("room"), MUL)
+        loc = tt(n32("loc1", F, 16), tt(n32("loc0", F, 16), inj, gh, GT), h("room"), MUL)
         jf = tt(n32("jf", F, 16), loc, h("inl", 15, 256, 16), GT)
         if t < 2:
-            n32("jk", F, 32)
             pb = ts(n32("pb", I, 16), kB, 1, SHR, 1, AND)
-            nn = ts(n32("nn", I, 16), kA, 31, AND)
-            hi0 = tt(n32("hi1", F, 16), ts(n32("hi0", F, 16), nn, 16.0, MUL, 1.0, ADD), h("c15"), ADD)
-            aff(h("jk", 16, 32), o1, 1.0, float(t))
-            tt(h("jk", 0, 16), tt(n32("jp", F, 16), jf, pb, GT if t else MUL), hi0, MUL)
-            tt(n32("jx", H, 256), ind(h("jk"), a("oMT")), a("MK2"), MUL)
-            o = a("b6", 224, 240)
-            mms([(o, a("ID"), a("cm"), True, False), (o, h("jx", 0, 128), a("R2a"), False, False), (o, h("jx", 128, 256), a("R2b"), False, True)])
-            k2 = a("key%d" % (t + 1), par, 32, 2)
-            tt(k2, o, k2, MAX)
+            nn = ts(n32("nm", F, 16), ts(n32("nn", I, 16), kA, 31, AND), 16384.0, MUL)
+            jk = tt(n32("jk", F, 16), tt(n32("j1", F, 16), nn, h("c15"), ADD), aff(n32("j2", F, 16), o1, 0.5), ADD)
+            k2 = a("key%d" % (t + 1), 16 * par, 16 * par + 16)
+            tt(k2, tt(n32("j3", F, 16), tt(n32("jp", F, 16), jf, pb, GT if t else MUL), jk, MUL), k2, MAX)
         tt(n32("dl", H, 256), ind(tt(n32("jv", F, 16), jf, o1, MUL), a("o16")), h("mkT"), MUL)
-        mms([(a("b7", 256 + 128 * k, 384 + 128 * k), h("dl", 128 * k, 128 * k + 128), a("IDh"), True, True) for k in range(2)])
+        o = a("b7", 256, 512)
+        mms([(o, a("IDh"), h("LSh"), True, False)]
+            + [(a("b7", 256 + 128 * k, 384 + 128 * k), h("dl", 128 * k, 128 * k + 128), a("IDh"), False, k == 1) for k in range(2)])
         if t == 0:
-            tt(a(LS, 16), a("b7", 256, 512), a(LS, 16), ADD)
-            ts(a("onS", 0, 512, 2), a(LS, 16), 1.0, MIN)
-            cp(a("off0"), a(LS, 16))
+            aff(a("onS", 0, 512, 2), o, on="S", f=AF.Sign)
+            cp(a("off0"), o)
+            aff(a(LS, 16), o, on="S")
             new("ky", 512, F)
         else:
-            tt(a("ky", par, 512, 2), a("b7", 256, 512), h("am"), ADD)
+            aff(a("ky", par, 512, 2), o, 1.0, -1.0)
         if t < 2:
             mm(a("b6", 208, 224), a("ones"), inj)
-            o, i_ = n32("c0", F, 16), a("b6", 208, 224)
-            vec(h("c0", 0, 1), [i_], lambda e, o=h("c0", 0, 1), i_=i_: e.tensor_reduce(o[0], i_[0], axis=AxisListType.X, op=ADD))
-            n32("cJ", I, 16)
-            cp(h("cJ", 0, 1), h("c0", 0, 1))
-            ts(h("cJ", 1, 2), h("cJ", 0, 1), 31, AND)
-            ts(h("c0", 1, 2), h("cJ", 1, 2), 4096.0, MUL)
-            aff(new("thK%d" % (t + 1), 16, F), a("thK0"), 1.0, h("c0", 1, 2))
+            n32("c0", F, 32)
+            o, i_, c = h("c0", 16, 32), a("b6", 208, 224), h("c0", 0, 1)
+            acc = spans(o, [i_]) + [(c[1][0], True)]
+            step({"S": (100, [(acc, lambda e, o=o, i_=i_, c=c: e.activation(o[0], i_[0], AF.Copy, bias=0.0, scale=128.0, accum_out=c[0]))])}, acc)
+            v = aff(h("c0", 2, 3), aff(h("c0", 1, 2), c, 1.0 / 32, -0.484375, on="S"), 1.0, 12582912.0, on="S")
+            v = aff(h("c0", 4, 5), aff(h("c0", 3, 4), v, 1.0, -12582912.0, on="S"), -131072.0, on="S")
+            aff(new("thK%d" % (t + 1), 16, F), a("thK0"), 1.0, aff(h("c0", 5, 6), c, 4096.0, v, on="S"), on="S")
             v = ts(n32("gv1", I), tt(n32("gv0", I), h("gl"), h("hs"), ADD), 15, AND)
             ghosts(t + 1, cp(n32("gv2", B), v))
+        if t == 0:
+            mms(sum(sizes(), []))
+            aff(a("TK", 1, 513), a("b0"))
+            elect(2, 0, members("TK", 0, True, False, ONGN[1]))
         v = ts(n32("dv1", I), tt(n32("dv0", I), dm, h("hl"), ADD), 15, AND)
         if t < 2:
             cp(new("d%d" % (t + 1), 32, B), v)
@@ -513,55 +566,90 @@ def rank_program(g, core, T, topo):
 
     if "order" not in PLAN:
         PLAN["order"] = arrange(steps)
+        PLAN["tiles"], PLAN["steps"] = tiles, steps
     issue(g, core, T, topo, eng, steps, PLAN["order"])
 
 
 def arrange(steps):
-    hist, last, deps = {}, {}, []
+    hist, last, deps, soft, after = {}, {}, [], [], []
     for k, s in enumerate(steps):
         d = set()
         for (n, lo, hi), w in s["acc"]:
             d.update(j for l2, h2, w2, j in hist.get(n, []) if lo < h2 and l2 < hi and (w or w2))
-            if n in BANKS and "P" in s["alts"] and n in last:
+            if n in OPEN and "P" in s["alts"] and n in last:
                 d.add(last[n])
         for (n, lo, hi), w in s["acc"]:
             hist[n] = [e for e in hist.get(n, []) if not (w and lo <= e[0] and e[1] <= hi)] + [(lo, hi, w, k)]
-            if n in BANKS and "P" in s["alts"]:
+            if n in OPEN and "P" in s["alts"]:
                 last[n] = k
         d.discard(k)
-        deps.append(d)
-    seen = []
+        before = {last[s["run"]]} - d if s["run"] in last else set()
+        soft.append(before if len(s["alts"]) == 1 else set())
+        after.append(before - soft[k])
+        if s["run"]:
+            last[s["run"]] = k
+        deps.append(d | soft[k])
+    n = len(steps)
+    cost = [{q: c for q, (c, _) in s["alts"].items()} for s in steps]
+    late = [s["late"] for s in steps]
+    cost[[s["kind"] for s in steps].index("send")]["G"] += FIRST
+    free = 0.0
     for k, s in enumerate(steps):
         if s["kind"] == "dma":
-            s["late"] += DMA0
-        if s["kind"] == "send" and not seen:
-            seen.append(k)
-            s["late"] += FIRST
-    way = [0.0] * len(steps)
-    for k in reversed(range(len(steps))):
-        way[k] += min(c for c, _ in steps[k]["alts"].values()) + steps[k]["late"] + WAIT
+            if deps[k] == soft[k]:
+                free += late[k]
+                late[k] = free
+            late[k] += DMA0
+    users = [set() for _ in steps]
+    for k in range(n):
         for j in deps[k]:
-            way[j] = max(way[j], way[k])
-    busy, bank, at, end, free = {q: [] for q in "VSPGD"}, {b: [] for b in BANKS}, {}, {}, [0.0]
-    for k in sorted(range(len(steps)), key=lambda k: (-way[k], k)):
-        s, best = steps[k], None
-        bs = {n for (n, _, _), _ in s["acc"] if n in BANKS}
-        for q, (c, _) in s["alts"].items():
-            t = max([0.0] + [end[j] + (0 if at[j][1] == q == "P" else WAIT) - (steps[j]["late"] if at[j][1] == q == "P" else 0) for j in deps[k]])
-            taken = busy[q] + [(u - WAIT - s["late"], v + WAIT) for b in bs for u, v, q2 in bank[b] if q2 != q]
-            for u, v in sorted(taken):
-                if u < t + c and t < v:
-                    t = v
-            if best is None or t + c < best[0] + best[2]:
-                best = (t, q, c)
-        t, q, c = best
-        busy[q].append((t, t + c))
-        at[k], end[k] = (t, q), t + c + s["late"]
-        if s["kind"] == "dma":
-            end[k] = max(end[k], free[0] + s["late"] - DMA0)
-            free[0] = end[k]
-        for b in bs:
-            bank[b].append((t, end[k], q))
+            users[j].add(k)
+    banks = [{b for (b, _, _), _ in s["acc"] if b in BANKS} for s in steps]
+
+    way = [0.0] * n
+    for k in reversed(range(n)):
+        way[k] += min(cost[k].values()) + late[k] + WAIT + MORE.get(steps[k]["name"], 0)
+        for j in deps[k]:
+            way[j] = max(way[j], way[k] - (late[j] + WAIT if j in soft[k] else 0))
+        for j in after[k]:
+            way[j] = max(way[j], way[k] - WAIT - min(cost[j].values()) / 2)
+    at, end, free, bank = {}, {}, {q: 0.0 for q in "VSPGD"}, {b: {} for b in BANKS}
+    left = [len(d) for d in deps]
+    front = {k: 0.0 for k in range(n) if not left[k]}
+    while front:
+        cand = {q: [] for q in free}
+        for k, u in front.items():
+            for q in cost[k]:
+                cand[q].append((max([u, free[q]] + [v for b in banks[k] for q2, v in bank[b].items() if q2 != q]), k))
+        t, q = min((min(c)[0], q) for q, c in cand.items() if c)
+        rivals = [(u, k) for u, k in cand[q] if u > t]
+        for j, u in front.items():
+            if q not in cost[j]:
+                for k in users[j]:
+                    if left[k] == 1 and q in cost[k]:
+                        rivals.append((max(u, free[min(cost[j])]) + min(cost[j].values()) + late[j] + WAIT, k))
+        pick = None
+        for u, k in sorted((c for c in cand[q] if c[0] <= t), key=lambda c: -way[c[1]]):
+            c = cost[k][q]
+            over = [t + c - v - FILL * (v - t) - HOLD for v, j in rivals if way[j] > way[k] and way[j] - way[k] > t + c - v]
+            if q == "V" and "S" in cost[k] and max(free["S"], t) + cost[k]["S"] < t + c + SPARE and not (c > 400 and free["S"] > t):
+                continue
+            if max(over + [0]) <= 0:
+                pick = k
+                break
+        if pick is None:
+            free[q] = min([u for u, k in rivals if u > t] + [t + 200])
+            continue
+        c = cost[pick][q]
+        at[pick], free[q], end[pick] = (t, q), t + c, t + c + late[pick]
+        for b in banks[pick]:
+            bank[b][q] = end[pick] + WAIT
+        del front[pick]
+        for k in users[pick]:
+            left[k] -= 1
+            if not left[k]:
+                front[k] = max(end[j] - late[j] if j in soft[k] or (at[j][1] == "P" and "P" in cost[k]) else end[j] + WAIT for j in deps[k])
+    PLAN["bound"], PLAN["end"] = max(way), max(end.values())
     return [(k, at[k][1]) for k in sorted(at, key=lambda k: (at[k][0], k))]
 
 

@@ -1,25 +1,31 @@
-from concourse.mybir import AluOpType, ActivationFunctionType, AxisListType
+import math
+from concourse.mybir import AluOpType, ActivationFunctionType
 
 F, B, H, I, U = "float32", "bfloat16", "float16", "int32", "uint16"
-POOL = {F: 12288, B: 65536, H: 5120, I: 8192, U: 3072}
+POOL = {F: 10752, B: 36352, H: 4096, I: 8192, U: 3072}
 OWN = {"valI": (32, I), "gI0": (32, I), "z0": (272, B), "z1": (272, B), "z2": (272, B), "z3": (272, B)}
 for _t in range(3):
     for _n in ("gs", "gl", "hs", "hl"):
         OWN[_n + str(_t)] = (32, B)
     OWN["zs%d" % _t] = (256, B)
+    OWN["WK%d" % _t] = (4608, B)
+OWN.update({"W": (4112, B), "GN0": (4096, B), "GN1": (4096, B), "GL": (4608, B), "sc": (4096, B)})
 SCRATCH = {"p" + _d: ("sbuf", [128, _c], _d) for _d, _c in POOL.items()}
 SCRATCH.update({_n: ("sbuf", [128, _c], _d) for _n, (_c, _d) in OWN.items()})
 BANKS = ["b%d" % _b for _b in range(8)]
 SCRATCH.update({_b: ("psum", [128, 512], F) for _b in BANKS})
 SEMAPHORES = ["sV", "sS", "sP", "sG"] + ["d%d" % i for i in range(12)] + [a + str(t) for a in ("az", "ah", "ag", "lz", "lh", "lg") for t in range(3)]
 
-GATHER, SCATTER, LEAST, WAIT, REMOTE, FIRST, DMA0, DMABYTES = 1.56, 3.8, 64, 125, 2400, 2400, 2000, 160.0
-SPARE, FILL, HOLD = 1000, 0.5, 150
-ONGN, ONGL = ("VS", "VS", "VS"), ("S", "S", "S")
+GATHER, SCATTER, LEAST, WAIT, REMOTE, FIRST, DMA0, DMABYTES = 1.56, 3.8, 64, 200, 1900, 2400, 2200, 200.0
+SPARE, FILL, HOLD, PASSES = 300, 1.0, 60, 5
+ONGN, ONGL = ("VS", "VS", "VS"), ("VS", "VS", "VS")
 OPEN = ("b0", "b4")
-MORE = {'Do2/2': 2000, 'inl1/1': -150, 't21/1': 4000, 'pk2/2': -150, 'out1/1': 4000, 'b5@15/2': 1000, 'loc02/2': 1500, 'uO2/2': -150,
-        'p40/0': 4000, 'b6@32/1': -150, 'w2/': 1000, 'eq0/0': 4000, 'b3@0/': 200}
-YV = 0
+MORE = {}
+CUT, OLD = 0.004, False
+RATES, MOVES, HEAT, SEED = ((1.0, 1.56, 3.8), (1.05, 1.2, 2.5), (1.4, 2.0, 5.5)), 60000, 0.0004, 1
+ONS, ONK, ONPK = ("rgb", "rb", "rb"), "VS", "VS"
+SOUT = (F, B, H, I, U)
+BIG = ("TB0",)
 PLAN = {}
 
 
@@ -42,6 +48,8 @@ def rank_program(g, core, T, topo):
         tiles[n] = (n, 0, 512, F)
 
     def new(n, c, d):
+        if n in OWN:
+            return a(n)
         tiles[n] = ("p" + d, top[d], c, d)
         top[d] += -(-c // 16) * 16
         assert top[d] <= POOL[d], (d, top)
@@ -68,8 +76,9 @@ def rank_program(g, core, T, topo):
             return r + [(o[1][0], True), (o[1][1], False)]
         return r + [(o[1][0], True)]
 
-    def step(alts, acc, late=0, kind=None):
-        steps.append({"alts": alts, "acc": acc, "late": late, "kind": kind, "run": None, "name": named.get(acc[-1][0], named.get(acc[0][0])) + now[0]})
+    def step(alts, acc, late=0, kind=None, o=None, ins=()):
+        gather = any(v is not None and not isinstance(v, (int, float)) and v[4] == "I" for v in ins)
+        steps.append({"n": (o[2] if gather else 0, o[2] if o and o[4] == "I" else 0), "alts": alts, "acc": acc, "late": late, "kind": kind, "run": None, "name": named.get(acc[-1][0], named.get(acc[0][0])) + now[0]})
 
     def run(name):
         steps[-1]["run"] = name
@@ -86,10 +95,12 @@ def rank_program(g, core, T, topo):
 
     def vec(o, ins, call, two=False):
         acc = spans(o, ins)
-        step({"V": (vcost(o, ins, two), [(acc, call)])}, acc)
+        step({"V": (vcost(o, ins, two), [(acc, call)])}, acc, o=o, ins=ins)
 
     def ts(o, i, s1, op0, s2=None, op1=None):
-        if op1 is None:
+        if o[3] in SOUT and (op0, op1) in ((ADD, None), (MUL, None), (MUL, ADD)):
+            aff(o, i, *((1.0, s1) if op0 == ADD else (s1, s2 or 0.0)))
+        elif op1 is None:
             vec(o, [i, s1], lambda e: e.tensor_scalar(o[0], i[0], x(s1), None, op0))
         else:
             vec(o, [i, s1, s2], lambda e: e.tensor_scalar(o[0], i[0], x(s1), x(s2), op0, op1))
@@ -100,6 +111,8 @@ def rank_program(g, core, T, topo):
         return o
 
     def cp(o, i):
+        if o[3] in SOUT and o[4] != "I":
+            return aff(o, i)
         vec(o, [i], lambda e: e.tensor_copy(o[0], i[0]))
         return o
 
@@ -111,8 +124,10 @@ def rank_program(g, core, T, topo):
         vec(o, [d0, d1], lambda e: e.tensor_tensor_scan(o[0], d0[0], d1[0], 0.0, op0, op1))
         return o
 
-    def aff(o, i, scale=1.0, bias=0.0, on="VS", f=None):
+    def aff(o, i, scale=1.0, bias=0.0, on="VS", f=None, v=None):
         acc, alts = spans(o, [i, scale, bias]), {}
+        if v is not None:
+            alts["V"], on = (vcost(o, [i]), [(acc, lambda e: e.tensor_scalar(o[0], i[0], *v))]), "S"
         plain = scale == 1.0 and bias == 0.0
         if "V" in on and f is None:
             if plain:
@@ -123,12 +138,12 @@ def rank_program(g, core, T, topo):
             fn = f if f is not None else AF.Copy if bias == 0.0 else AF.Identity
             c = 80 + GATHER * o[2] if i[4] == "I" else max(LEAST, o[2])
             alts["S"] = (c, [(acc, lambda e: e.activation(o[0], i[0], fn, bias=x(bias), scale=x(scale)))])
-        step(alts, acc)
+        step(alts, acc, o=o, ins=[i])
         return o
 
     def mms(calls):
         sub = [(spans(o, [l, r]), lambda e, o=o, l=l, r=r, s0=s0, s1=s1: e.matmul(o[0], l[0], r[0], s0, s1)) for o, l, r, s0, s1 in calls]
-        step({"P": (sum(max(64, c[2][2]) for c in calls), sub)}, [s for u in sub for s in u[0]], late=60)
+        step({"P": (sum(max(64, c[2][2]) for c in calls), sub)}, [s for u in sub for s in u[0]], late=40)
 
     def mm(o, l, r, start=True, stop=True):
         mms([(o, l, r, start, stop)])
@@ -136,6 +151,7 @@ def rank_program(g, core, T, topo):
     def iota(o, pat, base=0, cm=0):
         acc = spans(o, [])
         step({"G": (160 + 2 * o[2], [(acc, lambda e: e.iota(o[0], pat, base, cm, allow_small_or_imprecise_dtypes=True))])}, acc)
+        run("G")
         return o
 
     def dma(q, out, in_, acc, size):
@@ -143,7 +159,7 @@ def rank_program(g, core, T, topo):
         run(q)
 
     def send(dst, buf, rbuf, arr, loc, src):
-        step({"G": (400, [(buf, rbuf, arr, loc, dst, src)])}, [(buf[1][0], False), (rbuf[1][0], True)], late=REMOTE + buf[2], kind="send")
+        step({"G": (400, [(buf, rbuf, arr, loc, dst, src)])}, [(buf[1][0], False), (rbuf[1][0], True)], late=REMOTE + 3 * buf[2], kind="send")
 
     def es(E, q):
         return a(E, 15 - q, 143 - q)
@@ -170,11 +186,23 @@ def rank_program(g, core, T, topo):
     load("D", a("z0", 16), T.zl[:, :])
     new("W", 4112, B)
     load("D", a("W", 16), T.rec[:, :])
-    send(dn, a("valI"), a("gI0"), "ag0", "lg0", up)
 
     new("ci", 16, I)
     iota(col("ci"), [[0, 1]], 0, 1)
     iota(new("X", 256, F), [[1, 256]])
+    iota(new("kpat", 256, B), [[0, 16], [1, 16]])
+    iota(new("x8", 128, B), [[0, 16], [1, 8]])
+    new("pt", 64, F)
+    iota(a("pt", 48, 64), [[16, 2], [1, 8]])
+    iota(new("j16", 128, B), [[16, 4], [0, 32]])
+    send(dn, a("valI"), a("gI0"), "ag0", "lg0", up)
+    run("G")
+    iota(new("x16", 256, B), [[1, 16], [0, 16]])
+    iota(new("gx", 256, F), [[0, 2], [1, 8], [0, 16]])
+    iota(new("Mrow", 512, F), [[1, 32], [32, 16]], 1)
+    iota(a("pt", 32, 48), [[16, 2], [0, 8]])
+    iota(a("pt", 0, 32), [[1, 16], [0, 2]])
+    iota(new("x32", 512, B), [[0, 16], [1, 32]])
     for n, (op, c) in enumerate(((AND, 15), (AND, 112), (SHR, 4), (AND, 7), (AND, 8))):
         ts(col("ci", n + 1), col("ci"), c, op)
     new("cf", 16, F)
@@ -211,24 +239,24 @@ def rank_program(g, core, T, topo):
     new("onS", 512, B)
     for par in range(2):
         gp = a("glI", par, 512, 2)
-        ts(a("onS", par, 512, 2), gp, 0.0, GE, 1.0 - 2 * par, MUL)
+        aff(a("onS", par, 512, 2), gp, 1.0 - 2 * par, 1.0 - 2 * par, f=AF.Sign, v=(0.0, 1.0 - 2 * par, GE, MUL))
         ts(new("off%d" % par, 256, U), gp, 1.0, ADD)
         new("LS%d" % par, 272, F)
         fill(a("LS%d" % par, 0, 16), 0.0)
         ts(a("LS%d" % par, 16), gp, 1.0, ADD)
     cp(new("d0", 32, B), a("valI"))
 
-    def sizes():
-        return [(a("b0"), a("ID"), a("Kc"), True, False)], [(a("b0"), es("E1", 0), a("onS"), False, True)]
+    def sizes(bank, stop):
+        return [(a(bank), a("ID"), a("Kc"), True, False)], [(a(bank), es("E1", 0), a("onS"), False, stop)]
 
     def table(t):
-        if t == 0:
-            mms(sizes()[0])
+        if t < 2:
+            mms(sizes("b0", False)[0])
         if t == 1:
-            mm(a("b0"), a("ID"), a("TK", 1, 513), True, False)
+            mms(sizes("b0", False)[1])
         rows("b0", a("d%d" % t), t == 2, t > 0)
         if t == 0:
-            mms(sizes()[1])
+            mms(sizes("b0", True)[1])
         aff(a("TB%d" % t, 1, 513), a("b0"))
 
     def ghosts(t, src):
@@ -238,8 +266,9 @@ def rank_program(g, core, T, topo):
     def members(tab, par, keys, values, on):
         n = "GN%d" % par
         bank, lo, w = ("b2", 0 if keys else 128, 256) if values else ("b5", 256, 128)
-        for ch in range(8):
-            aff(a(n, 512 * ch, 512 * ch + 512), ind(a(tab, 0, 513), a("off%d" % par, 32 * ch, 32 * ch + 32)), on=on)
+        big = 2 if tab in BIG else 1
+        for ch in range(big - 1, 8, big):
+            aff(a(n, 512 * (ch + 1 - big), 512 * ch + 512), ind(a(tab, 0, 513), a("off%d" % par, 32 * (ch + 1 - big), 32 * ch + 32)), on=on)
             run(tab)
             k = ch // 4
             if ch % 4 == 3:
@@ -247,21 +276,22 @@ def rank_program(g, core, T, topo):
                       a("WKD", 0 if keys else 8, 16 if values else 8), True, True) for q in range(16)])
                 if values:
                     aff(a("dM", 128 * k, 128 * k + 128), a(bank, 256 * k + 128, 256 * k + 256))
-                    mm(a("b3", 128 * k, 128 * k + 128), a("dM", 128 * k, 128 * k + 128), a("ID"))
         return [a(bank, lo + w * k, lo + w * k + 128) for k in range(2)]
 
     def elect(t, par, src):
         for k in range(2):
             lo = 256 * par + 128 * k
             scan(a("ks%d" % t, lo, lo + 128), a("subp" if t & 1 else "addp"), src[k], ADD, MIN if t & 1 else MAX)
-        ts(a("key%d" % t, 16 * par, 16 * par + 16), a("ks%d" % t, 256 * par + 15, 256 * par + 256, 16), -1.0 if t & 1 else 1.0, MUL, 0.0, MAX)
+        sg = -1.0 if t & 1 else 1.0
+        aff(a("key%d" % t, 16 * par, 16 * par + 16), a("ks%d" % t, 256 * par + 15, 256 * par + 256, 16), sg, f=AF.Relu, v=(sg, 0.0, MUL, MAX))
 
     for n, c in (("GN0", 4096), ("GN1", 4096), ("G4", 2048), ("GL", 4608), ("sc", 4096)):
         for t in ("", "0", "1", "2") if n[1] != "N" else ("",):
             tiles[n + t] = tiles[n] if t else new(n, c, B) and tiles[n]
     table(0)
-    iota(new("kpat", 1024, B), [[0, 64], [1, 16]])
-    ts(new("mask", 1024, B), a("kpat"), 1.0, MIN)
+    new("mask", 1024, B)
+    for k in range(4):
+        aff(a("mask", 256 * k, 256 * k + 256), a("kpat"), f=AF.Sign, v=(1.0, None, MIN))
     aff(new("addp", 128, F), a("mask", 0, 128), 4194304.0 + 1024.0, -4194304.0)
     aff(new("subp", 128, F), a("addp"), -1.0)
     for t in range(3):
@@ -272,6 +302,9 @@ def rank_program(g, core, T, topo):
     aff(a("WKD", 0, 8), a("G8"), cc(isr(0), 16384.0, isr(1)))
     aff(a("WKD", 8, 16), a("G8"), isr(2))
     new("dM", 256, B)
+    fill(new("ones", 128, B), 1.0 / 128)
+    fill(new("m37c", 128, B), -37.0)
+    aff(new("ID32", 128, B), a("ID"), 32.0)
     aff(new("TK", 528, B) and col("TK"), isr(2), 0.0)
     keys = [members("TB0", 0, True, True, ONGN[0]), members("TB0", 1, True, False, ONGN[0])]
     for t in range(2):
@@ -282,23 +315,15 @@ def rank_program(g, core, T, topo):
     for n, c in (("m17", 17.0), ("m37", 37.0), ("m613", 613.0)):
         aff(new(n, 32, F), a("mA"), 2.0, c)
     for par in range(2):
-        aff(new("x17%d" % par, 256, H), a("X"), 4.0, 17.0 + 2 * par, on="V")
+        aff(new("x17%d" % par, 256, H), a("X"), 4.0, 17.0 + 2 * par)
         aff(new("x613%d" % par, 256, F), a("X"), 4.0, 613.0 + 2 * par)
-    iota(new("Mrow", 512, F), [[1, 32], [32, 16]], 1)
-    iota(new("gx", 256, F), [[0, 2], [1, 8], [0, 16]])
-    iota(new("x8", 256, B), [[0, 32], [1, 8]])
-    iota(new("x32", 512, B), [[0, 16], [1, 32]])
-    iota(new("j16", 128, B), [[16, 4], [0, 32]])
-    new("pt", 64, F)
-    iota(a("pt", 0, 32), [[1, 16], [0, 2]])
-    iota(a("pt", 32, 48), [[16, 2], [0, 8]])
-    iota(a("pt", 48, 64), [[16, 2], [1, 8]])
     for t in range(3):
         o = new("WK%d" % t, 4608, B)
-        for ch in range(4 if t < 2 else 0):
-            iota(a("WK%d" % t, 512 + 1024 * ch, 1536 + 1024 * ch), [[0, 1024]])
-            run("WK")
-    dma("D", a("WK2", 512)[0], a("WK1", 512)[0], [(a("WK1", 512)[1][0], False), (o[1][0], True)], 128 * 8192)
+        for ch in range(0 if t else 4):
+            iota(a("WK0", 512 + 1024 * ch, 1536 + 1024 * ch), [[0, 1024]])
+        if t:
+            src = a("WK%d" % (t - 1), 512)
+            dma("D", a("WK%d" % t, 512)[0], src[0], [(src[1][0], False), (o[1][0], True)], 128 * 8192)
     cp(new("o16", 16, U), a("X", 0, 16))
     cp(new("o32", 32, U), a("pt", 0, 32))
     ts(new("oML", 16, U), a("pt", 32, 48), r, ADD)
@@ -308,44 +333,57 @@ def rank_program(g, core, T, topo):
     aff(new("Es", 144, B), a("E1"), cc(r, 1.0, 1.0))
     aff(new("E0", 144, B), a("E1"), isr(0))
     cp(new("Eh", 144, H), a("E1"))
+
+    def total(o, parts):
+        p = a("b3", 256, 256 + o[2])
+        mms([(p, a("ID"), v, k == 0, k == len(parts) - 1) for k, v in enumerate(parts)])
+        aff(o, p, on="S")
+
     new("E2", 144, B)
-    tt(a("E2", 8, 144), a("E1", 8, 144), a("E1", 7, 143), ADD)
+    total(a("E2", 8, 144), [a("E1", 8, 144), a("E1", 7, 143)])
     new("E2n", 144, B)
     aff(a("E2n", 8), a("E2", 8), -1.0)
     new("E2h", 144, H)
     cp(a("E2h", 8), a("E2", 8))
-    aff(new("w1", 128, B), es("E2", 2), 49152.0)
-    aff(new("w2", 128, B), es("E1", 4), cc(r, -1.0, 15.0))
-    tt(new("w3", 128, B), a("w1"), a("w2"), ADD)
-    tt(new("Weq", 128, B), a("w3"), es("E1", 6), ADD)
+    aff(new("w1", 128, B), es("E2", 4), 49152.0)
+    aff(new("w2", 128, B), es("E1", 3), cc(r, -1.0, 15.0))
+    total(new("Weq", 128, B), [a("w1"), a("w2"), es("E1", 6)])
     ts(new("B32", 128, B), a("gx", 0, 128), gg, EQ, cc(isr(2), 32.0), MUL)
-    aff(new("B37", 128, B), a("B32"), 37.0 / 32)
     aff(new("ID64", 128, B), a("ID"), 64.0)
     aff(new("IDn", 128, B), a("ID"), -1.0)
-    aff(new("j4", 128, B), a("j16"), 1.0 / 16)
-    aff(new("k0", 128, B), a("mask", 0, 128), -1.0, 1.0)
+    aff(new("k0", 256, B), a("mask", 0, 256), -1.0, 1.0)
     acc = spans(new("Sh", 128, B), [a("mask", 0, 128)])
     step({"G": (460, [(acc, lambda e: e.affine_select(a("Sh")[0], a("mask", 0, 128)[0], [[-1, 128]], EQ, 0.0, 1, 1))])}, acc)
     aff(new("Shn", 128, B), a("Sh"), -1.0)
     cp(new("IDh", 128, H), a("ID"))
-    ts(new("tri", 128, B), a("X", 0, 128), pf, GT, 1.0 / 128, MUL)
-    aff(new("id64", 128, B), a("ID"), -0.5)
-    tt(new("TRI", 128, B), a("tri"), a("id64"), ADD)
-    fill(new("ones", 128, B), 1.0 / 128)
+    if OLD:
+        aff(new("IDz", 128, H), a("ID"), 0.49951171875)
+    ts(new("tri", 128, B), a("X", 0, 128), pf, GT, 8.0, MUL)
+    aff(new("id64", 128, B), a("ID"), -512.0)
+    fill(new("ones8", 128, B), 8.0)
+    fill(new("c46", 16, B), 4608.0)
+    total(new("TRI", 128, B), [a("tri"), a("id64")])
+    aff(new("ID8n", 128, B), a("ID"), -8.0)
+    aff(new("j8", 128, B), a("j16"), 1.0 / 16, -8.0)
     fill(a("W", 0, 16), 0.0)
     aff(new("G8n", 8, B), a("G8"), -1.0)
-    w = cc(isr(4), 256.0, cc(s01, 4096.0))
-    new("WAB", 16, B)
-    aff(a("WAB", 0, 16, 2), a("G8"), cc(isr(2), 0.125, cc(isr(5), 1.0, cc(isr(6), -6144.0, w))))
-    aff(a("WAB", 1, 16, 2), a("G8"), cc(isr(3), 1.0, cc(isr(6), 127.0, w)))
-    odd = cc(isr(1), 1.0, isr(3))
+    w = cc(isr(3), 256.0, cc(s01, 4096.0))
+    new("WAB", 24, B)
+    aff(a("WAB", 0, 16, 2), a("G8"), cc(isr(4), 0.125, cc(isr(7), 1.0, cc(isr(6), -6144.0, w))))
+    aff(a("WAB", 1, 16, 2), a("G8"), cc(isr(5), 1.0, cc(isr(6), 127.0, w)))
+    aff(a("WAB", 16, 24), a("G8"), isr(2))
+    odd = cc(isr(1), 1.0, isr(5))
     ts(new("MK1", 256, B), a("gx"), r7, EQ)
-    ts(new("MK2", 256, B), a("x8"), gg, EQ)
+    ts(new("MK2", 128, B), a("x8"), gg, EQ)
     ts(new("R1", 16, F), a("X", 0, 16), cc(r8, 1.0, gg), EQ)
     aff(new("R1a", 16, B), a("R1"), 262144.0)
     aff(new("R1b", 16, B), a("R1"), 4096.0)
     aff(new("R2", 16, B), a("I16"))
     aff(new("xQ", 256, B), a("kpat", 0, 256), 8.0, 128.0)
+    if OLD or any("g" not in v for v in ONS):
+        new("QT", 272, B)
+        fill(a("QT", 0, 16), 0.0)
+        ts(a("QT", 16), a("x16"), r, EQ)
     ts(new("nbh", 512, H), a("nbI"), 2.0, MUL, -127.0, ADD)
     mms([(a("b1", q, 512, 16), a("IDh"), a("nbh", 32 * q, 32 * q + 32), True, True) for q in range(16)])
     new("th2", 32, I)
@@ -362,7 +400,7 @@ def rank_program(g, core, T, topo):
         LS, TB, zt, d, key = "LS%d" % par, "TB" + s, "z" + s, a("d" + s), a("key" + s)
 
         def n32(n, dt=F, c=32):
-            if t == 2 and c >= 128:
+            if t == 2 and c >= 128 and n + "0" in tiles:
                 tiles[n + s] = tiles[n + "0"]
                 return a(n + s)
             return new(n + s, c, dt)
@@ -377,31 +415,56 @@ def rank_program(g, core, T, topo):
             tt(h("ex", 128 * p2, 128 * p2 + 128), ind(h("i1", 16 * p2, 16 * p2 + 16), a("oMT", 0, 8)), a("MK2", 0, 128), MUL)
             mm(a("b6", 224 + p2, 256, 2), h("ex", 128 * p2, 128 * p2 + 128), a("R2"))
         i1 = a("b6", 224, 256)
-        uE = ts(n32("uE", U), i1, 2.0, MUL, par - 1.0, ADD)
         uZ = ts(n32("uZ", U), i1, 15.0, ADD)
-        mms([(a("b6", 256, 384), a("ID"), a("j4"), True, False)] + [(a("b6", 256 + 32 * j, 288 + 32 * j), a("ID"), d, False, j == 3) for j in range(4)])
-        n32("pI", I, 256)
-        cp(h("pI", 0, 128), a("b6", 256, 384))
-        cp(n32("p4", B, 128), ts(h("pI", 128, 256), h("pI", 0, 128), 15, AND))
-        aff(n32("gr", B, 512), ind(a(TB, 0, 513), uE))
-        conv(a("b6", 0, 32), "Ed", every("gr" + s, 0, 512))
-        Zq = aff(n32("Zq", B, 512), ind(a(zt), uZ))
+        if "g" in ONS[t]:
+            uE = ts(n32("uE", U), i1, 2.0, MUL, par - 1.0, ADD)
+        else:
+            uE = cp(n32("uE", U), ts(n32("vc", I), ts(n32("vI", I), i1, 2.0, MUL, par - 2.0, ADD), 31, AND))
+            row = aff(n32("row", B, 512), ind(a("QT"), uZ), on="S")
+        n32("sg", B, 128)
+        for j in range(4):
+            aff(h("sg", 32 * j, 32 * j + 32), d, 1.0, j - 15.5, on="S", f=AF.Sign)
+        o = a("b4", 256, 384)
+        mms([(o, a("ID"), a("j8"), True, False)] + [(a("b4", 256 + 32 * j, 288 + 32 * j), a("ID"), d, False, False) for j in range(4)]
+            + [(o, a("ID8n"), h("sg"), False, True)])
+        aff(n32("p4", B, 128), o, on="S")
+        if "g" in ONS[t]:
+            aff(n32("gr", B, 512), ind(a(TB, 0, 513), uE))
+            conv(a("b6", 0, 32), "Ed", every("gr" + s, 0, 512))
+        else:
+            tt(n32("gr", B, 512), ind(a("dv1%d" % (t - 1) if t else "valI"), uE), row, MUL)
+            conv(a("b6", 0, 32), "E1", every("gr" + s, 0, 512))
+        Zq = aff(n32("Zq", B, 512), ind(a(zt), uZ), on=ONPK)
         eq = tt(n32("eq", B, 512), ind(a(LS), uZ), a("Mrow"), EQ)
         prod = tt(n32("prod", H, 512), a("b1"), eq, MUL)
         conv(a("b7", 64, 96), "Eh", every("prod" + s, 0, 512))
         conv(a("b7", 96, 128), "Es", every("eq" + s, 0, 512))
-        mms([(a("b4"), a("Weq"), eq, True, False), (a("b4"), es("E2h", 2), prod, False, False)])
+        halves = [(a(b, 0, 256), 256 * k, 256 * k + 256) for k, b in enumerate(("b4", "b0"))]
+        for o, lo, hi in halves:
+            mms([(o, a("Weq"), h("eq", lo, hi), True, False), (o, es("E2h", 4), h("prod", lo, hi), False, False)])
         f17 = aff(n32("f17"), i1, 4.0, 13.0 + 2 * par)
         n32("c5", F, 160)
         for j in range(4):
             aff(h("c5", 32 * j + 32, 32 * j + 64), f17, 1.0, 596.0, on="S")
-        base = ts(n32("base", I), tt(n32("b0_", I), f17, a("mA"), MUL), 4, SHR)
+
+        def by16(n, i, j):
+            return aff(n32(n, I), tt(n32(n + "_", I), i, j, MUL), 0.0625, -0.46875, f=AF.Identity, v=(4, None, SHR))
+
+        base = by16("base", f17, a("mA"))
         tt(n32("t4", F, 128), h("p4"), h("c5", 32), MUL)
         n32("r2", F, 64)
-        X2 = tt(h("r2", 32), tt(n32("X1"), a("b6", 0, 32), a("m37"), MUL), base, ADD)
+        X1 = tt(n32("X1"), a("b6", 0, 32), a("m37"), MUL)
+        X2 = tt(h("r2", 32), X1, base, ADD)
         n32("P4", I, 256)
+        if "b" in ONS[t]:
+            n32("t5", F, 128)
+            for j in range(4):
+                tt(h("t5", 32 * j, 32 * j + 32), h("t4", 32 * j, 32 * j + 32), base, ADD)
         for j in range(4):
-            tt(h("P4", 32 * j, 32 * j + 32), h("t4", 32 * j, 32 * j + 32), X2, ADD)
+            if "b" in ONS[t]:
+                tt(h("P4", 32 * j, 32 * j + 32), h("t5", 32 * j, 32 * j + 32), X1, ADD)
+            else:
+                tt(h("P4", 32 * j, 32 * j + 32), h("t4", 32 * j, 32 * j + 32), X2, ADD)
         ts(h("P4", 128, 256), h("P4", 0, 128), 4095, AND)
         ts(n32("u4", U, 128), h("P4", 128, 256), 16.0, ADD)
         uO = ts(n32("uO", U), a("b7", 64, 96), 0.5, MUL, 64.5, ADD)
@@ -413,8 +476,8 @@ def rank_program(g, core, T, topo):
         uP = cp(n32("uP", U), pos)
         gr2 = aff(n32("gr2", B, 512), ind(a(TB, 0, 1025), uO), on="S", f=AF.Abs)
         conv(a("b6", 32, 64), "Ed", every("gr2" + s, 0, 512))
-        if t < 2:
-            mm(a("b4"), es("E0", 5), gr2, False, False)
+        for o, lo, hi in halves if t < 2 else ():
+            mm(o, es("E0", 7), h("gr2", lo, hi), False, False)
         for k, bank in enumerate(("b6", "b7")):
             for j in (2 * k, 2 * k + 1):
                 tt(h("G4", 512 * j, 512 * j + 512), ind(a("W"), h("u4", 32 * j, 32 * j + 32)), Zq, MAX)
@@ -425,7 +488,7 @@ def rank_program(g, core, T, topo):
                  + [(a(bank, 128 + 32 * j, 160 + 32 * j), a("ID64"), out, False, False) for j in range(1 - k, 2)])
             if k == 0:
                 aff(n32("tA", F, 64), o)
-        i5 = ts(n32("i5", I), tt(n32("i5a", I), fo, a("m17"), MUL), 4, SHR)
+        i5 = by16("i5", fo, a("m17"))
         f19 = tt(h("r2", 0, 32), tt(n32("f21"), a("b6", 32, 64), a("m613"), MUL), i5, ADD)
 
         def place(n, p, c, rest):
@@ -434,101 +497,141 @@ def rank_program(g, core, T, topo):
 
         Do = tt(n32("Do", B, 512), ind(a("W"), place("uo", d, f20, f19)), Zq, MAX)
         run("W")
-        mm(a("b4"), es("E2n", 0), Do, False, False)
+        for o, lo, hi in halves:
+            mm(o, es("E2n", 0), h("Do", lo, hi), False, False)
         tt(n32("tk", F, 64), h("tA"), a("b7", 128, 192), MIN)
-        n32("kI", I, 64)
-        for k in range(2):
-            tt(h("kI", 32 * k, 32 * k + 32), h("tk", 0, 32), h("tk", 32, 64), MIN)
-        place("un", ts(n32("pn", I, 64), h("kI"), 15, AND), h("c5", 0, 64), h("r2"))
-        Dn = tt(n32("Dn", B, 512), ind(a("W"), h("un", 0, 32)), Zq, MAX)
-        mm(a("b4"), es("E2", 0), Dn, False, not YV)
-        aff(n32("hiT", B, 512), a("b4"), odd, on="S")
-        if YV:
-            mm(a("b4"), a("IDn"), h("hiT"), False, True)
-            yv = aff(n32("yv", B, 512), a("b4"), on="S")
-        else:
-            yv = tt(n32("yv", B, 512), a("b4"), h("hiT"), SUB)
-        cp(n32("LSh", H, 256), a(LS, 16))
-        mms([(a("b7", 256 + 128 * k, 384 + 128 * k), h("LSh", 128 * k, 128 * k + 128), a("IDh"), True, True) for k in range(2)])
-        aff(n32("LMT", F, 256), a("b7", 256, 512), on="S")
-        mms([(a("b7", 192 + 8 * k, 200 + 8 * k), a("onS", par + 256 * k, 256 * k + 256, 2), a("G8n" if par else "G8"), True, True) for k in range(2)])
-        aff(n32("room", F, 16), a("b7", 192, 208), -1.0, 15.5, on="S", f=AF.Sign)
-        if t < 2:
-            aff(n32("c15", F, 16), a("b7", 192, 208), -1024.0, 15360.0 + 0.5 * t, on="S")
-        for k in range(2):
-            o, on = a("b7", 256 + 128 * k, 384 + 128 * k), a("onS", par + 256 * k, 256 * k + 256, 2)
-            mms([(o, a("ones"), a("k0"), True, False), (o, on, a("Shn" if par else "Sh"), False, False), (o, on, a("ID" if par else "IDn"), False, True)])
-        aff(n32("mkT", B, 256), a("b7", 256, 512), on="S")
-        cp(ind(a("WK" + s), uP), yv)
-        for k in range(2):
-            mms([(a("b5", 256 * k + q, 256 * k + 256, 16), a("WK" + s, 512 + 2048 * k + q, 2560 + 2048 * k, 16), a("WAB"), True, True) for q in range(16)])
-        pk = aff(n32("pk", B, 512), ind(a("W"), h("un", 32, 64)))
-        dm = cp(h("gs"), h("pn", 0, 32))
-        if t < 2:
-            send(dn, dm, h("gl"), "ag%d" % (t + 1), "lg%d" % (t + 1), up)
+        pn = ts(n32("pn", I), tt(n32("kI", I), h("tk", 0, 32), h("tk", 32, 64), MIN), 15, AND)
+        place("un", pn, f20, f19)
+        for n in ("Dn", "hiT", "yv"):
+            n32(n, B, 512)
+        late = "p" in ONS[t]
+        if late:
+            tt(n32("dp", B), pn, d, SUB)
+        for (o, lo, hi), b in zip(halves, ("b4", "b0")):
+            if late:
+                mms([(a(b, q, 256, 16), a("FH", 128 * q, 128 * q + 128), h("dp", lo // 16, hi // 16), False, False) for q in range(16)])
+            tt(h("Dn", lo, hi), ind(a("W"), h("un", lo // 16, hi // 16)), h("Zq", lo, hi), MAX)
+            mm(o, es("E2", 0), h("Dn", lo, hi), False, True)
+            aff(h("hiT", lo, hi), o, odd, on="S")
+            tt(h("yv", lo, hi), o, h("hiT", lo, hi), SUB)
+            cp(ind(a("WK" + s), h("uP", lo // 16, hi // 16)), h("yv", lo, hi))
         if t:
             keys = members(TB, par, t == 1, True, ONGN[t])
         if t == 1:
             elect(2, 1, keys)
-        o, dv = a("b3", 256, 512), a(TB, 1 + par, 513, 2)
-        mms([(o, a("IDh"), a("x17%d" % par), True, False), (o, a("B32"), dv, False, True)])
-        aff(n32("am", F, 256), a(LS, 16), 1.0, -1.0, on="S")
-        n32("lI", I, 1024)
-        tt(h("lI", 0, 256), o, h("am"), MUL)
-        ts(h("lI", 256, 512), h("lI", 0, 256), 4, SHR)
-        mm(o, a("B37"), dv)
-        tt(n32("s1", F, 256), o, h("lI", 256, 512), ADD)
+        aff(n32("LSh", H, 256), a(LS, 16), on="S")
+        mms([(a("b7", 256 + 128 * k, 384 + 128 * k), h("LSh", 128 * k, 128 * k + 128), a("IDh"), True, True) for k in range(2)])
+        aff(n32("LMT", F, 256), a("b7", 256, 512), on="S")
+        mms([(a("b7", 192 + 8 * k, 200 + 8 * k), a("onS", par + 256 * k, 256 * k + 256, 2), a("G8n" if par else "G8"), True, True) for k in range(2)])
+        if t < 2:
+            n32("c15", F, 48)
+            aff(h("c15", 16, 32), a("b7", 192, 208), 1048576.0, -15728640.0, on="S", f=AF.Relu)
+            aff(h("c15", 32, 48), a("b7", 192, 208), -1024.0, 15360.0 + 0.5 * t, on="S")
+            tt(h("c15", 0, 16), h("c15", 32, 48), h("c15", 16, 32), SUB)
+        for k in range(2):
+            o, on = a("b7", 256 + 128 * k, 384 + 128 * k), a("onS", par + 256 * k, 256 * k + 256, 2)
+            mms([(o, a("ones"), a("k0", 0, 128), True, False), (o, on, a("Shn" if par else "Sh"), False, False), (o, on, a("ID" if par else "IDn"), False, True)])
+        aff(n32("mkT", B, 256), a("b7", 256, 512), on="S")
+        for k, b in enumerate(("b5", "b2")):
+            mms([(a(b, q, 256 + 128 * late, 16), a("WK" + s, 512 + 2048 * k + q, 2560 + 2048 * k, 16), a("WAB", 0, 16 + 8 * late), True, True)
+                 for q in range(16)])
+            o, parts = a("b3", 128 * k, 128 * k + 128), ["dM"]
+            if late:
+                parts.append("dD" + s)
+                aff((k or n32("dD", B, 256)) and h("dD", 128 * k, 128 * k + 128), a(b, 256, 384))
+            mms([(o, a("ones"), a("m37c"), True, False)] + [(o, a(n, 128 * k, 128 * k + 128), a("ID32"), False, n == parts[-1]) for n in parts])
+        if not late:
+            pk = aff(n32("pk", B, 512), ind(a("W"), place("up", pn, h("c5", 32, 64), X2)), on=ONPK)
+        dm = aff(h("gs"), pn, on="S")
+        if t < 2:
+            send(dn, dm, h("gl"), "ag%d" % (t + 1), "lg%d" % (t + 1), up)
+        o = a("b3", 256, 512)
+        mms([(o, a("IDh"), a("x17%d" % par), True, False), (o, a("B32"), a(TB, 1 + par, 513, 2), False, True)])
+        tt(n32("s0", F, 256), o, aff(n32("a37", F, 256), a(LS, 16), 2.0, 35.0, on="S"), MUL)
+        aff(n32("s1", F, 256), h("s0"), 1.0, 22052.0, on="S")
+        n32("lI", I, 512)
         n32("offM", U, 256)
         for k in range(2):
             lo, hi = 128 * k, 128 * k + 128
             tt(a("b3", lo, hi), a("b3", lo, hi), a("x613%d" % par, lo, hi), MUL)
-            tt(h("lI", 512 + lo, 512 + hi), a("b3", lo, hi), h("s1", lo, hi), ADD)
-            ts(h("lI", 768 + lo, 768 + hi), h("lI", 512 + lo, 512 + hi), -2147479553, AND)
-            ts(h("offM", lo, hi), h("lI", 768 + lo, 768 + hi), 16.0, ADD)
-            for ch in range(4 * k, 4 * k + 4):
-                aff(h("GL", 512 + 512 * ch, 1024 + 512 * ch), ind(a("W"), h("offM", 32 * ch, 32 * ch + 32)), on=ONGL[t])
+            tt(h("lI", lo, hi), a("b3", lo, hi), h("s1", lo, hi), ADD)
+            ts(h("lI", 256 + lo, 256 + hi), h("lI", lo, hi), 5, SHR, -2147479553, AND)
+            ts(h("offM", lo, hi), h("lI", 256 + lo, 256 + hi), 16.0, ADD)
+            big = 2 if "GL" + s in BIG else 1
+            for ch in range(4 * k, 4 * k + 4, big):
+                aff(h("GL", 512 + 512 * ch, 512 + 512 * (ch + big)), ind(a("W"), h("offM", 32 * ch, 32 * (ch + big))), on=ONGL[t])
                 run("GL")
-        cp(ind(h("GL"), uP), pk)
+        if not late:
+            cp(ind(h("GL"), uP), pk)
         for ch in range(4):
             scan(h("sc", 1024 * ch, 1024 * ch + 1024), a("mask"), h("GL", 512 + 1024 * ch, 1536 + 1024 * ch), MUL, MAX)
             run("sc")
         o = a("b3", 0, 256)
-        mms([(o, a("ID"), a(zt, 16), True, False), (o, a("ID"), h("sc", 15, 4096, 16), False, True)])
-        aff(n32("zf", F, 256), o, 0.4995, 12582912.0, on="S")
-        aff(h("zs"), h("zf"), 1.0, -12582912.0)
+        if "z" in ONS[t]:
+            mms([(o, a("ones"), a("q25"), True, False), (o, a("id64"), a(zt, 16), False, False), (o, a("id64"), h("sc", 15, 4096, 16), False, True)])
+            ts(h("zs"), o, 12582912.0, SUB, -12582912.0, SUB)
+        else:
+            mms([(o, a("ID"), a(zt, 16), True, False), (o, a("ID"), h("sc", 15, 4096, 16), False, True)])
+            aff(n32("zf", F, 256), o, 0.4995, 12582912.0, on="S")
+            aff(h("zs"), h("zf"), 1.0, -12582912.0)
         send((rank + 1 + t) % N, h("zs"), a("z%d" % (t + 1), 16), "az" + s, "lz" + s, (rank - 1 - t) % N)
-        n32("kw", F, 512)
-        for k in range(2):
-            scan(h("kw", 256 * k, 256 * k + 256), a("mask", 0, 256), a("b5", 256 * k, 256 * k + 256), MUL, MAX)
-        cp(n32("kAB", I), h("kw", 15, 512, 16))
-        kA, kB = h("kAB", 0, 32, 2), h("kAB", 1, 32, 2)
-        inj = tt(n32("inj", B, 16), h("kw", 15, 512, 32), a("thK" + s), GT)
+        n32("kw", I, 512)
+        for k, b in enumerate(("b5", "b2")):
+            scan(h("kw", 256 * k, 256 * k + 256), a("mask", 0, 256), a(b, 0, 256), MUL, MAX)
+        kA, kB = h("kw", 15, 512, 32), h("kw", 31, 512, 32)
+        inj = tt(n32("inj", B, 16), kA, a("thK" + s), GT)
         t1 = ts(n32("t1", I, 16), kA, 224, AND)
         cI = ts(n32("cI", I, 16), kB, 1, SHR, 31, AND)
         t2 = ts(n32("t2", I, 16), kB, 3, SHR, 24, AND)
         gh = tt(n32("gh", B, 16), ts(n32("g1", I, 16), kA, 128, AND), inj, MUL)
-        mms([(a("b6", 192, 208), a("TRI"), gh, True, False), (a("b6", 200, 208), a("ones"), h("gh", 0, 8), False, True)])
-        rt = tt(n32("rt", B, 512), ind(cI, a("o32")), a("x32"), EQ)
+        o = a("b6", 192, 208)
+        mms([(o, a("ones"), a("c46"), True, False), (o, a("TRI"), gh, False, False), (a("b6", 200, 208), a("ones8"), h("gh", 0, 8), False, True)])
+
+        def same(o, tab, v, w):
+            for k in range(16):
+                aff(h(o + "a", w * k, w * k + w), tab(k), -1.0, h(v, k, k + 1), on="S", f=AF.Abs)
+                run(o)
+            aff(h(o), h(o + "a"), -1.0, 1.0, on="S", f=AF.Relu)
+
+        n32("rt", B, 512)
+        if "r" in ONS[t]:
+            n32("rta", B, 512)
+            cp(n32("cF", F, 16), cI)
+            same("rt", lambda k: a("x32", 0, 32), "cF", 32)
+        else:
+            tt(h("rt"), ind(cI, a("o32")), a("x32"), EQ)
         q8 = tt(n32("q8", F, 16), t1, t2, ADD)
-        q9 = tt(n32("q9", F, 16), ts(n32("nt", F, 16), a("b6", 192, 208), -4.5, GE, 1024.0, MUL), q8, ADD)
-        tt(n32("lt", B, 256), ind(q9, a("o16")), a("xQ"), EQ)
+        q9 = tt(n32("q9", F, 16), a("b6", 192, 208), q8, MAX)
+        n32("lt", B, 256)
+        if "l" in ONS[t]:
+            n32("lta", B, 256)
+            same("lt", lambda k: a("xQ", 0, 16), "q9", 16)
+        else:
+            tt(h("lt"), ind(q9, a("o16")), a("xQ"), EQ)
         mms([(a("b5", 0, 256), h("lt", 128 * k, 128 * k + 128), h("rt", 256 * k, 256 * k + 256), k == 0, k == 1) for k in range(2)])
         aff(n32("hx", B, 256), a("b5", 0, 256))
         aff(h("hs"), ind(h("hx"), a("oH")))
         send(up, h("hs"), h("hl"), "ah" + s, "lh" + s, dn)
-        lI = ts(n32("l7", I, 16), kB, 1, SHR, 127, AND)
-        o1 = tt(n32("o1", F, 16), ts(n32("o4", F, 16), t1, 4.0, MUL, 1.0, ADD), lI, ADD)
-        tt(n32("test", B, 256), ind(o1, a("o16")), h("LMT"), EQ)
-        scan(n32("inl", B, 256), a("mask", 0, 256), h("test"), MUL, MAX)
-        loc = tt(n32("loc1", F, 16), tt(n32("loc0", F, 16), inj, gh, GT), h("room"), MUL)
-        jf = tt(n32("jf", F, 16), loc, h("inl", 15, 256, 16), GT)
+        o1 = tt(n32("o1", F, 16), aff(n32("o4", F, 16), t1, 4.0, 1.0), ts(n32("l7", I, 16), kB, 1, SHR, 127, AND), ADD)
+        tt(n32("test", B, 256), ind(o1, a("o16")), h("LMT"), OP.not_equal)
+        scan(n32("out_", B, 256), a("k0"), h("test"), MAX, MIN)
+        fresh = h("out_", 15, 256, 16)
+        loc = tt(n32("loc0", F, 16), inj, gh, GT)
         if t < 2:
             pb = ts(n32("pb", I, 16), kB, 1, SHR, 1, AND)
             nn = ts(n32("nm", F, 16), ts(n32("nn", I, 16), kA, 31, AND), 16384.0, MUL)
-            jk = tt(n32("jk", F, 16), tt(n32("j1", F, 16), nn, h("c15"), ADD), aff(n32("j2", F, 16), o1, 0.5), ADD)
+            jk = tt(n32("jk", F, 16), tt(n32("j1", F, 16), nn, h("c15", 0, 16), ADD), aff(n32("j2", F, 16), o1, 0.5), ADD)
+            jk = tt(n32("jq", F, 16), tt(n32("jp", F, 16), loc, pb, GT if t else MUL), jk, MUL)
             k2 = a("key%d" % (t + 1), 16 * par, 16 * par + 16)
-            tt(k2, tt(n32("j3", F, 16), tt(n32("jp", F, 16), jf, pb, GT if t else MUL), jk, MUL), k2, MAX)
-        tt(n32("dl", H, 256), ind(tt(n32("jv", F, 16), jf, o1, MUL), a("o16")), h("mkT"), MUL)
+            tt(k2, tt(n32("j3", F, 16), jk, fresh, MUL), k2, MAX)
+        jv = tt(n32("jv", F, 16), tt(n32("jo", F, 16), loc, o1, MUL), fresh, MUL)
+        n32("dl", H, 256)
+        if "d" in ONS[t]:
+            for k in range(16):
+                aff(h("dl", 16 * k, 16 * k + 16), h("mkT", 16 * k, 16 * k + 16), h("jv", k, k + 1), on="S")
+                run("dl")
+        else:
+            tt(h("dl"), ind(jv, a("o16")), h("mkT"), MUL)
         o = a("b7", 256, 512)
         mms([(o, a("IDh"), h("LSh"), True, False)]
             + [(a("b7", 256 + 128 * k, 384 + 128 * k), h("dl", 128 * k, 128 * k + 128), a("IDh"), False, k == 1) for k in range(2)])
@@ -545,15 +648,14 @@ def rank_program(g, core, T, topo):
             o, i_, c = h("c0", 16, 32), a("b6", 208, 224), h("c0", 0, 1)
             acc = spans(o, [i_]) + [(c[1][0], True)]
             step({"S": (100, [(acc, lambda e, o=o, i_=i_, c=c: e.activation(o[0], i_[0], AF.Copy, bias=0.0, scale=128.0, accum_out=c[0]))])}, acc)
-            v = aff(h("c0", 2, 3), aff(h("c0", 1, 2), c, 1.0 / 32, -0.484375, on="S"), 1.0, 12582912.0, on="S")
-            v = aff(h("c0", 4, 5), aff(h("c0", 3, 4), v, 1.0, -12582912.0, on="S"), -131072.0, on="S")
-            aff(new("thK%d" % (t + 1), 16, F), a("thK0"), 1.0, aff(h("c0", 5, 6), c, 4096.0, v, on="S"), on="S")
+            v = aff(h("c0", 1, 2), aff(n32("cJ", I, 1), c, 1.0 / 32, -0.484375), -131072.0)
+            aff(new("thK%d" % (t + 1), 16, F), a("thK0"), 1.0, aff(h("c0", 2, 3), c, 4096.0, v))
             v = ts(n32("gv1", I), tt(n32("gv0", I), h("gl"), h("hs"), ADD), 15, AND)
             ghosts(t + 1, cp(n32("gv2", B), v))
         if t == 0:
-            mms(sum(sizes(), []))
-            aff(a("TK", 1, 513), a("b0"))
-            elect(2, 0, members("TK", 0, True, False, ONGN[1]))
+            mms(sum(sizes("b4", True), []))
+            aff(a("TK", 1, 513), a("b4"))
+            elect(2, 0, members("TK", 0, True, False, ONK))
         v = ts(n32("dv1", I), tt(n32("dv0", I), dm, h("hl"), ADD), 15, AND)
         if t < 2:
             cp(new("d%d" % (t + 1), 32, B), v)
@@ -613,44 +715,165 @@ def arrange(steps):
             way[j] = max(way[j], way[k] - (late[j] + WAIT if j in soft[k] else 0))
         for j in after[k]:
             way[j] = max(way[j], way[k] - WAIT - min(cost[j].values()) / 2)
-    at, end, free, bank = {}, {}, {q: 0.0 for q in "VSPGD"}, {b: {} for b in BANKS}
-    left = [len(d) for d in deps]
-    front = {k: 0.0 for k in range(n) if not left[k]}
-    while front:
-        cand = {q: [] for q in free}
-        for k, u in front.items():
-            for q in cost[k]:
-                cand[q].append((max([u, free[q]] + [v for b in banks[k] for q2, v in bank[b].items() if q2 != q]), k))
-        t, q = min((min(c)[0], q) for q, c in cand.items() if c)
-        rivals = [(u, k) for u, k in cand[q] if u > t]
-        for j, u in front.items():
-            if q not in cost[j]:
-                for k in users[j]:
-                    if left[k] == 1 and q in cost[k]:
-                        rivals.append((max(u, free[min(cost[j])]) + min(cost[j].values()) + late[j] + WAIT, k))
-        pick = None
-        for u, k in sorted((c for c in cand[q] if c[0] <= t), key=lambda c: -way[c[1]]):
-            c = cost[k][q]
-            over = [t + c - v - FILL * (v - t) - HOLD for v, j in rivals if way[j] > way[k] and way[j] - way[k] > t + c - v]
-            if q == "V" and "S" in cost[k] and max(free["S"], t) + cost[k]["S"] < t + c + SPARE and not (c > 400 and free["S"] > t):
+
+    def place(way, deps, users, back):
+        at, end, free, bank = {}, {}, {q: 0.0 for q in "VSPGD"}, {b: {} for b in BANKS}
+        left = [len(d) for d in deps]
+        pre, post = (late, [0.0] * n) if back else ([0.0] * n, late)
+        front = {k: pre[k] for k in range(n) if not left[k]}
+        while front:
+            cand = {q: [] for q in free}
+            for k, u in front.items():
+                for q in cost[k]:
+                    cand[q].append((max([u, free[q]] + [v + pre[k] for b in banks[k] for q2, v in bank[b].items() if q2 != q]), k))
+            t, q = min((min(c)[0], q) for q, c in cand.items() if c)
+            rivals = [(u, k) for u, k in cand[q] if u > t]
+            for j, u in front.items():
+                if q not in cost[j]:
+                    for k in users[j]:
+                        if left[k] == 1 and q in cost[k]:
+                            rivals.append((max(u, free[min(cost[j])]) + min(cost[j].values()) + post[j] + pre[k] + WAIT, k))
+            pick = None
+            for u, k in sorted((c for c in cand[q] if c[0] <= t), key=lambda c: -way[c[1]]):
+                c = cost[k][q]
+                over = [t + c - v - FILL * (v - t) - HOLD for v, j in rivals if way[j] > way[k] and way[j] - way[k] > t + c - v]
+                if q == "V" and "S" in cost[k] and max(free["S"], t) + cost[k]["S"] < t + c + SPARE and not (c > 400 and free["S"] > t):
+                    continue
+                if max(over + [0]) <= 0:
+                    pick = k
+                    break
+            if pick is None:
+                free[q] = min([u for u, k in rivals if u > t] + [t + 200])
                 continue
-            if max(over + [0]) <= 0:
-                pick = k
+            c = cost[pick][q]
+            at[pick], free[q], end[pick] = (t, q), t + c, t + c + post[pick]
+            for b in banks[pick]:
+                bank[b][q] = end[pick] + WAIT
+            del front[pick]
+            for k in users[pick]:
+                left[k] -= 1
+                if not left[k]:
+                    front[k] = max(end[j] - post[j] if j in soft[k] or k in soft[j] or (at[j][1] == "P" and "P" in cost[k])
+                                   else end[j] + WAIT + pre[k] for j in deps[k])
+        return at, end
+
+    PLAN["bound"], best, PLAN["ends"] = max(way), None, []
+    for _ in range(PASSES):
+        at, end = place(way, deps, users, False)
+        PLAN["ends"].append(round(max(end.values()) * .83e-3, 1))
+        if best is None or max(end.values()) < best[0]:
+            best = (max(end.values()), at, way)
+        way = place(end, users, deps, True)[1]
+    PLAN["end"], at, way = best
+    PLAN["hook"] = (place, way, deps, users)
+    hard = [deps[k] if steps[k]["kind"] == "dma" else deps[k] - soft[k] for k in range(n)]
+    return polish(steps, hard, soft, [(k, at[k][1]) for k in sorted(at, key=lambda k: (at[k][0], k))])
+
+
+def polish(steps, deps, soft, order):
+    n = len(steps)
+    users = [[] for _ in steps]
+    for k in range(n):
+        for j in deps[k]:
+            users[j].append(k)
+    wait = [[j for j in deps[k] if j not in soft[k] and not ("P" in steps[j]["alts"] and "P" in steps[k]["alts"])] for k in range(n)]
+    banks = [sorted({int(b[1]) for (b, _, _), _ in s["acc"] if b in BANKS}) for s in steps]
+    first = [s["kind"] for s in steps].index("send")
+    late = [-s["late"] if s["kind"] == "dma" else s["late"] + WAIT for s in steps]
+    busy = [[{q: c + (FIRST if k == first else 0) if s["kind"] else f * (c + (ga - GATHER) * s["n"][0] + (sc - SCATTER) * s["n"][1])
+              for q, (c, _) in s["alts"].items()} for k, s in enumerate(steps)] for f, ga, sc in RATES]
+
+    def replay(order, busy, was, at):
+        end, marks = list(was[1]), was[2][:at // 32 + 1]
+        free, bq, be, bo = [type_(v) for type_, v in zip((dict, list, list, list), marks[-1])]
+        for p in range(at // 32 * 32, n):
+            if p % 32 == 0 and p // 32 == len(marks):
+                marks.append((dict(free), list(bq), list(be), list(bo)))
+            k, q = order[p]
+            t = free[q]
+            for j in wait[k]:
+                if end[j] > t:
+                    t = end[j]
+            for b in banks[k]:
+                v = be[b] if bq[b] != q else bo[b]
+                if v > t:
+                    t = v
+            free[q] = e = t + busy[k][q]
+            if late[k] < 0:
+                free["M"] = e = max(t + DMA0, free["M"]) - late[k]
+                e += WAIT
+            else:
+                e += late[k]
+            end[k] = e
+            for b in banks[k]:
+                if bq[b] != q:
+                    bo[b], bq[b] = be[b], q
+                be[b] = e
+        return max(end), end, marks
+
+    start = (0, [0.0] * n, [({q: 0.0 for q in "VSPGDM"}, [""] * 8, [0.0] * 8, [0.0] * 8)])
+    now = [replay(order, b, start, 0) for b in busy]
+    unit = [v[0] for v in now]
+    seed = [SEED]
+
+    def draw():
+        seed[0] = (seed[0] * 1103515245 + 12345) % 2147483648
+        return (seed[0] + 1) / 2147483649.0
+
+    def chain(order, busy, end):
+        out, t = [], max(end)
+        for p in reversed(range(n)):
+            k, q = order[p]
+            if abs(end[k] - t) < 0.01 or (out and q == out[-1][1] and late[k] >= 0 and abs(end[k] - late[k] - t) < 0.01):
+                out.append((k, q))
+                t = end[k] - late[k] - busy[k][q] if late[k] >= 0 else max([end[j] for j in wait[k]] + [-1])
+        return out
+
+    score = best = 1.0
+    kept = order
+    for it in range(MOVES):
+        if it % 24 == 0:
+            m = it // 24 % len(busy)
+            hot = chain(order, busy[m], now[m][1])
+            PLAN["hot"] = len(hot)
+        i = int(draw() * n)
+        if draw() < 0.7:
+            k = hot[int(draw() * len(hot))][0]
+            i = [v[0] for v in order].index(k)
+        k, q = order[i]
+        r, d = draw(), 1 + int(-12 * math.log(draw()))
+        if r < 0.15:
+            if len(steps[k]["alts"]) == 1:
+                continue
+            lo, new = i, order[:i] + [(k, "V" if q == "S" else "S")] + order[i + 1:]
+        else:
+            back = draw() < 0.6
+            if r > 0.6:
+                d, m, w = 0, 1 + d // 8, -1 if back else 1
+                while m and 0 <= i + w * (d + 1) < n:
+                    d += 1
+                    m -= order[i + w * d][1] == q
+            lo, hi = (max(0, i - d), i + 1) if back else (i, i + d + 1)
+            drag = {k}
+            for j, _ in (order[lo:hi][::-1] if back else order[lo:hi]):
+                if any(u in drag for u in (users[j] if back else deps[j])):
+                    drag.add(j)
+            x, y = [v for v in order[lo:hi] if v[0] in drag], [v for v in order[lo:hi] if v[0] not in drag]
+            new = order[:lo] + (x + y if back else y + x) + order[hi:]
+        limit = score - HEAT * (1 - it / MOVES) * math.log(draw())
+        then = []
+        for b, w, u in zip(busy, now, unit):
+            then.append(replay(new, b, w, lo))
+            if then[-1][0] > w[0] + 3 * u * (limit - score) + CUT * u:
                 break
-        if pick is None:
-            free[q] = min([u for u, k in rivals if u > t] + [t + 200])
-            continue
-        c = cost[pick][q]
-        at[pick], free[q], end[pick] = (t, q), t + c, t + c + late[pick]
-        for b in banks[pick]:
-            bank[b][q] = end[pick] + WAIT
-        del front[pick]
-        for k in users[pick]:
-            left[k] -= 1
-            if not left[k]:
-                front[k] = max(end[j] - late[j] if j in soft[k] or (at[j][1] == "P" and "P" in cost[k]) else end[j] + WAIT for j in deps[k])
-    PLAN["bound"], PLAN["end"] = max(way), max(end.values())
-    return [(k, at[k][1]) for k in sorted(at, key=lambda k: (at[k][0], k))]
+        else:
+            e = sum(v[0] / u for v, u in zip(then, unit)) / len(unit)
+            if e <= limit:
+                score, order, now = e, new, then
+                if e < best:
+                    best, kept = e, new
+    PLAN["rates"] = [round(replay(kept, b, start, 0)[0] * .83e-3, 1) for b in busy]
+    return kept
 
 
 def issue(g, core, T, topo, eng, steps, plan):

@@ -2,7 +2,7 @@ import math
 from concourse.mybir import AluOpType, ActivationFunctionType
 
 F, B, H, I, U = "float32", "bfloat16", "float16", "int32", "uint16"
-POOL = {F: 10752, B: 36352, H: 4096, I: 8192, U: 3072}
+POOL = {F: 10240, B: 36352, H: 4096, I: 8704, U: 3072}
 OWN = {"valI": (32, I), "gI0": (32, I), "z0": (272, B), "z1": (272, B), "z2": (272, B), "z3": (272, B)}
 for _t in range(3):
     for _n in ("gs", "gl", "hs", "hl"):
@@ -14,16 +14,18 @@ SCRATCH = {"p" + _d: ("sbuf", [128, _c], _d) for _d, _c in POOL.items()}
 SCRATCH.update({_n: ("sbuf", [128, _c], _d) for _n, (_c, _d) in OWN.items()})
 BANKS = ["b%d" % _b for _b in range(8)]
 SCRATCH.update({_b: ("psum", [128, 512], F) for _b in BANKS})
-SEMAPHORES = ["sV", "sS", "sP", "sG"] + ["d%d" % i for i in range(12)] + [a + str(t) for a in ("az", "ah", "ag", "lz", "lh", "lg") for t in range(3)]
+SEMAPHORES = ["sV", "sS", "sP", "sG"] + ["d%d" % i for i in range(20)] + [a + str(t) for a in ("az", "ay", "ah", "ag", "lz", "ly", "lh", "lg") for t in range(3)]
 
-GATHER, SCATTER, LEAST, WAIT, REMOTE, FIRST, DMA0, DMABYTES = 1.56, 3.8, 64, 200, 1900, 2400, 2200, 200.0
-SPARE, FILL, HOLD, PASSES = 300, 1.0, 60, 5
+GATHER, SCATTER, LEAST, WAIT, REMOTE, FIRST, DMA0, DMABYTES = 1.56, 3.8, 64, 210, 1600, 2400, 1800, 200.0
+LAG = {"V": 240, "S": 200, "P": 170, "G": 170, "D": 170}
+RULES, PASSES = ((300, 300, 0.5, 200), (300, 600, 1.0, 60)), 4
 ONGN, ONGL = ("VS", "VS", "VS"), ("VS", "VS", "VS")
-OPEN = ("b0", "b4")
+HALF = FREE = True
+OPEN = ("b0", "b2", "b4")
 MORE = {}
-CUT, OLD = 0.004, False
-RATES, MOVES, HEAT, SEED = ((1.0, 1.56, 3.8), (1.05, 1.2, 2.5), (1.4, 2.0, 5.5)), 60000, 0.0004, 1
-ONS, ONK, ONPK = ("rgb", "rb", "rb"), "VS", "VS"
+CUT, MERGE, SWAP, EARLY = 0.004, False, 0.3, 0.1
+RATES, MOVES, HEAT, SEED = ((1.0, 1.5, 3.6, 0.9), (1.25, 1.25, 4.6, 1.0), (1.3, 1.85, 3.0, 0.9)), (2000, 170000), (0.0002, 0.0004), 1
+ONS, ONK, ONPK = ("r", "r", "r"), "VS", "VS"
 SOUT = (F, B, H, I, U)
 BIG = ("TB0",)
 PLAN = {}
@@ -61,6 +63,11 @@ def rank_program(g, core, T, topo):
         ap = T[b][:, o + lo:o + hi:st] if st > 1 else T[b][:, o + lo:o + hi]
         named[(b, o + lo, o + hi)] = n + ("@%d" % lo if b in BANKS else "")
         return (ap, [(b, o + lo, o + hi)], len(range(lo, hi, st)), d, "P" if b in BANKS else "S")
+
+    def top8(n, lo=0, hi=None):
+        v = a(n, lo, hi)
+        b, lo, hi = v[1][0]
+        return (T[b][0:8, lo:hi],) + v[1:]
 
     def ind(w, o):
         return (w[0].indirect(o[0]), w[1] + o[1], 16 * o[2], w[3], "I")
@@ -126,6 +133,8 @@ def rank_program(g, core, T, topo):
 
     def aff(o, i, scale=1.0, bias=0.0, on="VS", f=None, v=None):
         acc, alts = spans(o, [i, scale, bias]), {}
+        if f is None and FREE:
+            on = "VS"
         if v is not None:
             alts["V"], on = (vcost(o, [i]), [(acc, lambda e: e.tensor_scalar(o[0], i[0], *v))]), "S"
         plain = scale == 1.0 and bias == 0.0
@@ -143,7 +152,7 @@ def rank_program(g, core, T, topo):
 
     def mms(calls):
         sub = [(spans(o, [l, r]), lambda e, o=o, l=l, r=r, s0=s0, s1=s1: e.matmul(o[0], l[0], r[0], s0, s1)) for o, l, r, s0, s1 in calls]
-        step({"P": (sum(max(64, c[2][2]) for c in calls), sub)}, [s for u in sub for s in u[0]], late=40)
+        step({"P": (sum(max(64, c[2][2]) * (4 if c[2][3] == F else 1) for c in calls), sub)}, [s for u in sub for s in u[0]])
 
     def mm(o, l, r, start=True, stop=True):
         mms([(o, l, r, start, stop)])
@@ -151,6 +160,12 @@ def rank_program(g, core, T, topo):
     def iota(o, pat, base=0, cm=0):
         acc = spans(o, [])
         step({"G": (160 + 2 * o[2], [(acc, lambda e: e.iota(o[0], pat, base, cm, allow_small_or_imprecise_dtypes=True))])}, acc)
+        run("G")
+        return o
+
+    def keep(o, i, pat, op, base, cm, c):
+        acc = spans(o, [i])
+        step({"G": (205 + 2 * o[2], [(acc, lambda e: e.affine_select(o[0], i[0], pat, op, c, base, cm))])}, acc)
         run("G")
         return o
 
@@ -181,7 +196,8 @@ def rank_program(g, core, T, topo):
 
     load("S", a("valI"), T.val[:, :])
     load("D", new("glI", 512, I), T.gl[:, :])
-    load("D", new("thI", 16, I), T.th[:, :])
+    new("thI", 256, I)
+    dma("D", top8("thI")[0], T.th[:, :], [(a("thI")[1][0], True)], 8192)
     load("D", new("nbI", 512, I), T.nb[:, :])
     load("D", a("z0", 16), T.zl[:, :])
     new("W", 4112, B)
@@ -190,7 +206,6 @@ def rank_program(g, core, T, topo):
     new("ci", 16, I)
     iota(col("ci"), [[0, 1]], 0, 1)
     iota(new("X", 256, F), [[1, 256]])
-    iota(new("kpat", 256, B), [[0, 16], [1, 16]])
     iota(new("x8", 128, B), [[0, 16], [1, 8]])
     new("pt", 64, F)
     iota(a("pt", 48, 64), [[16, 2], [1, 8]])
@@ -198,16 +213,14 @@ def rank_program(g, core, T, topo):
     send(dn, a("valI"), a("gI0"), "ag0", "lg0", up)
     run("G")
     iota(new("x16", 256, B), [[1, 16], [0, 16]])
-    iota(new("gx", 256, F), [[0, 2], [1, 8], [0, 16]])
     iota(new("Mrow", 512, F), [[1, 32], [32, 16]], 1)
-    iota(a("pt", 32, 48), [[16, 2], [0, 8]])
     iota(a("pt", 0, 32), [[1, 16], [0, 2]])
     iota(new("x32", 512, B), [[0, 16], [1, 32]])
-    for n, (op, c) in enumerate(((AND, 15), (AND, 112), (SHR, 4), (AND, 7), (AND, 8))):
+    for n, (op, c) in enumerate(((AND, 15), (AND, 112), (SHR, 4), (AND, 8))):
         ts(col("ci", n + 1), col("ci"), c, op)
     new("cf", 16, F)
-    cp(a("cf", 0, 6), a("ci", 0, 6))
-    pf, r, g16, gg, r7, r8 = [col("cf", k) for k in range(6)]
+    cp(a("cf", 0, 5), a("ci", 0, 5))
+    pf, r, g16, gg, r8 = [col("cf", k) for k in range(5)]
     new("cc", 32, F)
     used = [0]
 
@@ -230,11 +243,19 @@ def rank_program(g, core, T, topo):
     new("Kc", 512, B)
     aff(a("Kc", 0, 512, 2), a("X"), isr(1), s01)
     aff(a("Kc", 1, 512, 2), a("Kc", 0, 512, 2), -1.0)
-    aff(new("Ed", 144, B), a("E1"), isr(2))
+    keep(new("Ed", 144, B), a("E1"), [[1, 144]], EQ, -13, -1, 0.0)
+    fill(a("WK2", 512, 1024), 0.0)
+    for src, dst in ([(("WK2", 512, 512 + n), ("WK2", 512 + n, 512 + 2 * n)) for n in (512, 1024)]
+                     + [(("WK2", 512, 2560), (n, lo, lo + 2048)) for n, lo in (("WK0", 512), ("WK0", 2560), ("WK2", 2560), ("WK1", 512), ("WK1", 2560))]):
+        dma("D", a(*dst)[0], a(*src)[0], [(a(*src)[1][0], False), (a(*dst)[1][0], True)], 256 * a(*dst)[2])
+
+    def diag(n, c):
+        keep(new(n, 128, B), a("WK2", 512, 640), [[-1, 128]], OP.not_equal, 0, 1, c)
+
     for t in range(3):
         new("TB%d" % t, 1040, B)
-        aff(col("TB%d" % t), isr(2), -128.0)
-        fill(a("z%d" % t, 0, 16), 0.0)
+        aff(col("TB%d" % t), isr(2), -128.0, isr(4))
+        iota(a("z%d" % t, 0, 16), [[0, 16]])
 
     new("onS", 512, B)
     for par in range(2):
@@ -242,7 +263,7 @@ def rank_program(g, core, T, topo):
         aff(a("onS", par, 512, 2), gp, 1.0 - 2 * par, 1.0 - 2 * par, f=AF.Sign, v=(0.0, 1.0 - 2 * par, GE, MUL))
         ts(new("off%d" % par, 256, U), gp, 1.0, ADD)
         new("LS%d" % par, 272, F)
-        fill(a("LS%d" % par, 0, 16), 0.0)
+        iota(a("LS%d" % par, 0, 16), [[0, 16]])
         ts(a("LS%d" % par, 16), gp, 1.0, ADD)
     cp(new("d0", 32, B), a("valI"))
 
@@ -250,14 +271,30 @@ def rank_program(g, core, T, topo):
         return [(a(bank), a("ID"), a("Kc"), True, False)], [(a(bank), es("E1", 0), a("onS"), False, stop)]
 
     def table(t):
-        if t < 2:
+        if t < 2 or MERGE:
             mms(sizes("b0", False)[0])
-        if t == 1:
+        if t == 1 or (t and MERGE):
             mms(sizes("b0", False)[1])
-        rows("b0", a("d%d" % t), t == 2, t > 0)
+        rows("b0", a("d%d" % t), t == 2 and not MERGE, t > 0)
         if t == 0:
             mms(sizes("b0", True)[1])
         aff(a("TB%d" % t, 1, 513), a("b0"))
+
+    def table2(t):
+        for k, b in enumerate(("b0", "b2")):
+            lo, o = 256 * k, a(b, 0, 256)
+            if t < 2:
+                mm(o, a("ID"), a("Kc", lo, lo + 256), True, False)
+            if t == 1:
+                mm(o, es("E1", 0), a("onS", lo, lo + 256), False, False)
+            mms([(a(b, 32 * q, 32 * q + 32), a("FH", 128 * (q + 8 * k), 128 * (q + 8 * k) + 128), a("d%d" % t), t == 2, t == 2 or (t == 1 and q == 7))
+                 for q in range(8)])
+            if t == 0:
+                mm(o, es("E1", 0), a("onS", lo, lo + 256), False, True)
+            aff(a("TB%d" % t, 1 + lo, 257 + lo), o)
+
+    if HALF:
+        table = table2
 
     def ghosts(t, src):
         rows("b0", src, True)
@@ -273,7 +310,7 @@ def rank_program(g, core, T, topo):
             k = ch // 4
             if ch % 4 == 3:
                 mms([(a(bank, lo + w * k + q, lo // w * w + w * k + w, 16), a(n, 2048 * k + q, 2048 * k + 2048, 16),
-                      a("WKD", 0 if keys else 8, 16 if values else 8), True, True) for q in range(16)])
+                      a("WK16" if tab == "TB0" else "WKD", 0 if keys else 8, 16 if values else 8), True, True) for q in range(16)])
                 if values:
                     aff(a("dM", 128 * k, 128 * k + 128), a(bank, 256 * k + 128, 256 * k + 256))
         return [a(bank, lo + w * k, lo + w * k + 128) for k in range(2)]
@@ -281,19 +318,21 @@ def rank_program(g, core, T, topo):
     def elect(t, par, src):
         for k in range(2):
             lo = 256 * par + 128 * k
-            scan(a("ks%d" % t, lo, lo + 128), a("subp" if t & 1 else "addp"), src[k], ADD, MIN if t & 1 else MAX)
-        sg = -1.0 if t & 1 else 1.0
-        aff(a("key%d" % t, 16 * par, 16 * par + 16), a("ks%d" % t, 256 * par + 15, 256 * par + 256, 16), sg, f=AF.Relu, v=(sg, 0.0, MUL, MAX))
+            scan(a("ks%d" % t, lo, lo + 128), a(("add16", "sub16", "addp")[t]), src[k], ADD, MIN if t & 1 else MAX)
+        o, i = a("key%d" % t, 16 * par, 16 * par + 16), a("ks%d" % t, 256 * par + 15, 256 * par + 256, 16)
+        if t == 1:
+            aff(o, i, -0.0625, 0.46875, on="S", f=AF.Relu)
+        else:
+            aff(o, i, f=AF.Relu, v=(0.0, None, MAX))
 
     for n, c in (("GN0", 4096), ("GN1", 4096), ("G4", 2048), ("GL", 4608), ("sc", 4096)):
         for t in ("", "0", "1", "2") if n[1] != "N" else ("",):
             tiles[n + t] = tiles[n] if t else new(n, c, B) and tiles[n]
     table(0)
     new("mask", 1024, B)
-    for k in range(4):
-        aff(a("mask", 256 * k, 256 * k + 256), a("kpat"), f=AF.Sign, v=(1.0, None, MIN))
-    aff(new("addp", 128, F), a("mask", 0, 128), 4194304.0 + 1024.0, -4194304.0)
-    aff(new("subp", 128, F), a("addp"), -1.0)
+    keep(a("mask", 0, 256), a("WK2", 512, 768), [[0, 16], [1, 16]], EQ, 0, 0, 1.0)
+    for n, c in (("add16", 16384), ("sub16", -16384), ("addp", 1024)):
+        keep(iota(new(n, 128, F), [[0, 128]], c), a(n), [[0, 8], [1, 16]], GT, 0, 0, -8388608.0 if c > 0 else 8388608.0)
     for t in range(3):
         new("key%d" % t, 32, I)
         new("ks%d" % t, 512, F)
@@ -301,10 +340,16 @@ def rank_program(g, core, T, topo):
     new("WKD", 16, B)
     aff(a("WKD", 0, 8), a("G8"), cc(isr(0), 16384.0, isr(1)))
     aff(a("WKD", 8, 16), a("G8"), isr(2))
+    new("WK16", 16, B)
+    aff(a("WK16", 0, 8), a("G8"), cc(isr(0), 262144.0, cc(isr(1), 16.0, cc(isr(4), 128.0, isr(2)))))
+    aff(a("WK16", 8, 16), a("G8"), isr(2))
     new("dM", 256, B)
     fill(new("ones", 128, B), 1.0 / 128)
-    fill(new("m37c", 128, B), -37.0)
-    aff(new("ID32", 128, B), a("ID"), 32.0)
+    iota(new("m37c", 128, B), [[0, 128]], -37)
+    diag("ID32", 32.0)
+    iota(new("j8", 128, B), [[1, 4], [0, 32]], -8)
+    diag("ID8n", -8.0)
+    keep(new("B32", 128, B), a("WK2", 512, 640), [[-16, 8], [0, 16]], OP.not_equal, -2, 1, 32.0)
     aff(new("TK", 528, B) and col("TK"), isr(2), 0.0)
     keys = [members("TB0", 0, True, True, ONGN[0]), members("TB0", 1, True, False, ONGN[0])]
     for t in range(2):
@@ -316,22 +361,14 @@ def rank_program(g, core, T, topo):
         aff(new(n, 32, F), a("mA"), 2.0, c)
     for par in range(2):
         aff(new("x17%d" % par, 256, H), a("X"), 4.0, 17.0 + 2 * par)
-        aff(new("x613%d" % par, 256, F), a("X"), 4.0, 613.0 + 2 * par)
-    for t in range(3):
-        o = new("WK%d" % t, 4608, B)
-        for ch in range(0 if t else 4):
-            iota(a("WK0", 512 + 1024 * ch, 1536 + 1024 * ch), [[0, 1024]])
-        if t:
-            src = a("WK%d" % (t - 1), 512)
-            dma("D", a("WK%d" % t, 512)[0], src[0], [(src[1][0], False), (o[1][0], True)], 128 * 8192)
+        iota(new("x613%d" % par, 256, F), [[4, 256]], 613 + 2 * par)
     cp(new("o16", 16, U), a("X", 0, 16))
     cp(new("o32", 32, U), a("pt", 0, 32))
-    ts(new("oML", 16, U), a("pt", 32, 48), r, ADD)
     ts(new("oMT", 16, U), a("pt", 48, 64), r8, ADD)
     ts(new("oH", 2, U), a("X", 0, 32, 16), cc(g16, 2.0, r), ADD)
     aff(new("E64", 144, B), a("E1"), 64.0)
     aff(new("Es", 144, B), a("E1"), cc(r, 1.0, 1.0))
-    aff(new("E0", 144, B), a("E1"), isr(0))
+    keep(new("E0", 144, B), a("E1"), [[1, 144]], EQ, -15, -1, 0.0)
     cp(new("Eh", 144, H), a("E1"))
 
     def total(o, parts):
@@ -348,50 +385,41 @@ def rank_program(g, core, T, topo):
     aff(new("w1", 128, B), es("E2", 4), 49152.0)
     aff(new("w2", 128, B), es("E1", 3), cc(r, -1.0, 15.0))
     total(new("Weq", 128, B), [a("w1"), a("w2"), es("E1", 6)])
-    ts(new("B32", 128, B), a("gx", 0, 128), gg, EQ, cc(isr(2), 32.0), MUL)
-    aff(new("ID64", 128, B), a("ID"), 64.0)
-    aff(new("IDn", 128, B), a("ID"), -1.0)
-    aff(new("k0", 256, B), a("mask", 0, 256), -1.0, 1.0)
-    acc = spans(new("Sh", 128, B), [a("mask", 0, 128)])
-    step({"G": (460, [(acc, lambda e: e.affine_select(a("Sh")[0], a("mask", 0, 128)[0], [[-1, 128]], EQ, 0.0, 1, 1))])}, acc)
+    diag("ID64", 64.0)
+    diag("IDn", -1.0)
+    keep(new("k0", 256, B), a("WK2", 512, 768), [[0, 16], [1, 16]], OP.not_equal, 0, 0, 1.0)
+    keep(new("Sh", 128, B), a("mask", 0, 128), [[-1, 128]], EQ, 1, 1, 0.0)
     aff(new("Shn", 128, B), a("Sh"), -1.0)
     cp(new("IDh", 128, H), a("ID"))
-    if OLD:
-        aff(new("IDz", 128, H), a("ID"), 0.49951171875)
-    ts(new("tri", 128, B), a("X", 0, 128), pf, GT, 8.0, MUL)
-    aff(new("id64", 128, B), a("ID"), -512.0)
-    fill(new("ones8", 128, B), 8.0)
-    fill(new("c46", 16, B), 4608.0)
-    total(new("TRI", 128, B), [a("tri"), a("id64")])
-    aff(new("ID8n", 128, B), a("ID"), -8.0)
-    aff(new("j8", 128, B), a("j16"), 1.0 / 16, -8.0)
-    fill(a("W", 0, 16), 0.0)
-    aff(new("G8n", 8, B), a("G8"), -1.0)
+    iota(new("ones8", 128, B), [[0, 128]], 8)
+    iota(new("c46", 16, B), [[0, 16]], 4608)
+    keep(new("tri", 128, B), a("ones8"), [[1, 128]], GT, 0, -1, 0.0)
+    keep(new("TRI", 128, B), a("tri"), [[1, 128]], OP.not_equal, 0, -1, -512.0)
+    for k in range(1, 4):
+        keep(a("mask", 256 * k, 256 * k + 256), a("WK2", 512, 768), [[0, 16], [1, 16]], EQ, 0, 0, 1.0)
+    iota(a("W", 0, 16), [[0, 16]])
+    aff(new("G8c", 8, B), a("G8"), cc(isr(15), 1047552.0, 1024.0))
     w = cc(isr(3), 256.0, cc(s01, 4096.0))
     new("WAB", 24, B)
     aff(a("WAB", 0, 16, 2), a("G8"), cc(isr(4), 0.125, cc(isr(7), 1.0, cc(isr(6), -6144.0, w))))
     aff(a("WAB", 1, 16, 2), a("G8"), cc(isr(5), 1.0, cc(isr(6), 127.0, w)))
     aff(a("WAB", 16, 24), a("G8"), isr(2))
     odd = cc(isr(1), 1.0, isr(5))
-    ts(new("MK1", 256, B), a("gx"), r7, EQ)
     ts(new("MK2", 128, B), a("x8"), gg, EQ)
-    ts(new("R1", 16, F), a("X", 0, 16), cc(r8, 1.0, gg), EQ)
-    aff(new("R1a", 16, B), a("R1"), 262144.0)
-    aff(new("R1b", 16, B), a("R1"), 4096.0)
     aff(new("R2", 16, B), a("I16"))
-    aff(new("xQ", 256, B), a("kpat", 0, 256), 8.0, 128.0)
-    if OLD or any("g" not in v for v in ONS):
+    iota(new("xQ", 256, B), [[0, 16], [8, 16]], 128)
+    if any("g" not in v for v in ONS):
         new("QT", 272, B)
-        fill(a("QT", 0, 16), 0.0)
+        iota(a("QT", 0, 16), [[0, 16]])
         ts(a("QT", 16), a("x16"), r, EQ)
     ts(new("nbh", 512, H), a("nbI"), 2.0, MUL, -127.0, ADD)
     mms([(a("b1", q, 512, 16), a("IDh"), a("nbh", 32 * q, 32 * q + 32), True, True) for q in range(16)])
-    new("th2", 32, I)
-    ts(a("th2", 0, 16), a("thI"), 6, SHR)
-    ts(a("th2", 16, 32), a("thI"), 63, AND)
-    tt(new("thx", 256, B), ind(a("th2"), a("oML")), a("MK1"), MUL)
-    mms([(a("b7", 208, 224), a("thx", 0, 128), a("R1a"), True, False), (a("b7", 208, 224), a("thx", 128, 256), a("R1b"), False, True)])
-    aff(new("thK0", 16, F), a("b7", 208, 224), 1.0, 4095.0)
+    new("thF", 256, F)
+    cp(top8("thF"), top8("thI"))
+    keep(new("I8", 8, F), a("X", 0, 8), [[0, 8]], GT, 0, 0, 0.0)
+    keep(a("I8"), a("I8"), [[-1, 8]], OP.not_equal, 0, 1, 1.0)
+    mms([(a("b7", 208 + 8 * k, 216 + 8 * k), top8("thF", 128 * k, 128 * k + 128), top8("I8"), True, True) for k in range(2)])
+    aff(new("thK0", 16, F), a("b7", 208, 224), 4096.0, 4095.0)
     ghosts(0, cp(new("gb0", 32, B), a("gI0")))
 
     for t in range(3):
@@ -408,15 +436,23 @@ def rank_program(g, core, T, topo):
         def h(n, lo=0, hi=None, st=1):
             return a(n + s, lo, hi, st)
 
+        if t == 2 and MERGE:
+            elect(2, 0, members(TB, 0, True, True, ONGN[t]))
         n32("i1", I)
         n32("ex", B, 256)
         for p2 in (par, 1 - par):
-            ts(h("i1", 16 * p2, 16 * p2 + 16), a("key" + s, 16 * p2, 16 * p2 + 16), 1023, AND)
-            tt(h("ex", 128 * p2, 128 * p2 + 128), ind(h("i1", 16 * p2, 16 * p2 + 16), a("oMT", 0, 8)), a("MK2", 0, 128), MUL)
-            mm(a("b6", 224 + p2, 256, 2), h("ex", 128 * p2, 128 * p2 + 128), a("R2"))
+            kp = a("key" + s, 16 * p2, 16 * p2 + 16)
+            for n, at, op in ((("i1", 224, (4, SHR, 1023, AND)), ("de", 0, (15, AND))) if t == 0 else (("i1", 224, (1023, AND)),)):
+                if n == "de" and p2 == par:
+                    n32("de", I)
+                    n32("dex", B, 256)
+                v, e = ts(h(n, 16 * p2, 16 * p2 + 16), kp, *op), h("ex" if n == "i1" else "dex", 128 * p2, 128 * p2 + 128)
+                mm(a("b6", at + p2, at + 32, 2), tt(e, ind(v, a("oMT", 0, 8)), a("MK2"), MUL), a("R2"))
         i1 = a("b6", 224, 256)
         uZ = ts(n32("uZ", U), i1, 15.0, ADD)
-        if "g" in ONS[t]:
+        if t == 0:
+            pass
+        elif "g" in ONS[t]:
             uE = ts(n32("uE", U), i1, 2.0, MUL, par - 1.0, ADD)
         else:
             uE = cp(n32("uE", U), ts(n32("vc", I), ts(n32("vI", I), i1, 2.0, MUL, par - 2.0, ADD), 31, AND))
@@ -428,7 +464,9 @@ def rank_program(g, core, T, topo):
         mms([(o, a("ID"), a("j8"), True, False)] + [(a("b4", 256 + 32 * j, 288 + 32 * j), a("ID"), d, False, False) for j in range(4)]
             + [(o, a("ID8n"), h("sg"), False, True)])
         aff(n32("p4", B, 128), o, on="S")
-        if "g" in ONS[t]:
+        if t == 0:
+            pass
+        elif "g" in ONS[t]:
             aff(n32("gr", B, 512), ind(a(TB, 0, 513), uE))
             conv(a("b6", 0, 32), "Ed", every("gr" + s, 0, 512))
         else:
@@ -465,22 +503,23 @@ def rank_program(g, core, T, topo):
                 tt(h("P4", 32 * j, 32 * j + 32), h("t5", 32 * j, 32 * j + 32), X1, ADD)
             else:
                 tt(h("P4", 32 * j, 32 * j + 32), h("t4", 32 * j, 32 * j + 32), X2, ADD)
-        ts(h("P4", 128, 256), h("P4", 0, 128), 4095, AND)
-        ts(n32("u4", U, 128), h("P4", 128, 256), 16.0, ADD)
+        n32("u4", U, 128)
+        for lo in (0, 64):
+            cp(h("u4", lo, lo + 64), ts(h("P4", 128 + lo, 192 + lo), h("P4", lo, lo + 64), 4095, AND))
         uO = ts(n32("uO", U), a("b7", 64, 96), 0.5, MUL, 64.5, ADD)
         fo = aff(n32("fo"), a("b7", 64, 96), 0.5, 63.5)
         f20 = aff(h("c5", 0, 32), fo, 2.0, 37.0, on="S")
-        out = aff(n32("out", B), a("b7", 96, 128), -8192.0, 8192.0, on="S", f=AF.Relu)
+        out = aff(n32("out", B), a("b7", 96, 128), -8192.0, 8192.0, f=AF.Relu, v=(0.5, 8192.0, LT, MUL))
         pos = tt(n32("pos0"), a("b7", 96, 128), aff(n32("f16i"), f17, 4.0, 443.0 - 8 * par, on="S"), ADD)
         pos = tt(n32("pos2"), tt(n32("pos1"), pos, out, SUB), a("mA"), MAX)
         uP = cp(n32("uP", U), pos)
-        gr2 = aff(n32("gr2", B, 512), ind(a(TB, 0, 1025), uO), on="S", f=AF.Abs)
+        gr2 = aff(n32("gr2", B, 512), ind(a(TB, 0, 1025), uO), f=AF.Abs if t < 2 else None)
         conv(a("b6", 32, 64), "Ed", every("gr2" + s, 0, 512))
         for o, lo, hi in halves if t < 2 else ():
             mm(o, es("E0", 7), h("gr2", lo, hi), False, False)
         for k, bank in enumerate(("b6", "b7")):
             for j in (2 * k, 2 * k + 1):
-                tt(h("G4", 512 * j, 512 * j + 512), ind(a("W"), h("u4", 32 * j, 32 * j + 32)), Zq, MAX)
+                tt(h("G4", 512 * j, 512 * j + 512), ind(a("W", 16), h("u4", 32 * j, 32 * j + 32)), Zq, MAX)
                 run("W")
             o = a(bank, 128, 192)
             conv(o, "E64", every("G4" + s, 1024 * k, 1024 * k + 1024), False, True,
@@ -493,9 +532,9 @@ def rank_program(g, core, T, topo):
 
         def place(n, p, c, rest):
             v = tt(n32(n + "b", I, p[2]), tt(n32(n + "a", F, p[2]), p, c, MUL), rest, ADD)
-            return ts(n32(n, U, p[2]), ts(n32(n + "c", I, p[2]), v, 4095, AND), 16.0, ADD)
+            return cp(n32(n, U, p[2]), ts(n32(n + "c", I, p[2]), v, 4095, AND))
 
-        Do = tt(n32("Do", B, 512), ind(a("W"), place("uo", d, f20, f19)), Zq, MAX)
+        Do = tt(n32("Do", B, 512), ind(a("W", 16), place("uo", d, f20, f19)), Zq, MAX)
         run("W")
         for o, lo, hi in halves:
             mm(o, es("E2n", 0), h("Do", lo, hi), False, False)
@@ -510,24 +549,21 @@ def rank_program(g, core, T, topo):
         for (o, lo, hi), b in zip(halves, ("b4", "b0")):
             if late:
                 mms([(a(b, q, 256, 16), a("FH", 128 * q, 128 * q + 128), h("dp", lo // 16, hi // 16), False, False) for q in range(16)])
-            tt(h("Dn", lo, hi), ind(a("W"), h("un", lo // 16, hi // 16)), h("Zq", lo, hi), MAX)
+            tt(h("Dn", lo, hi), ind(a("W", 16), h("un", lo // 16, hi // 16)), h("Zq", lo, hi), MAX)
             mm(o, es("E2", 0), h("Dn", lo, hi), False, True)
             aff(h("hiT", lo, hi), o, odd, on="S")
             tt(h("yv", lo, hi), o, h("hiT", lo, hi), SUB)
             cp(ind(a("WK" + s), h("uP", lo // 16, hi // 16)), h("yv", lo, hi))
-        if t:
+        if t == 1 or (t and not MERGE):
             keys = members(TB, par, t == 1, True, ONGN[t])
         if t == 1:
             elect(2, 1, keys)
         aff(n32("LSh", H, 256), a(LS, 16), on="S")
         mms([(a("b7", 256 + 128 * k, 384 + 128 * k), h("LSh", 128 * k, 128 * k + 128), a("IDh"), True, True) for k in range(2)])
         aff(n32("LMT", F, 256), a("b7", 256, 512), on="S")
-        mms([(a("b7", 192 + 8 * k, 200 + 8 * k), a("onS", par + 256 * k, 256 * k + 256, 2), a("G8n" if par else "G8"), True, True) for k in range(2)])
         if t < 2:
-            n32("c15", F, 48)
-            aff(h("c15", 16, 32), a("b7", 192, 208), 1048576.0, -15728640.0, on="S", f=AF.Relu)
-            aff(h("c15", 32, 48), a("b7", 192, 208), -1024.0, 15360.0 + 0.5 * t, on="S")
-            tt(h("c15", 0, 16), h("c15", 32, 48), h("c15", 16, 32), SUB)
+            mms([(a("b7", 192 + 8 * k, 200 + 8 * k), a("onS", par + 256 * k, 256 * k + 256, 2), a("G8c"), True, True) for k in range(2)])
+            aff(n32("c15", F, 16), a("b7", 192, 208), 2.0 * par - 1.0, 15360.0 + 0.5 * t)
         for k in range(2):
             o, on = a("b7", 256 + 128 * k, 384 + 128 * k), a("onS", par + 256 * k, 256 * k + 256, 2)
             mms([(o, a("ones"), a("k0", 0, 128), True, False), (o, on, a("Shn" if par else "Sh"), False, False), (o, on, a("ID" if par else "IDn"), False, True)])
@@ -541,10 +577,10 @@ def rank_program(g, core, T, topo):
                 aff((k or n32("dD", B, 256)) and h("dD", 128 * k, 128 * k + 128), a(b, 256, 384))
             mms([(o, a("ones"), a("m37c"), True, False)] + [(o, a(n, 128 * k, 128 * k + 128), a("ID32"), False, n == parts[-1]) for n in parts])
         if not late:
-            pk = aff(n32("pk", B, 512), ind(a("W"), place("up", pn, h("c5", 32, 64), X2)), on=ONPK)
-        dm = aff(h("gs"), pn, on="S")
+            pk = aff(n32("pk", B, 512), ind(a("W", 16), place("up", pn, h("c5", 32, 64), X2)), on=ONPK)
+        dm = pn
         if t < 2:
-            send(dn, dm, h("gl"), "ag%d" % (t + 1), "lg%d" % (t + 1), up)
+            send(dn, aff(h("gs"), pn), h("gl"), "ag%d" % (t + 1), "lg%d" % (t + 1), up)
         o = a("b3", 256, 512)
         mms([(o, a("IDh"), a("x17%d" % par), True, False), (o, a("B32"), a(TB, 1 + par, 513, 2), False, True)])
         tt(n32("s0", F, 256), o, aff(n32("a37", F, 256), a(LS, 16), 2.0, 35.0, on="S"), MUL)
@@ -566,15 +602,17 @@ def rank_program(g, core, T, topo):
         for ch in range(4):
             scan(h("sc", 1024 * ch, 1024 * ch + 1024), a("mask"), h("GL", 512 + 1024 * ch, 1536 + 1024 * ch), MUL, MAX)
             run("sc")
-        o = a("b3", 0, 256)
-        if "z" in ONS[t]:
-            mms([(o, a("ones"), a("q25"), True, False), (o, a("id64"), a(zt, 16), False, False), (o, a("id64"), h("sc", 15, 4096, 16), False, True)])
-            ts(h("zs"), o, 12582912.0, SUB, -12582912.0, SUB)
-        else:
-            mms([(o, a("ID"), a(zt, 16), True, False), (o, a("ID"), h("sc", 15, 4096, 16), False, True)])
-            aff(n32("zf", F, 256), o, 0.4995, 12582912.0, on="S")
-            aff(h("zs"), h("zf"), 1.0, -12582912.0)
-        send((rank + 1 + t) % N, h("zs"), a("z%d" % (t + 1), 16), "az" + s, "lz" + s, (rank - 1 - t) % N)
+        n32("zf", I, 256)
+        w = 128 if "z" in ONS[t] else 256
+        for lo in range(0, 256, w):
+            o, n = a("b3", lo, lo + w), "zy"[lo // 128] + s
+            mms([(o, a("ID"), a(zt, 16 + lo, 16 + lo + w), True, False), (o, a("ID"), h("sc", 15 + 16 * lo, 16 * (lo + w), 16), False, True)])
+            cp(h("zs", lo, lo + w), aff(h("zf", lo, lo + w), o, 0.4995))
+            send((rank + 1 + t) % N, h("zs", lo, lo + w), a("z%d" % (t + 1), 16 + lo, 16 + lo + w), "a" + n, "l" + n, (rank - 1 - t) % N)
+            if t == 2:
+                v = a("z3", 16 + lo, 16 + lo + w)
+                dma("DS"[lo // 128], T.yz[:, lo:lo + w], v[0], [(v[1][0], False)], 256 * w)
+                steps[-1]["run"] = None
         n32("kw", I, 512)
         for k, b in enumerate(("b5", "b2")):
             scan(h("kw", 256 * k, 256 * k + 256), a("mask", 0, 256), a(b, 0, 256), MUL, MAX)
@@ -613,7 +651,14 @@ def rank_program(g, core, T, topo):
         aff(h("hs"), ind(h("hx"), a("oH")))
         send(up, h("hs"), h("hl"), "ah" + s, "lh" + s, dn)
         o1 = tt(n32("o1", F, 16), aff(n32("o4", F, 16), t1, 4.0, 1.0), ts(n32("l7", I, 16), kB, 1, SHR, 127, AND), ADD)
-        tt(n32("test", B, 256), ind(o1, a("o16")), h("LMT"), OP.not_equal)
+        n32("test", B, 256)
+        if "t" in ONS[t]:
+            for k in range(16):
+                aff(h("test", 16 * k, 16 * k + 16), a("b7", 256 + 16 * k, 272 + 16 * k) if "T" in ONS[t] else h("LMT", 16 * k, 16 * k + 16),
+                    -1.0, h("o1", k, k + 1), on="S", f=AF.Abs)
+                run("test")
+        else:
+            tt(h("test"), ind(o1, a("o16")), h("LMT"), OP.not_equal)
         scan(n32("out_", B, 256), a("k0"), h("test"), MAX, MIN)
         fresh = h("out_", 15, 256, 16)
         loc = tt(n32("loc0", F, 16), inj, gh, GT)
@@ -636,7 +681,7 @@ def rank_program(g, core, T, topo):
         mms([(o, a("IDh"), h("LSh"), True, False)]
             + [(a("b7", 256 + 128 * k, 384 + 128 * k), h("dl", 128 * k, 128 * k + 128), a("IDh"), False, k == 1) for k in range(2)])
         if t == 0:
-            aff(a("onS", 0, 512, 2), o, on="S", f=AF.Sign)
+            aff(a("onS", 0, 512, 2), o, f=AF.Sign, v=(1.0, None, MIN))
             cp(a("off0"), o)
             aff(a(LS, 16), o, on="S")
             new("ky", 512, F)
@@ -652,7 +697,7 @@ def rank_program(g, core, T, topo):
             aff(new("thK%d" % (t + 1), 16, F), a("thK0"), 1.0, aff(h("c0", 2, 3), c, 4096.0, v))
             v = ts(n32("gv1", I), tt(n32("gv0", I), h("gl"), h("hs"), ADD), 15, AND)
             ghosts(t + 1, cp(n32("gv2", B), v))
-        if t == 0:
+        if t == 0 and not MERGE:
             mms(sum(sizes("b4", True), []))
             aff(a("TK", 1, 513), a("b4"))
             elect(2, 0, members("TK", 0, True, False, ONK))
@@ -664,7 +709,6 @@ def rank_program(g, core, T, topo):
             o = cp(new("dF", 32, F), v)
             dma("D", T.yl[:, :], a("ky")[0], [(a("ky")[1][0], False)], 128 * 2048)
             dma("S", T.yd[:, :], o[0], [(o[1][0], False)], 128 * 128)
-            dma("D", T.yz[:, :], a("z3", 16)[0], [(a("z3", 16)[1][0], False)], 128 * 512)
 
     if "order" not in PLAN:
         PLAN["order"] = arrange(steps)
@@ -716,7 +760,7 @@ def arrange(steps):
         for j in after[k]:
             way[j] = max(way[j], way[k] - WAIT - min(cost[j].values()) / 2)
 
-    def place(way, deps, users, back):
+    def place(way, deps, users, back, SPARE, GRAB, FILL, HOLD):
         at, end, free, bank = {}, {}, {q: 0.0 for q in "VSPGD"}, {b: {} for b in BANKS}
         left = [len(d) for d in deps]
         pre, post = (late, [0.0] * n) if back else ([0.0] * n, late)
@@ -737,7 +781,7 @@ def arrange(steps):
             for u, k in sorted((c for c in cand[q] if c[0] <= t), key=lambda c: -way[c[1]]):
                 c = cost[k][q]
                 over = [t + c - v - FILL * (v - t) - HOLD for v, j in rivals if way[j] > way[k] and way[j] - way[k] > t + c - v]
-                if q == "V" and "S" in cost[k] and max(free["S"], t) + cost[k]["S"] < t + c + SPARE and not (c > 400 and free["S"] > t):
+                if q == "V" and "S" in cost[k] and max(free["S"], t) + cost[k]["S"] < t + c + SPARE and not (c > 400 and free["S"] > t and all(t + c - v < GRAB for v, j in rivals if len(cost[j]) == 1)):
                     continue
                 if max(over + [0]) <= 0:
                     pick = k
@@ -757,20 +801,22 @@ def arrange(steps):
                                    else end[j] + WAIT + pre[k] for j in deps[k])
         return at, end
 
-    PLAN["bound"], best, PLAN["ends"] = max(way), None, []
-    for _ in range(PASSES):
-        at, end = place(way, deps, users, False)
-        PLAN["ends"].append(round(max(end.values()) * .83e-3, 1))
-        if best is None or max(end.values()) < best[0]:
-            best = (max(end.values()), at, way)
-        way = place(end, users, deps, True)[1]
-    PLAN["end"], at, way = best
-    PLAN["hook"] = (place, way, deps, users)
     hard = [deps[k] if steps[k]["kind"] == "dma" else deps[k] - soft[k] for k in range(n)]
-    return polish(steps, hard, soft, [(k, at[k][1]) for k in sorted(at, key=lambda k: (at[k][0], k))])
+    PLAN["bound"], PLAN["ends"], tried = max(way), [], []
+    for rule in RULES:
+        best, w = None, way
+        for _ in range(PASSES):
+            at, end = place(w, deps, users, False, *rule)
+            if best is None or max(end.values()) < best[0]:
+                best = (max(end.values()), at)
+            w = place(end, users, deps, True, *rule)[1]
+        PLAN["end"], at = best
+        tried.append(polish(steps, hard, soft, [(k, at[k][1]) for k in sorted(at, key=lambda k: (at[k][0], k))], MOVES[0], HEAT[0]))
+        PLAN["ends"].append(PLAN["rates"])
+    return polish(steps, hard, soft, min(tried)[1], MOVES[1], HEAT[1])[1]
 
 
-def polish(steps, deps, soft, order):
+def polish(steps, deps, soft, order, moves, heat):
     n = len(steps)
     users = [[] for _ in steps]
     for k in range(n):
@@ -779,37 +825,54 @@ def polish(steps, deps, soft, order):
     wait = [[j for j in deps[k] if j not in soft[k] and not ("P" in steps[j]["alts"] and "P" in steps[k]["alts"])] for k in range(n)]
     banks = [sorted({int(b[1]) for (b, _, _), _ in s["acc"] if b in BANKS}) for s in steps]
     first = [s["kind"] for s in steps].index("send")
-    late = [-s["late"] if s["kind"] == "dma" else s["late"] + WAIT for s in steps]
+    late = [-s["late"] if s["kind"] == "dma" else s["late"] for s in steps]
     busy = [[{q: c + (FIRST if k == first else 0) if s["kind"] else f * (c + (ga - GATHER) * s["n"][0] + (sc - SCATTER) * s["n"][1])
-              for q, (c, _) in s["alts"].items()} for k, s in enumerate(steps)] for f, ga, sc in RATES]
+              for q, (c, _) in s["alts"].items()} for k, s in enumerate(steps)] for f, ga, sc, w in RATES]
+    busy = [[{q: (c, r[3] * (max(late[k], 0) + LAG[q])) for q, c in v.items()} for k, v in enumerate(b)] for b, r in zip(busy, RATES)]
 
-    def replay(order, busy, was, at):
-        end, marks = list(was[1]), was[2][:at // 32 + 1]
-        free, bq, be, bo = [type_(v) for type_, v in zip((dict, list, list, list), marks[-1])]
-        for p in range(at // 32 * 32, n):
-            if p % 32 == 0 and p // 32 == len(marks):
+    def replay(order, busy, was, at, begin=None, reach=n, last=None):
+        end, marks = list(was[1]), was[2][:at // 24 + 1]
+        free, bq, be, bo = marks[-1]
+        free, bq, be, bo = dict(free), list(bq), list(be), list(bo)
+        for p in range(at // 24 * 24, n, 24):
+            if p // 24 == len(marks):
+                if p >= reach and was[2][p // 24] == (free, bq, be, bo):
+                    return max(end), end, marks + was[2][p // 24:]
                 marks.append((dict(free), list(bq), list(be), list(bo)))
-            k, q = order[p]
-            t = free[q]
-            for j in wait[k]:
-                if end[j] > t:
-                    t = end[j]
-            for b in banks[k]:
-                v = be[b] if bq[b] != q else bo[b]
-                if v > t:
-                    t = v
-            free[q] = e = t + busy[k][q]
-            if late[k] < 0:
-                free["M"] = e = max(t + DMA0, free["M"]) - late[k]
-                e += WAIT
-            else:
-                e += late[k]
-            end[k] = e
-            for b in banks[k]:
-                if bq[b] != q:
-                    bo[b], bq[b] = be[b], q
-                be[b] = e
+            for k, q in order[p:p + 24]:
+                t = free[q]
+                for j in wait[k]:
+                    if end[j] > t:
+                        t = end[j]
+                bs = banks[k]
+                for b in bs:
+                    v = be[b] if bq[b] != q else bo[b]
+                    if v > t:
+                        t = v
+                if begin is not None:
+                    begin[k] = (t, len(begin))
+                c, after = busy[k][q]
+                free[q] = e = t + c
+                if late[k] < 0:
+                    free["M"] = e = max(t + DMA0, free["M"]) - late[k]
+                e += after
+                if e != end[k]:
+                    end[k] = e
+                    if last and last[k] >= reach:
+                        reach = last[k] + 1
+                for b in bs:
+                    if bq[b] != q:
+                        bo[b], bq[b] = be[b], q
+                    be[b] = e
         return max(end), end, marks
+
+    def lasts(order):
+        last = [0] * n
+        for p, (k, q) in enumerate(order):
+            for j in wait[k]:
+                last[j] = p
+        return last
+
 
     start = (0, [0.0] * n, [({q: 0.0 for q in "VSPGDM"}, [""] * 8, [0.0] * 8, [0.0] * 8)])
     now = [replay(order, b, start, 0) for b in busy]
@@ -824,30 +887,53 @@ def polish(steps, deps, soft, order):
         out, t = [], max(end)
         for p in reversed(range(n)):
             k, q = order[p]
-            if abs(end[k] - t) < 0.01 or (out and q == out[-1][1] and late[k] >= 0 and abs(end[k] - late[k] - t) < 0.01):
+            if abs(end[k] - t) < 0.01 or (out and q == out[-1][1] and late[k] >= 0 and abs(end[k] - busy[k][q][1] - t) < 0.01):
                 out.append((k, q))
-                t = end[k] - late[k] - busy[k][q] if late[k] >= 0 else max([end[j] for j in wait[k]] + [-1])
+                t = end[k] - sum(busy[k][q]) if late[k] >= 0 else max([end[j] for j in wait[k]] + [-1])
         return out
 
-    score = best = 1.0
+    def value(then):
+        return sum((v[0] + EARLY * sum(v[1]) / n) / u for v, u in zip(then, unit)) / len(unit)
+
+    score = best = value(now)
     kept = order
-    for it in range(MOVES):
+    for it in range(moves):
         if it % 24 == 0:
             m = it // 24 % len(busy)
-            hot = chain(order, busy[m], now[m][1])
-            PLAN["hot"] = len(hot)
+            if it % 480 == 0:
+                begin = {}
+                replay(order, busy[0], start, 0, begin)
+                new = sorted(order, key=lambda v: begin[v[0]])
+                then = [replay(new, b, start, 0) for b in busy]
+                if value(then) <= score + 1e-9:
+                    order, now = new, then
+            hot, last = chain(order, busy[m], now[m][1]), [p + 40 for p in lasts(order)]
+            held = [(u, v) for u, v in zip(hot, hot[1:]) if u[1] == v[1] and v[0] not in deps[u[0]]]
         i = int(draw() * n)
-        if draw() < 0.7:
-            k = hot[int(draw() * len(hot))][0]
-            i = [v[0] for v in order].index(k)
-        k, q = order[i]
         r, d = draw(), 1 + int(-12 * math.log(draw()))
+        if draw() < 0.7 and hot[0] in order:
+            u = hot[int(draw() * len(hot))]
+            if u not in order:
+                continue
+            i = order.index(u)
+        k, q = order[i]
+        if r > 1 - SWAP and held:
+            u, v = held[int(draw() * len(held))]
+            if u not in order or v not in order:
+                continue
+            i, j = order.index(u), order.index(v)
+            if j > i:
+                continue
+            d, r = i - j, 0.5
+            if draw() < 0.4:
+                i, r = j, 0.55
+            k, q = order[i]
         if r < 0.15:
             if len(steps[k]["alts"]) == 1:
                 continue
-            lo, new = i, order[:i] + [(k, "V" if q == "S" else "S")] + order[i + 1:]
+            lo, hi, new = i, i + 1, order[:i] + [(k, "V" if q == "S" else "S")] + order[i + 1:]
         else:
-            back = draw() < 0.6
+            back = r == 0.5 or (r != 0.55 and draw() < 0.6)
             if r > 0.6:
                 d, m, w = 0, 1 + d // 8, -1 if back else 1
                 while m and 0 <= i + w * (d + 1) < n:
@@ -860,20 +946,20 @@ def polish(steps, deps, soft, order):
                     drag.add(j)
             x, y = [v for v in order[lo:hi] if v[0] in drag], [v for v in order[lo:hi] if v[0] not in drag]
             new = order[:lo] + (x + y if back else y + x) + order[hi:]
-        limit = score - HEAT * (1 - it / MOVES) * math.log(draw())
+        limit = score - heat * (1 - it / moves) * math.log(draw())
         then = []
         for b, w, u in zip(busy, now, unit):
-            then.append(replay(new, b, w, lo))
+            then.append(replay(new, b, w, lo, None, hi, last))
             if then[-1][0] > w[0] + 3 * u * (limit - score) + CUT * u:
                 break
         else:
-            e = sum(v[0] / u for v, u in zip(then, unit)) / len(unit)
+            e = value(then)
             if e <= limit:
                 score, order, now = e, new, then
                 if e < best:
                     best, kept = e, new
     PLAN["rates"] = [round(replay(kept, b, start, 0)[0] * .83e-3, 1) for b in busy]
-    return kept
+    return sum(math.log(v) for v in PLAN["rates"]), kept
 
 
 def issue(g, core, T, topo, eng, steps, plan):

import math
from concourse.mybir import AluOpType, ActivationFunctionType

F, B, H, I, U = "float32", "bfloat16", "float16", "int32", "uint16"
POOL = {F: 10240, B: 36352, H: 4096, I: 8704, U: 3072}
OWN = {"valI": (32, I), "gI0": (32, I), "z0": (272, B), "z1": (272, B), "z2": (272, B), "z3": (272, B)}
for _t in range(3):
    for _n in ("gs", "gl", "hs", "hl"):
        OWN[_n + str(_t)] = (32, B)
    OWN["zs%d" % _t] = (256, B)
    OWN["WK%d" % _t] = (4608, B)
OWN.update({"W": (4112, B), "GN0": (4096, B), "GN1": (4096, B), "GL": (4608, B), "sc": (4096, B)})
SCRATCH = {"p" + _d: ("sbuf", [128, _c], _d) for _d, _c in POOL.items()}
SCRATCH.update({_n: ("sbuf", [128, _c], _d) for _n, (_c, _d) in OWN.items()})
BANKS = ["b%d" % _b for _b in range(8)]
SCRATCH.update({_b: ("psum", [128, 512], F) for _b in BANKS})
SEMAPHORES = ["sV", "sS", "sP", "sG"] + ["d%d" % i for i in range(20)] + [a + str(t) for a in ("az", "ay", "ah", "ag", "lz", "ly", "lh", "lg") for t in range(3)]

GATHER, SCATTER, LEAST, WAIT, REMOTE, FIRST, DMA0, DMABYTES = 1.56, 3.8, 64, 210, 1600, 2400, 1800, 200.0
LAG = {"V": 240, "S": 200, "P": 170, "G": 170, "D": 170}
RULES, PASSES = ((300, 300, 0.5, 200), (300, 600, 1.0, 60)), 4
ONGN, ONGL = ("VS", "VS", "VS"), ("VS", "VS", "VS")
HALF = FREE = True
OPEN = ("b0", "b2", "b4")
MORE = {}
CUT, MERGE, SWAP, EARLY = 0.004, False, 0.3, 0.1
RATES, MOVES, HEAT, SEED = ((1.0, 1.5, 3.6, 0.9), (1.25, 1.25, 4.6, 1.0), (1.3, 1.85, 3.0, 0.9)), (2000, 170000), (0.0002, 0.0004), 1
ONS, ONK, ONPK = ("r", "r", "r"), "VS", "VS"
SOUT = (F, B, H, I, U)
BIG = ("TB0",)
PLAN = {}


def rank_program(g, core, T, topo):
    rank = T.rank_of(core)
    if rank is None:
        return
    N = len(T.cores)
    OP, AF = AluOpType, ActivationFunctionType
    ADD, SUB, MUL, MAX, MIN = OP.add, OP.subtract, OP.mult, OP.max, OP.min
    GT, GE, LT, EQ = OP.is_gt, OP.is_ge, OP.is_lt, OP.is_equal
    SHR, AND = OP.arith_shift_right, OP.bitwise_and
    eng = {"V": g.vector, "S": g.scalar, "P": g.tensor, "G": g, "D": g.sync}
    up, dn = (rank + 1) % N, (rank - 1) % N

    tiles, top, named, now = {}, {d: 0 for d in POOL}, {}, ["/"]
    for n, (c, d) in OWN.items():
        tiles[n] = (n, 0, c, d)
    for n in BANKS:
        tiles[n] = (n, 0, 512, F)

    def new(n, c, d):
        if n in OWN:
            return a(n)
        tiles[n] = ("p" + d, top[d], c, d)
        top[d] += -(-c // 16) * 16
        assert top[d] <= POOL[d], (d, top)
        return a(n)

    def a(n, lo=0, hi=None, st=1):
        b, o, c, d = tiles[n]
        hi = c if hi is None else min(hi, c)
        ap = T[b][:, o + lo:o + hi:st] if st > 1 else T[b][:, o + lo:o + hi]
        named[(b, o + lo, o + hi)] = n + ("@%d" % lo if b in BANKS else "")
        return (ap, [(b, o + lo, o + hi)], len(range(lo, hi, st)), d, "P" if b in BANKS else "S")

    def top8(n, lo=0, hi=None):
        v = a(n, lo, hi)
        b, lo, hi = v[1][0]
        return (T[b][0:8, lo:hi],) + v[1:]

    def ind(w, o):
        return (w[0].indirect(o[0]), w[1] + o[1], 16 * o[2], w[3], "I")

    def x(v):
        return v if v is None or isinstance(v, (int, float)) else v[0]

    steps = []

    def spans(o, ins):
        r = [(s, False) for v in ins if v is not None and not isinstance(v, (int, float)) for s in v[1]]
        if o[4] == "I":
            return r + [(o[1][0], True), (o[1][1], False)]
        return r + [(o[1][0], True)]

    def step(alts, acc, late=0, kind=None, o=None, ins=()):
        gather = any(v is not None and not isinstance(v, (int, float)) and v[4] == "I" for v in ins)
        steps.append({"n": (o[2] if gather else 0, o[2] if o and o[4] == "I" else 0), "alts": alts, "acc": acc, "late": late, "kind": kind, "run": None, "name": named.get(acc[-1][0], named.get(acc[0][0])) + now[0]})

    def run(name):
        steps[-1]["run"] = name

    def vcost(o, ins, two=False):
        full = [v for v in ins if v is not None and not isinstance(v, (int, float)) and v[2] > 1]
        if o[4] == "I":
            return 60 + SCATTER * o[2]
        if any(v[4] == "I" for v in full):
            return 60 + GATHER * o[2]
        if two:
            return max(LEAST, o[2] * (2 if all(v[4] == "S" for v in full) else 1))
        return max(LEAST, o[2] * (0.5 if all(v[3] in (B, H, U) for v in full + [o]) else 1))

    def vec(o, ins, call, two=False):
        acc = spans(o, ins)
        step({"V": (vcost(o, ins, two), [(acc, call)])}, acc, o=o, ins=ins)

    def ts(o, i, s1, op0, s2=None, op1=None):
        if o[3] in SOUT and (op0, op1) in ((ADD, None), (MUL, None), (MUL, ADD)):
            aff(o, i, *((1.0, s1) if op0 == ADD else (s1, s2 or 0.0)))
        elif op1 is None:
            vec(o, [i, s1], lambda e: e.tensor_scalar(o[0], i[0], x(s1), None, op0))
        else:
            vec(o, [i, s1, s2], lambda e: e.tensor_scalar(o[0], i[0], x(s1), x(s2), op0, op1))
        return o

    def tt(o, i, j, op):
        vec(o, [i, j], lambda e: e.tensor_tensor(o[0], i[0], j[0], op), True)
        return o

    def cp(o, i):
        if o[3] in SOUT and o[4] != "I":
            return aff(o, i)
        vec(o, [i], lambda e: e.tensor_copy(o[0], i[0]))
        return o

    def fill(o, c):
        vec(o, [], lambda e: e.memset(o[0], c))
        return o

    def scan(o, d0, d1, op0, op1):
        vec(o, [d0, d1], lambda e: e.tensor_tensor_scan(o[0], d0[0], d1[0], 0.0, op0, op1))
        return o

    def aff(o, i, scale=1.0, bias=0.0, on="VS", f=None, v=None):
        acc, alts = spans(o, [i, scale, bias]), {}
        if f is None and FREE:
            on = "VS"
        if v is not None:
            alts["V"], on = (vcost(o, [i]), [(acc, lambda e: e.tensor_scalar(o[0], i[0], *v))]), "S"
        plain = scale == 1.0 and bias == 0.0
        if "V" in on and f is None:
            if plain:
                alts["V"] = (vcost(o, [i]), [(acc, lambda e: e.tensor_copy(o[0], i[0]))])
            else:
                alts["V"] = (vcost(o, [i]), [(acc, lambda e: e.tensor_scalar(o[0], i[0], x(scale), x(bias), MUL, ADD))])
        if "S" in on:
            fn = f if f is not None else AF.Copy if bias == 0.0 else AF.Identity
            c = 80 + GATHER * o[2] if i[4] == "I" else max(LEAST, o[2])
            alts["S"] = (c, [(acc, lambda e: e.activation(o[0], i[0], fn, bias=x(bias), scale=x(scale)))])
        step(alts, acc, o=o, ins=[i])
        return o

    def mms(calls):
        sub = [(spans(o, [l, r]), lambda e, o=o, l=l, r=r, s0=s0, s1=s1: e.matmul(o[0], l[0], r[0], s0, s1)) for o, l, r, s0, s1 in calls]
        step({"P": (sum(max(64, c[2][2]) * (4 if c[2][3] == F else 1) for c in calls), sub)}, [s for u in sub for s in u[0]])

    def mm(o, l, r, start=True, stop=True):
        mms([(o, l, r, start, stop)])

    def iota(o, pat, base=0, cm=0):
        acc = spans(o, [])
        step({"G": (160 + 2 * o[2], [(acc, lambda e: e.iota(o[0], pat, base, cm, allow_small_or_imprecise_dtypes=True))])}, acc)
        run("G")
        return o

    def keep(o, i, pat, op, base, cm, c):
        acc = spans(o, [i])
        step({"G": (205 + 2 * o[2], [(acc, lambda e: e.affine_select(o[0], i[0], pat, op, c, base, cm))])}, acc)
        run("G")
        return o

    def dma(q, out, in_, acc, size):
        step({q: (60, [(acc, lambda e: e.dma_start(out, in_))])}, acc, late=size / DMABYTES, kind="dma")
        run(q)

    def send(dst, buf, rbuf, arr, loc, src):
        step({"G": (400, [(buf, rbuf, arr, loc, dst, src)])}, [(buf[1][0], False), (rbuf[1][0], True)], late=REMOTE + 3 * buf[2], kind="send")

    def es(E, q):
        return a(E, 15 - q, 143 - q)

    def conv(o, E, src, first=True, last=True, pre=()):
        mms(list(pre) + [(o, es(E, q), src(q), first and q == 0, last and q == 15) for q in range(16)])

    def every(n, lo, hi):
        return lambda q: a(n, lo + q, hi, 16)

    def rows(bank, src, alone, last=True):
        mms([(a(bank, 32 * q, 32 * q + 32), a("FH", 128 * q, 128 * q + 128), src, alone, alone or (last and q == 15)) for q in range(16)])

    def col(n, k=0):
        return a(n, k, k + 1)

    def load(q, v, src):
        dma(q, v[0], src, [(v[1][0], True)], 128 * v[2] * (4 if v[3] == I else 2))

    load("S", a("valI"), T.val[:, :])
    load("D", new("glI", 512, I), T.gl[:, :])
    new("thI", 256, I)
    dma("D", top8("thI")[0], T.th[:, :], [(a("thI")[1][0], True)], 8192)
    load("D", new("nbI", 512, I), T.nb[:, :])
    load("D", a("z0", 16), T.zl[:, :])
    new("W", 4112, B)
    load("D", a("W", 16), T.rec[:, :])

    new("ci", 16, I)
    iota(col("ci"), [[0, 1]], 0, 1)
    iota(new("X", 256, F), [[1, 256]])
    iota(new("x8", 128, B), [[0, 16], [1, 8]])
    new("pt", 64, F)
    iota(a("pt", 48, 64), [[16, 2], [1, 8]])
    iota(new("j16", 128, B), [[16, 4], [0, 32]])
    send(dn, a("valI"), a("gI0"), "ag0", "lg0", up)
    run("G")
    iota(new("x16", 256, B), [[1, 16], [0, 16]])
    iota(new("Mrow", 512, F), [[1, 32], [32, 16]], 1)
    iota(a("pt", 0, 32), [[1, 16], [0, 2]])
    iota(new("x32", 512, B), [[0, 16], [1, 32]])
    for n, (op, c) in enumerate(((AND, 15), (AND, 112), (SHR, 4), (AND, 8))):
        ts(col("ci", n + 1), col("ci"), c, op)
    new("cf", 16, F)
    cp(a("cf", 0, 5), a("ci", 0, 5))
    pf, r, g16, gg, r8 = [col("cf", k) for k in range(5)]
    new("cc", 32, F)
    used = [0]

    def cc(i, scale, bias=0.0):
        used[0] += 1
        return aff(col("cc", used[0]), i, scale, bias)

    ts(new("I16", 16, F), a("X", 0, 16), r, EQ)

    def isr(q):
        return col("I16", q)

    ts(new("E1", 144, B), a("X", 0, 144), cc(g16, 1.0, 15.0), EQ)
    for q in range(16):
        if q == 0:
            new("FH", 2048, B)
        aff(a("FH", 128 * q, 128 * q + 128), es("E1", 2), isr(q), on="S" if q % 3 == 2 else "V")
    ts(new("ID", 128, B), a("X", 0, 128), pf, EQ)
    s01 = cc(isr(0), 1.0, isr(1))
    new("Kc", 512, B)
    aff(a("Kc", 0, 512, 2), a("X"), isr(1), s01)
    aff(a("Kc", 1, 512, 2), a("Kc", 0, 512, 2), -1.0)
    keep(new("Ed", 144, B), a("E1"), [[1, 144]], EQ, -13, -1, 0.0)
    fill(a("WK2", 512, 1024), 0.0)
    for src, dst in ([(("WK2", 512, 512 + n), ("WK2", 512 + n, 512 + 2 * n)) for n in (512, 1024)]
                     + [(("WK2", 512, 2560), (n, lo, lo + 2048)) for n, lo in (("WK0", 512), ("WK0", 2560), ("WK2", 2560), ("WK1", 512), ("WK1", 2560))]):
        dma("D", a(*dst)[0], a(*src)[0], [(a(*src)[1][0], False), (a(*dst)[1][0], True)], 256 * a(*dst)[2])

    def diag(n, c):
        keep(new(n, 128, B), a("WK2", 512, 640), [[-1, 128]], OP.not_equal, 0, 1, c)

    for t in range(3):
        new("TB%d" % t, 1040, B)
        aff(col("TB%d" % t), isr(2), -128.0, isr(4))
        iota(a("z%d" % t, 0, 16), [[0, 16]])

    new("onS", 512, B)
    for par in range(2):
        gp = a("glI", par, 512, 2)
        aff(a("onS", par, 512, 2), gp, 1.0 - 2 * par, 1.0 - 2 * par, f=AF.Sign, v=(0.0, 1.0 - 2 * par, GE, MUL))
        ts(new("off%d" % par, 256, U), gp, 1.0, ADD)
        new("LS%d" % par, 272, F)
        iota(a("LS%d" % par, 0, 16), [[0, 16]])
        ts(a("LS%d" % par, 16), gp, 1.0, ADD)
    cp(new("d0", 32, B), a("valI"))

    def sizes(bank, stop):
        return [(a(bank), a("ID"), a("Kc"), True, False)], [(a(bank), es("E1", 0), a("onS"), False, stop)]

    def table(t):
        if t < 2 or MERGE:
            mms(sizes("b0", False)[0])
        if t == 1 or (t and MERGE):
            mms(sizes("b0", False)[1])
        rows("b0", a("d%d" % t), t == 2 and not MERGE, t > 0)
        if t == 0:
            mms(sizes("b0", True)[1])
        aff(a("TB%d" % t, 1, 513), a("b0"))

    def table2(t):
        for k, b in enumerate(("b0", "b2")):
            lo, o = 256 * k, a(b, 0, 256)
            if t < 2:
                mm(o, a("ID"), a("Kc", lo, lo + 256), True, False)
            if t == 1:
                mm(o, es("E1", 0), a("onS", lo, lo + 256), False, False)
            mms([(a(b, 32 * q, 32 * q + 32), a("FH", 128 * (q + 8 * k), 128 * (q + 8 * k) + 128), a("d%d" % t), t == 2, t == 2 or (t == 1 and q == 7))
                 for q in range(8)])
            if t == 0:
                mm(o, es("E1", 0), a("onS", lo, lo + 256), False, True)
            aff(a("TB%d" % t, 1 + lo, 257 + lo), o)

    if HALF:
        table = table2

    def ghosts(t, src):
        rows("b0", src, True)
        aff(a("TB%d" % t, 513, 1025), a("b0"))

    def members(tab, par, keys, values, on):
        n = "GN%d" % par
        bank, lo, w = ("b2", 0 if keys else 128, 256) if values else ("b5", 256, 128)
        big = 2 if tab in BIG else 1
        for ch in range(big - 1, 8, big):
            aff(a(n, 512 * (ch + 1 - big), 512 * ch + 512), ind(a(tab, 0, 513), a("off%d" % par, 32 * (ch + 1 - big), 32 * ch + 32)), on=on)
            run(tab)
            k = ch // 4
            if ch % 4 == 3:
                mms([(a(bank, lo + w * k + q, lo // w * w + w * k + w, 16), a(n, 2048 * k + q, 2048 * k + 2048, 16),
                      a("WK16" if tab == "TB0" else "WKD", 0 if keys else 8, 16 if values else 8), True, True) for q in range(16)])
                if values:
                    aff(a("dM", 128 * k, 128 * k + 128), a(bank, 256 * k + 128, 256 * k + 256))
        return [a(bank, lo + w * k, lo + w * k + 128) for k in range(2)]

    def elect(t, par, src):
        for k in range(2):
            lo = 256 * par + 128 * k
            scan(a("ks%d" % t, lo, lo + 128), a(("add16", "sub16", "addp")[t]), src[k], ADD, MIN if t & 1 else MAX)
        o, i = a("key%d" % t, 16 * par, 16 * par + 16), a("ks%d" % t, 256 * par + 15, 256 * par + 256, 16)
        if t == 1:
            aff(o, i, -0.0625, 0.46875, on="S", f=AF.Relu)
        else:
            aff(o, i, f=AF.Relu, v=(0.0, None, MAX))

    for n, c in (("GN0", 4096), ("GN1", 4096), ("G4", 2048), ("GL", 4608), ("sc", 4096)):
        for t in ("", "0", "1", "2") if n[1] != "N" else ("",):
            tiles[n + t] = tiles[n] if t else new(n, c, B) and tiles[n]
    table(0)
    new("mask", 1024, B)
    keep(a("mask", 0, 256), a("WK2", 512, 768), [[0, 16], [1, 16]], EQ, 0, 0, 1.0)
    for n, c in (("add16", 16384), ("sub16", -16384), ("addp", 1024)):
        keep(iota(new(n, 128, F), [[0, 128]], c), a(n), [[0, 8], [1, 16]], GT, 0, 0, -8388608.0 if c > 0 else 8388608.0)
    for t in range(3):
        new("key%d" % t, 32, I)
        new("ks%d" % t, 512, F)
    ts(new("G8", 8, B), a("X", 0, 8), gg, EQ)
    new("WKD", 16, B)
    aff(a("WKD", 0, 8), a("G8"), cc(isr(0), 16384.0, isr(1)))
    aff(a("WKD", 8, 16), a("G8"), isr(2))
    new("WK16", 16, B)
    aff(a("WK16", 0, 8), a("G8"), cc(isr(0), 262144.0, cc(isr(1), 16.0, cc(isr(4), 128.0, isr(2)))))
    aff(a("WK16", 8, 16), a("G8"), isr(2))
    new("dM", 256, B)
    fill(new("ones", 128, B), 1.0 / 128)
    iota(new("m37c", 128, B), [[0, 128]], -37)
    diag("ID32", 32.0)
    iota(new("j8", 128, B), [[1, 4], [0, 32]], -8)
    diag("ID8n", -8.0)
    keep(new("B32", 128, B), a("WK2", 512, 640), [[-16, 8], [0, 16]], OP.not_equal, -2, 1, 32.0)
    aff(new("TK", 528, B) and col("TK"), isr(2), 0.0)
    keys = [members("TB0", 0, True, True, ONGN[0]), members("TB0", 1, True, False, ONGN[0])]
    for t in range(2):
        for par in range(2):
            elect(t, par, keys[par])

    ts(new("mA", 32, F), a("X", 0, 32), cc(r, 32.0), ADD)
    for n, c in (("m17", 17.0), ("m37", 37.0), ("m613", 613.0)):
        aff(new(n, 32, F), a("mA"), 2.0, c)
    for par in range(2):
        aff(new("x17%d" % par, 256, H), a("X"), 4.0, 17.0 + 2 * par)
        iota(new("x613%d" % par, 256, F), [[4, 256]], 613 + 2 * par)
    cp(new("o16", 16, U), a("X", 0, 16))
    cp(new("o32", 32, U), a("pt", 0, 32))
    ts(new("oMT", 16, U), a("pt", 48, 64), r8, ADD)
    ts(new("oH", 2, U), a("X", 0, 32, 16), cc(g16, 2.0, r), ADD)
    aff(new("E64", 144, B), a("E1"), 64.0)
    aff(new("Es", 144, B), a("E1"), cc(r, 1.0, 1.0))
    keep(new("E0", 144, B), a("E1"), [[1, 144]], EQ, -15, -1, 0.0)
    cp(new("Eh", 144, H), a("E1"))

    def total(o, parts):
        p = a("b3", 256, 256 + o[2])
        mms([(p, a("ID"), v, k == 0, k == len(parts) - 1) for k, v in enumerate(parts)])
        aff(o, p, on="S")

    new("E2", 144, B)
    total(a("E2", 8, 144), [a("E1", 8, 144), a("E1", 7, 143)])
    new("E2n", 144, B)
    aff(a("E2n", 8), a("E2", 8), -1.0)
    new("E2h", 144, H)
    cp(a("E2h", 8), a("E2", 8))
    aff(new("w1", 128, B), es("E2", 4), 49152.0)
    aff(new("w2", 128, B), es("E1", 3), cc(r, -1.0, 15.0))
    total(new("Weq", 128, B), [a("w1"), a("w2"), es("E1", 6)])
    diag("ID64", 64.0)
    diag("IDn", -1.0)
    keep(new("k0", 256, B), a("WK2", 512, 768), [[0, 16], [1, 16]], OP.not_equal, 0, 0, 1.0)
    keep(new("Sh", 128, B), a("mask", 0, 128), [[-1, 128]], EQ, 1, 1, 0.0)
    aff(new("Shn", 128, B), a("Sh"), -1.0)
    cp(new("IDh", 128, H), a("ID"))
    iota(new("ones8", 128, B), [[0, 128]], 8)
    iota(new("c46", 16, B), [[0, 16]], 4608)
    keep(new("tri", 128, B), a("ones8"), [[1, 128]], GT, 0, -1, 0.0)
    keep(new("TRI", 128, B), a("tri"), [[1, 128]], OP.not_equal, 0, -1, -512.0)
    for k in range(1, 4):
        keep(a("mask", 256 * k, 256 * k + 256), a("WK2", 512, 768), [[0, 16], [1, 16]], EQ, 0, 0, 1.0)
    iota(a("W", 0, 16), [[0, 16]])
    aff(new("G8c", 8, B), a("G8"), cc(isr(15), 1047552.0, 1024.0))
    w = cc(isr(3), 256.0, cc(s01, 4096.0))
    new("WAB", 24, B)
    aff(a("WAB", 0, 16, 2), a("G8"), cc(isr(4), 0.125, cc(isr(7), 1.0, cc(isr(6), -6144.0, w))))
    aff(a("WAB", 1, 16, 2), a("G8"), cc(isr(5), 1.0, cc(isr(6), 127.0, w)))
    aff(a("WAB", 16, 24), a("G8"), isr(2))
    odd = cc(isr(1), 1.0, isr(5))
    ts(new("MK2", 128, B), a("x8"), gg, EQ)
    aff(new("R2", 16, B), a("I16"))
    iota(new("xQ", 256, B), [[0, 16], [8, 16]], 128)
    if any("g" not in v for v in ONS):
        new("QT", 272, B)
        iota(a("QT", 0, 16), [[0, 16]])
        ts(a("QT", 16), a("x16"), r, EQ)
    ts(new("nbh", 512, H), a("nbI"), 2.0, MUL, -127.0, ADD)
    mms([(a("b1", q, 512, 16), a("IDh"), a("nbh", 32 * q, 32 * q + 32), True, True) for q in range(16)])
    new("thF", 256, F)
    cp(top8("thF"), top8("thI"))
    keep(new("I8", 8, F), a("X", 0, 8), [[0, 8]], GT, 0, 0, 0.0)
    keep(a("I8"), a("I8"), [[-1, 8]], OP.not_equal, 0, 1, 1.0)
    mms([(a("b7", 208 + 8 * k, 216 + 8 * k), top8("thF", 128 * k, 128 * k + 128), top8("I8"), True, True) for k in range(2)])
    aff(new("thK0", 16, F), a("b7", 208, 224), 4096.0, 4095.0)
    ghosts(0, cp(new("gb0", 32, B), a("gI0")))

    for t in range(3):
        par, s = t & 1, str(t)
        now[0] = "/" + s
        LS, TB, zt, d, key = "LS%d" % par, "TB" + s, "z" + s, a("d" + s), a("key" + s)

        def n32(n, dt=F, c=32):
            if t == 2 and c >= 128 and n + "0" in tiles:
                tiles[n + s] = tiles[n + "0"]
                return a(n + s)
            return new(n + s, c, dt)

        def h(n, lo=0, hi=None, st=1):
            return a(n + s, lo, hi, st)

        if t == 2 and MERGE:
            elect(2, 0, members(TB, 0, True, True, ONGN[t]))
        n32("i1", I)
        n32("ex", B, 256)
        for p2 in (par, 1 - par):
            kp = a("key" + s, 16 * p2, 16 * p2 + 16)
            for n, at, op in ((("i1", 224, (4, SHR, 1023, AND)), ("de", 0, (15, AND))) if t == 0 else (("i1", 224, (1023, AND)),)):
                if n == "de" and p2 == par:
                    n32("de", I)
                    n32("dex", B, 256)
                v, e = ts(h(n, 16 * p2, 16 * p2 + 16), kp, *op), h("ex" if n == "i1" else "dex", 128 * p2, 128 * p2 + 128)
                mm(a("b6", at + p2, at + 32, 2), tt(e, ind(v, a("oMT", 0, 8)), a("MK2"), MUL), a("R2"))
        i1 = a("b6", 224, 256)
        uZ = ts(n32("uZ", U), i1, 15.0, ADD)
        if t == 0:
            pass
        elif "g" in ONS[t]:
            uE = ts(n32("uE", U), i1, 2.0, MUL, par - 1.0, ADD)
        else:
            uE = cp(n32("uE", U), ts(n32("vc", I), ts(n32("vI", I), i1, 2.0, MUL, par - 2.0, ADD), 31, AND))
            row = aff(n32("row", B, 512), ind(a("QT"), uZ), on="S")
        n32("sg", B, 128)
        for j in range(4):
            aff(h("sg", 32 * j, 32 * j + 32), d, 1.0, j - 15.5, on="S", f=AF.Sign)
        o = a("b4", 256, 384)
        mms([(o, a("ID"), a("j8"), True, False)] + [(a("b4", 256 + 32 * j, 288 + 32 * j), a("ID"), d, False, False) for j in range(4)]
            + [(o, a("ID8n"), h("sg"), False, True)])
        aff(n32("p4", B, 128), o, on="S")
        if t == 0:
            pass
        elif "g" in ONS[t]:
            aff(n32("gr", B, 512), ind(a(TB, 0, 513), uE))
            conv(a("b6", 0, 32), "Ed", every("gr" + s, 0, 512))
        else:
            tt(n32("gr", B, 512), ind(a("dv1%d" % (t - 1) if t else "valI"), uE), row, MUL)
            conv(a("b6", 0, 32), "E1", every("gr" + s, 0, 512))
        Zq = aff(n32("Zq", B, 512), ind(a(zt), uZ), on=ONPK)
        eq = tt(n32("eq", B, 512), ind(a(LS), uZ), a("Mrow"), EQ)
        prod = tt(n32("prod", H, 512), a("b1"), eq, MUL)
        conv(a("b7", 64, 96), "Eh", every("prod" + s, 0, 512))
        conv(a("b7", 96, 128), "Es", every("eq" + s, 0, 512))
        halves = [(a(b, 0, 256), 256 * k, 256 * k + 256) for k, b in enumerate(("b4", "b0"))]
        for o, lo, hi in halves:
            mms([(o, a("Weq"), h("eq", lo, hi), True, False), (o, es("E2h", 4), h("prod", lo, hi), False, False)])
        f17 = aff(n32("f17"), i1, 4.0, 13.0 + 2 * par)
        n32("c5", F, 160)
        for j in range(4):
            aff(h("c5", 32 * j + 32, 32 * j + 64), f17, 1.0, 596.0, on="S")

        def by16(n, i, j):
            return aff(n32(n, I), tt(n32(n + "_", I), i, j, MUL), 0.0625, -0.46875, f=AF.Identity, v=(4, None, SHR))

        base = by16("base", f17, a("mA"))
        tt(n32("t4", F, 128), h("p4"), h("c5", 32), MUL)
        n32("r2", F, 64)
        X1 = tt(n32("X1"), a("b6", 0, 32), a("m37"), MUL)
        X2 = tt(h("r2", 32), X1, base, ADD)
        n32("P4", I, 256)
        if "b" in ONS[t]:
            n32("t5", F, 128)
            for j in range(4):
                tt(h("t5", 32 * j, 32 * j + 32), h("t4", 32 * j, 32 * j + 32), base, ADD)
        for j in range(4):
            if "b" in ONS[t]:
                tt(h("P4", 32 * j, 32 * j + 32), h("t5", 32 * j, 32 * j + 32), X1, ADD)
            else:
                tt(h("P4", 32 * j, 32 * j + 32), h("t4", 32 * j, 32 * j + 32), X2, ADD)
        n32("u4", U, 128)
        for lo in (0, 64):
            cp(h("u4", lo, lo + 64), ts(h("P4", 128 + lo, 192 + lo), h("P4", lo, lo + 64), 4095, AND))
        uO = ts(n32("uO", U), a("b7", 64, 96), 0.5, MUL, 64.5, ADD)
        fo = aff(n32("fo"), a("b7", 64, 96), 0.5, 63.5)
        f20 = aff(h("c5", 0, 32), fo, 2.0, 37.0, on="S")
        out = aff(n32("out", B), a("b7", 96, 128), -8192.0, 8192.0, f=AF.Relu, v=(0.5, 8192.0, LT, MUL))
        pos = tt(n32("pos0"), a("b7", 96, 128), aff(n32("f16i"), f17, 4.0, 443.0 - 8 * par, on="S"), ADD)
        pos = tt(n32("pos2"), tt(n32("pos1"), pos, out, SUB), a("mA"), MAX)
        uP = cp(n32("uP", U), pos)
        gr2 = aff(n32("gr2", B, 512), ind(a(TB, 0, 1025), uO), f=AF.Abs if t < 2 else None)
        conv(a("b6", 32, 64), "Ed", every("gr2" + s, 0, 512))
        for o, lo, hi in halves if t < 2 else ():
            mm(o, es("E0", 7), h("gr2", lo, hi), False, False)
        for k, bank in enumerate(("b6", "b7")):
            for j in (2 * k, 2 * k + 1):
                tt(h("G4", 512 * j, 512 * j + 512), ind(a("W", 16), h("u4", 32 * j, 32 * j + 32)), Zq, MAX)
                run("W")
            o = a(bank, 128, 192)
            conv(o, "E64", every("G4" + s, 1024 * k, 1024 * k + 1024), False, True,
                 [(o, a("ID"), h("p4", 64 * k, 64 * k + 64), True, False), (o, a("ID"), a("j16", 64 * k, 64 * k + 64), False, False)]
                 + [(a(bank, 128 + 32 * j, 160 + 32 * j), a("ID64"), out, False, False) for j in range(1 - k, 2)])
            if k == 0:
                aff(n32("tA", F, 64), o)
        i5 = by16("i5", fo, a("m17"))
        f19 = tt(h("r2", 0, 32), tt(n32("f21"), a("b6", 32, 64), a("m613"), MUL), i5, ADD)

        def place(n, p, c, rest):
            v = tt(n32(n + "b", I, p[2]), tt(n32(n + "a", F, p[2]), p, c, MUL), rest, ADD)
            return cp(n32(n, U, p[2]), ts(n32(n + "c", I, p[2]), v, 4095, AND))

        Do = tt(n32("Do", B, 512), ind(a("W", 16), place("uo", d, f20, f19)), Zq, MAX)
        run("W")
        for o, lo, hi in halves:
            mm(o, es("E2n", 0), h("Do", lo, hi), False, False)
        tt(n32("tk", F, 64), h("tA"), a("b7", 128, 192), MIN)
        pn = ts(n32("pn", I), tt(n32("kI", I), h("tk", 0, 32), h("tk", 32, 64), MIN), 15, AND)
        place("un", pn, f20, f19)
        for n in ("Dn", "hiT", "yv"):
            n32(n, B, 512)
        late = "p" in ONS[t]
        if late:
            tt(n32("dp", B), pn, d, SUB)
        for (o, lo, hi), b in zip(halves, ("b4", "b0")):
            if late:
                mms([(a(b, q, 256, 16), a("FH", 128 * q, 128 * q + 128), h("dp", lo // 16, hi // 16), False, False) for q in range(16)])
            tt(h("Dn", lo, hi), ind(a("W", 16), h("un", lo // 16, hi // 16)), h("Zq", lo, hi), MAX)
            mm(o, es("E2", 0), h("Dn", lo, hi), False, True)
            aff(h("hiT", lo, hi), o, odd, on="S")
            tt(h("yv", lo, hi), o, h("hiT", lo, hi), SUB)
            cp(ind(a("WK" + s), h("uP", lo // 16, hi // 16)), h("yv", lo, hi))
        if t == 1 or (t and not MERGE):
            keys = members(TB, par, t == 1, True, ONGN[t])
        if t == 1:
            elect(2, 1, keys)
        aff(n32("LSh", H, 256), a(LS, 16), on="S")
        mms([(a("b7", 256 + 128 * k, 384 + 128 * k), h("LSh", 128 * k, 128 * k + 128), a("IDh"), True, True) for k in range(2)])
        aff(n32("LMT", F, 256), a("b7", 256, 512), on="S")
        if t < 2:
            mms([(a("b7", 192 + 8 * k, 200 + 8 * k), a("onS", par + 256 * k, 256 * k + 256, 2), a("G8c"), True, True) for k in range(2)])
            aff(n32("c15", F, 16), a("b7", 192, 208), 2.0 * par - 1.0, 15360.0 + 0.5 * t)
        for k in range(2):
            o, on = a("b7", 256 + 128 * k, 384 + 128 * k), a("onS", par + 256 * k, 256 * k + 256, 2)
            mms([(o, a("ones"), a("k0", 0, 128), True, False), (o, on, a("Shn" if par else "Sh"), False, False), (o, on, a("ID" if par else "IDn"), False, True)])
        aff(n32("mkT", B, 256), a("b7", 256, 512), on="S")
        for k, b in enumerate(("b5", "b2")):
            mms([(a(b, q, 256 + 128 * late, 16), a("WK" + s, 512 + 2048 * k + q, 2560 + 2048 * k, 16), a("WAB", 0, 16 + 8 * late), True, True)
                 for q in range(16)])
            o, parts = a("b3", 128 * k, 128 * k + 128), ["dM"]
            if late:
                parts.append("dD" + s)
                aff((k or n32("dD", B, 256)) and h("dD", 128 * k, 128 * k + 128), a(b, 256, 384))
            mms([(o, a("ones"), a("m37c"), True, False)] + [(o, a(n, 128 * k, 128 * k + 128), a("ID32"), False, n == parts[-1]) for n in parts])
        if not late:
            pk = aff(n32("pk", B, 512), ind(a("W", 16), place("up", pn, h("c5", 32, 64), X2)), on=ONPK)
        dm = pn
        if t < 2:
            send(dn, aff(h("gs"), pn), h("gl"), "ag%d" % (t + 1), "lg%d" % (t + 1), up)
        o = a("b3", 256, 512)
        mms([(o, a("IDh"), a("x17%d" % par), True, False), (o, a("B32"), a(TB, 1 + par, 513, 2), False, True)])
        tt(n32("s0", F, 256), o, aff(n32("a37", F, 256), a(LS, 16), 2.0, 35.0, on="S"), MUL)
        aff(n32("s1", F, 256), h("s0"), 1.0, 22052.0, on="S")
        n32("lI", I, 512)
        n32("offM", U, 256)
        for k in range(2):
            lo, hi = 128 * k, 128 * k + 128
            tt(a("b3", lo, hi), a("b3", lo, hi), a("x613%d" % par, lo, hi), MUL)
            tt(h("lI", lo, hi), a("b3", lo, hi), h("s1", lo, hi), ADD)
            ts(h("lI", 256 + lo, 256 + hi), h("lI", lo, hi), 5, SHR, -2147479553, AND)
            ts(h("offM", lo, hi), h("lI", 256 + lo, 256 + hi), 16.0, ADD)
            big = 2 if "GL" + s in BIG else 1
            for ch in range(4 * k, 4 * k + 4, big):
                aff(h("GL", 512 + 512 * ch, 512 + 512 * (ch + big)), ind(a("W"), h("offM", 32 * ch, 32 * (ch + big))), on=ONGL[t])
                run("GL")
        if not late:
            cp(ind(h("GL"), uP), pk)
        for ch in range(4):
            scan(h("sc", 1024 * ch, 1024 * ch + 1024), a("mask"), h("GL", 512 + 1024 * ch, 1536 + 1024 * ch), MUL, MAX)
            run("sc")
        n32("zf", I, 256)
        w = 128 if "z" in ONS[t] else 256
        for lo in range(0, 256, w):
            o, n = a("b3", lo, lo + w), "zy"[lo // 128] + s
            mms([(o, a("ID"), a(zt, 16 + lo, 16 + lo + w), True, False), (o, a("ID"), h("sc", 15 + 16 * lo, 16 * (lo + w), 16), False, True)])
            cp(h("zs", lo, lo + w), aff(h("zf", lo, lo + w), o, 0.4995))
            send((rank + 1 + t) % N, h("zs", lo, lo + w), a("z%d" % (t + 1), 16 + lo, 16 + lo + w), "a" + n, "l" + n, (rank - 1 - t) % N)
            if t == 2:
                v = a("z3", 16 + lo, 16 + lo + w)
                dma("DS"[lo // 128], T.yz[:, lo:lo + w], v[0], [(v[1][0], False)], 256 * w)
                steps[-1]["run"] = None
        n32("kw", I, 512)
        for k, b in enumerate(("b5", "b2")):
            scan(h("kw", 256 * k, 256 * k + 256), a("mask", 0, 256), a(b, 0, 256), MUL, MAX)
        kA, kB = h("kw", 15, 512, 32), h("kw", 31, 512, 32)
        inj = tt(n32("inj", B, 16), kA, a("thK" + s), GT)
        t1 = ts(n32("t1", I, 16), kA, 224, AND)
        cI = ts(n32("cI", I, 16), kB, 1, SHR, 31, AND)
        t2 = ts(n32("t2", I, 16), kB, 3, SHR, 24, AND)
        gh = tt(n32("gh", B, 16), ts(n32("g1", I, 16), kA, 128, AND), inj, MUL)
        o = a("b6", 192, 208)
        mms([(o, a("ones"), a("c46"), True, False), (o, a("TRI"), gh, False, False), (a("b6", 200, 208), a("ones8"), h("gh", 0, 8), False, True)])

        def same(o, tab, v, w):
            for k in range(16):
                aff(h(o + "a", w * k, w * k + w), tab(k), -1.0, h(v, k, k + 1), on="S", f=AF.Abs)
                run(o)
            aff(h(o), h(o + "a"), -1.0, 1.0, on="S", f=AF.Relu)

        n32("rt", B, 512)
        if "r" in ONS[t]:
            n32("rta", B, 512)
            cp(n32("cF", F, 16), cI)
            same("rt", lambda k: a("x32", 0, 32), "cF", 32)
        else:
            tt(h("rt"), ind(cI, a("o32")), a("x32"), EQ)
        q8 = tt(n32("q8", F, 16), t1, t2, ADD)
        q9 = tt(n32("q9", F, 16), a("b6", 192, 208), q8, MAX)
        n32("lt", B, 256)
        if "l" in ONS[t]:
            n32("lta", B, 256)
            same("lt", lambda k: a("xQ", 0, 16), "q9", 16)
        else:
            tt(h("lt"), ind(q9, a("o16")), a("xQ"), EQ)
        mms([(a("b5", 0, 256), h("lt", 128 * k, 128 * k + 128), h("rt", 256 * k, 256 * k + 256), k == 0, k == 1) for k in range(2)])
        aff(n32("hx", B, 256), a("b5", 0, 256))
        aff(h("hs"), ind(h("hx"), a("oH")))
        send(up, h("hs"), h("hl"), "ah" + s, "lh" + s, dn)
        o1 = tt(n32("o1", F, 16), aff(n32("o4", F, 16), t1, 4.0, 1.0), ts(n32("l7", I, 16), kB, 1, SHR, 127, AND), ADD)
        n32("test", B, 256)
        if "t" in ONS[t]:
            for k in range(16):
                aff(h("test", 16 * k, 16 * k + 16), a("b7", 256 + 16 * k, 272 + 16 * k) if "T" in ONS[t] else h("LMT", 16 * k, 16 * k + 16),
                    -1.0, h("o1", k, k + 1), on="S", f=AF.Abs)
                run("test")
        else:
            tt(h("test"), ind(o1, a("o16")), h("LMT"), OP.not_equal)
        scan(n32("out_", B, 256), a("k0"), h("test"), MAX, MIN)
        fresh = h("out_", 15, 256, 16)
        loc = tt(n32("loc0", F, 16), inj, gh, GT)
        if t < 2:
            pb = ts(n32("pb", I, 16), kB, 1, SHR, 1, AND)
            nn = ts(n32("nm", F, 16), ts(n32("nn", I, 16), kA, 31, AND), 16384.0, MUL)
            jk = tt(n32("jk", F, 16), tt(n32("j1", F, 16), nn, h("c15", 0, 16), ADD), aff(n32("j2", F, 16), o1, 0.5), ADD)
            jk = tt(n32("jq", F, 16), tt(n32("jp", F, 16), loc, pb, GT if t else MUL), jk, MUL)
            k2 = a("key%d" % (t + 1), 16 * par, 16 * par + 16)
            tt(k2, tt(n32("j3", F, 16), jk, fresh, MUL), k2, MAX)
        jv = tt(n32("jv", F, 16), tt(n32("jo", F, 16), loc, o1, MUL), fresh, MUL)
        n32("dl", H, 256)
        if "d" in ONS[t]:
            for k in range(16):
                aff(h("dl", 16 * k, 16 * k + 16), h("mkT", 16 * k, 16 * k + 16), h("jv", k, k + 1), on="S")
                run("dl")
        else:
            tt(h("dl"), ind(jv, a("o16")), h("mkT"), MUL)
        o = a("b7", 256, 512)
        mms([(o, a("IDh"), h("LSh"), True, False)]
            + [(a("b7", 256 + 128 * k, 384 + 128 * k), h("dl", 128 * k, 128 * k + 128), a("IDh"), False, k == 1) for k in range(2)])
        if t == 0:
            aff(a("onS", 0, 512, 2), o, f=AF.Sign, v=(1.0, None, MIN))
            cp(a("off0"), o)
            aff(a(LS, 16), o, on="S")
            new("ky", 512, F)
        else:
            aff(a("ky", par, 512, 2), o, 1.0, -1.0)
        if t < 2:
            mm(a("b6", 208, 224), a("ones"), inj)
            n32("c0", F, 32)
            o, i_, c = h("c0", 16, 32), a("b6", 208, 224), h("c0", 0, 1)
            acc = spans(o, [i_]) + [(c[1][0], True)]
            step({"S": (100, [(acc, lambda e, o=o, i_=i_, c=c: e.activation(o[0], i_[0], AF.Copy, bias=0.0, scale=128.0, accum_out=c[0]))])}, acc)
            v = aff(h("c0", 1, 2), aff(n32("cJ", I, 1), c, 1.0 / 32, -0.484375), -131072.0)
            aff(new("thK%d" % (t + 1), 16, F), a("thK0"), 1.0, aff(h("c0", 2, 3), c, 4096.0, v))
            v = ts(n32("gv1", I), tt(n32("gv0", I), h("gl"), h("hs"), ADD), 15, AND)
            ghosts(t + 1, cp(n32("gv2", B), v))
        if t == 0 and not MERGE:
            mms(sum(sizes("b4", True), []))
            aff(a("TK", 1, 513), a("b4"))
            elect(2, 0, members("TK", 0, True, False, ONK))
        v = ts(n32("dv1", I), tt(n32("dv0", I), dm, h("hl"), ADD), 15, AND)
        if t < 2:
            cp(new("d%d" % (t + 1), 32, B), v)
            table(t + 1)
        else:
            o = cp(new("dF", 32, F), v)
            dma("D", T.yl[:, :], a("ky")[0], [(a("ky")[1][0], False)], 128 * 2048)
            dma("S", T.yd[:, :], o[0], [(o[1][0], False)], 128 * 128)

    if "order" not in PLAN:
        PLAN["order"] = arrange(steps)
        PLAN["tiles"], PLAN["steps"] = tiles, steps
    issue(g, core, T, topo, eng, steps, PLAN["order"])


def arrange(steps):
    hist, last, deps, soft, after = {}, {}, [], [], []
    for k, s in enumerate(steps):
        d = set()
        for (n, lo, hi), w in s["acc"]:
            d.update(j for l2, h2, w2, j in hist.get(n, []) if lo < h2 and l2 < hi and (w or w2))
            if n in OPEN and "P" in s["alts"] and n in last:
                d.add(last[n])
        for (n, lo, hi), w in s["acc"]:
            hist[n] = [e for e in hist.get(n, []) if not (w and lo <= e[0] and e[1] <= hi)] + [(lo, hi, w, k)]
            if n in OPEN and "P" in s["alts"]:
                last[n] = k
        d.discard(k)
        before = {last[s["run"]]} - d if s["run"] in last else set()
        soft.append(before if len(s["alts"]) == 1 else set())
        after.append(before - soft[k])
        if s["run"]:
            last[s["run"]] = k
        deps.append(d | soft[k])
    n = len(steps)
    cost = [{q: c for q, (c, _) in s["alts"].items()} for s in steps]
    late = [s["late"] for s in steps]
    cost[[s["kind"] for s in steps].index("send")]["G"] += FIRST
    free = 0.0
    for k, s in enumerate(steps):
        if s["kind"] == "dma":
            if deps[k] == soft[k]:
                free += late[k]
                late[k] = free
            late[k] += DMA0
    users = [set() for _ in steps]
    for k in range(n):
        for j in deps[k]:
            users[j].add(k)
    banks = [{b for (b, _, _), _ in s["acc"] if b in BANKS} for s in steps]

    way = [0.0] * n
    for k in reversed(range(n)):
        way[k] += min(cost[k].values()) + late[k] + WAIT + MORE.get(steps[k]["name"], 0)
        for j in deps[k]:
            way[j] = max(way[j], way[k] - (late[j] + WAIT if j in soft[k] else 0))
        for j in after[k]:
            way[j] = max(way[j], way[k] - WAIT - min(cost[j].values()) / 2)

    def place(way, deps, users, back, SPARE, GRAB, FILL, HOLD):
        at, end, free, bank = {}, {}, {q: 0.0 for q in "VSPGD"}, {b: {} for b in BANKS}
        left = [len(d) for d in deps]
        pre, post = (late, [0.0] * n) if back else ([0.0] * n, late)
        front = {k: pre[k] for k in range(n) if not left[k]}
        while front:
            cand = {q: [] for q in free}
            for k, u in front.items():
                for q in cost[k]:
                    cand[q].append((max([u, free[q]] + [v + pre[k] for b in banks[k] for q2, v in bank[b].items() if q2 != q]), k))
            t, q = min((min(c)[0], q) for q, c in cand.items() if c)
            rivals = [(u, k) for u, k in cand[q] if u > t]
            for j, u in front.items():
                if q not in cost[j]:
                    for k in users[j]:
                        if left[k] == 1 and q in cost[k]:
                            rivals.append((max(u, free[min(cost[j])]) + min(cost[j].values()) + post[j] + pre[k] + WAIT, k))
            pick = None
            for u, k in sorted((c for c in cand[q] if c[0] <= t), key=lambda c: -way[c[1]]):
                c = cost[k][q]
                over = [t + c - v - FILL * (v - t) - HOLD for v, j in rivals if way[j] > way[k] and way[j] - way[k] > t + c - v]
                if q == "V" and "S" in cost[k] and max(free["S"], t) + cost[k]["S"] < t + c + SPARE and not (c > 400 and free["S"] > t and all(t + c - v < GRAB for v, j in rivals if len(cost[j]) == 1)):
                    continue
                if max(over + [0]) <= 0:
                    pick = k
                    break
            if pick is None:
                free[q] = min([u for u, k in rivals if u > t] + [t + 200])
                continue
            c = cost[pick][q]
            at[pick], free[q], end[pick] = (t, q), t + c, t + c + post[pick]
            for b in banks[pick]:
                bank[b][q] = end[pick] + WAIT
            del front[pick]
            for k in users[pick]:
                left[k] -= 1
                if not left[k]:
                    front[k] = max(end[j] - post[j] if j in soft[k] or k in soft[j] or (at[j][1] == "P" and "P" in cost[k])
                                   else end[j] + WAIT + pre[k] for j in deps[k])
        return at, end

    hard = [deps[k] if steps[k]["kind"] == "dma" else deps[k] - soft[k] for k in range(n)]
    PLAN["bound"], PLAN["ends"], tried = max(way), [], []
    for rule in RULES:
        best, w = None, way
        for _ in range(PASSES):
            at, end = place(w, deps, users, False, *rule)
            if best is None or max(end.values()) < best[0]:
                best = (max(end.values()), at)
            w = place(end, users, deps, True, *rule)[1]
        PLAN["end"], at = best
        tried.append(polish(steps, hard, soft, [(k, at[k][1]) for k in sorted(at, key=lambda k: (at[k][0], k))], MOVES[0], HEAT[0]))
        PLAN["ends"].append(PLAN["rates"])
    return polish(steps, hard, soft, min(tried)[1], MOVES[1], HEAT[1])[1]


def polish(steps, deps, soft, order, moves, heat):
    n = len(steps)
    users = [[] for _ in steps]
    for k in range(n):
        for j in deps[k]:
            users[j].append(k)
    wait = [[j for j in deps[k] if j not in soft[k] and not ("P" in steps[j]["alts"] and "P" in steps[k]["alts"])] for k in range(n)]
    banks = [sorted({int(b[1]) for (b, _, _), _ in s["acc"] if b in BANKS}) for s in steps]
    first = [s["kind"] for s in steps].index("send")
    late = [-s["late"] if s["kind"] == "dma" else s["late"] for s in steps]
    busy = [[{q: c + (FIRST if k == first else 0) if s["kind"] else f * (c + (ga - GATHER) * s["n"][0] + (sc - SCATTER) * s["n"][1])
              for q, (c, _) in s["alts"].items()} for k, s in enumerate(steps)] for f, ga, sc, w in RATES]
    busy = [[{q: (c, r[3] * (max(late[k], 0) + LAG[q])) for q, c in v.items()} for k, v in enumerate(b)] for b, r in zip(busy, RATES)]

    def replay(order, busy, was, at, begin=None, reach=n, last=None):
        end, marks = list(was[1]), was[2][:at // 24 + 1]
        free, bq, be, bo = marks[-1]
        free, bq, be, bo = dict(free), list(bq), list(be), list(bo)
        for p in range(at // 24 * 24, n, 24):
            if p // 24 == len(marks):
                if p >= reach and was[2][p // 24] == (free, bq, be, bo):
                    return max(end), end, marks + was[2][p // 24:]
                marks.append((dict(free), list(bq), list(be), list(bo)))
            for k, q in order[p:p + 24]:
                t = free[q]
                for j in wait[k]:
                    if end[j] > t:
                        t = end[j]
                bs = banks[k]
                for b in bs:
                    v = be[b] if bq[b] != q else bo[b]
                    if v > t:
                        t = v
                if begin is not None:
                    begin[k] = (t, len(begin))
                c, after = busy[k][q]
                free[q] = e = t + c
                if late[k] < 0:
                    free["M"] = e = max(t + DMA0, free["M"]) - late[k]
                e += after
                if e != end[k]:
                    end[k] = e
                    if last and last[k] >= reach:
                        reach = last[k] + 1
                for b in bs:
                    if bq[b] != q:
                        bo[b], bq[b] = be[b], q
                    be[b] = e
        return max(end), end, marks

    def lasts(order):
        last = [0] * n
        for p, (k, q) in enumerate(order):
            for j in wait[k]:
                last[j] = p
        return last


    start = (0, [0.0] * n, [({q: 0.0 for q in "VSPGDM"}, [""] * 8, [0.0] * 8, [0.0] * 8)])
    now = [replay(order, b, start, 0) for b in busy]
    unit = [v[0] for v in now]
    seed = [SEED]

    def draw():
        seed[0] = (seed[0] * 1103515245 + 12345) % 2147483648
        return (seed[0] + 1) / 2147483649.0

    def chain(order, busy, end):
        out, t = [], max(end)
        for p in reversed(range(n)):
            k, q = order[p]
            if abs(end[k] - t) < 0.01 or (out and q == out[-1][1] and late[k] >= 0 and abs(end[k] - busy[k][q][1] - t) < 0.01):
                out.append((k, q))
                t = end[k] - sum(busy[k][q]) if late[k] >= 0 else max([end[j] for j in wait[k]] + [-1])
        return out

    def value(then):
        return sum((v[0] + EARLY * sum(v[1]) / n) / u for v, u in zip(then, unit)) / len(unit)

    score = best = value(now)
    kept = order
    for it in range(moves):
        if it % 24 == 0:
            m = it // 24 % len(busy)
            if it % 480 == 0:
                begin = {}
                replay(order, busy[0], start, 0, begin)
                new = sorted(order, key=lambda v: begin[v[0]])
                then = [replay(new, b, start, 0) for b in busy]
                if value(then) <= score + 1e-9:
                    order, now = new, then
            hot, last = chain(order, busy[m], now[m][1]), [p + 40 for p in lasts(order)]
            held = [(u, v) for u, v in zip(hot, hot[1:]) if u[1] == v[1] and v[0] not in deps[u[0]]]
        i = int(draw() * n)
        r, d = draw(), 1 + int(-12 * math.log(draw()))
        if draw() < 0.7 and hot[0] in order:
            u = hot[int(draw() * len(hot))]
            if u not in order:
                continue
            i = order.index(u)
        k, q = order[i]
        if r > 1 - SWAP and held:
            u, v = held[int(draw() * len(held))]
            if u not in order or v not in order:
                continue
            i, j = order.index(u), order.index(v)
            if j > i:
                continue
            d, r = i - j, 0.5
            if draw() < 0.4:
                i, r = j, 0.55
            k, q = order[i]
        if r < 0.15:
            if len(steps[k]["alts"]) == 1:
                continue
            lo, hi, new = i, i + 1, order[:i] + [(k, "V" if q == "S" else "S")] + order[i + 1:]
        else:
            back = r == 0.5 or (r != 0.55 and draw() < 0.6)
            if r > 0.6:
                d, m, w = 0, 1 + d // 8, -1 if back else 1
                while m and 0 <= i + w * (d + 1) < n:
                    d += 1
                    m -= order[i + w * d][1] == q
            lo, hi = (max(0, i - d), i + 1) if back else (i, i + d + 1)
            drag = {k}
            for j, _ in (order[lo:hi][::-1] if back else order[lo:hi]):
                if any(u in drag for u in (users[j] if back else deps[j])):
                    drag.add(j)
            x, y = [v for v in order[lo:hi] if v[0] in drag], [v for v in order[lo:hi] if v[0] not in drag]
            new = order[:lo] + (x + y if back else y + x) + order[hi:]
        limit = score - heat * (1 - it / moves) * math.log(draw())
        then = []
        for b, w, u in zip(busy, now, unit):
            then.append(replay(new, b, w, lo, None, hi, last))
            if then[-1][0] > w[0] + 3 * u * (limit - score) + CUT * u:
                break
        else:
            e = value(then)
            if e <= limit:
                score, order, now = e, new, then
                if e < best:
                    best, kept = e, new
    PLAN["rates"] = [round(replay(kept, b, start, 0)[0] * .83e-3, 1) for b in busy]
    return sum(math.log(v) for v in PLAN["rates"]), kept


def issue(g, core, T, topo, eng, steps, plan):
    hist, known, total, nd = {}, {q: {} for q in "VSPGD"}, {}, [0]

    def order(q, acc):
        toks = []
        for (n, lo, hi), w in acc:
            for r in hist.get(n, []):
                if n in BANKS and r[3] != q:
                    toks.append(r[4])
                elif lo < r[1] and r[0] < hi and (w or r[2]) and not r[3] == q == "P":
                    toks.append(r[4])
        toks.sort(key=lambda k: -len(k[2]))
        for i, (s, v, kn) in enumerate(toks):
            if known[q].get(s, 0) >= v:
                continue
            if any(j != i and (k[2].get(s, 0) >= v and (k[0] != s or k[1] > v)) for j, k in enumerate(toks)):
                continue
            eng[q].wait_ge(T.sem[s], v)
            for n, c in kn.items():
                known[q][n] = max(known[q].get(n, 0), c)
            known[q][s] = max(known[q].get(s, 0), v)

    def note(q, acc, tok, dma=False):
        for (n, lo, hi), w in acc:
            keep = []
            for r in hist.get(n, []):
                inside, ps = lo <= r[0] and r[1] <= hi, n in BANKS
                if inside and (w if not ps else (w or not r[2])) and not (ps and r[3] != q and not w):
                    continue
                if inside and not w and not r[2] and r[3] == q and not dma:
                    continue
                keep.append(r)
            hist[n] = keep + [(lo, hi, w, "dma" if dma else q, tok)]

    for s in steps:
        if s["kind"] == "send":
            buf, rbuf, arr, loc, dst, src = s["alts"]["G"][1][0]
            total[arr] = len(topo.engines(T.cores[src], core)[:8])
            note("R", [(rbuf[1][0], True)], (arr, total[arr], {arr: total[arr]}), True)
    for k, q in plan:
        s = steps[k]
        if s["kind"] == "send":
            buf, rbuf, arr, loc, dst, src = s["alts"][q][1][0]
            to = T.cores[dst]
            use = topo.engines(core, to)[:8]
            acc = [(buf[1][0], False)]
            order(q, acc)
            g.remote_dma(rbuf[0], buf[0], T.sem[arr], T.sem[loc], topo.addr(to)[1], topo.addr(to)[0], sum(1 << e for e in use))
            total[loc] = len(use)
            note(q, acc, (loc, len(use), {loc: len(use)}), True)
            continue
        for acc, call in s["alts"][q][1]:
            order(q, acc)
            if s["kind"] == "dma":
                sem, n = "d%d" % nd[0], 16
                nd[0] += 1
            else:
                sem, n = "s" + q, 1
            total[sem] = total.get(sem, 0) + n
            call(eng[q]).then_inc(T.sem[sem], n)
            kn = dict(known[q])
            kn[sem] = total[sem]
            note(q, acc, (sem, total[sem], kn), s["kind"] == "dma")
    for s, v in total.items():
        g.wait_ge(T.sem[s], v)
